import numpy as np, ml_dtypes
CORES = [5,29,101,125,133,157,229,253]
N = 8
BF = ml_dtypes.bfloat16
L, W, RO, LX, M = 128, 4096, 5, 4, 32
KS = np.arange(16, dtype=np.int32)[:, None]
def places(c, u, a):
    return (((c * (2 * u + 1)) >> 5) + c + a) & (W - 1)
def pick(x, at):
    return np.take_along_axis(x, at.reshape(N, 8, 1, 16 * L), 3).reshape(N, 8, 16, 16, L)
def score(p):
    before = np.add.accumulate(p, axis=3) - p; e = np.add.reduce((16 - KS) * p, axis=3)
    return e, e[:, :, :, None] + KS * p - before
def plain(rng):
    return (rng.integers(0, 16, (N, 8, 16, W), dtype=np.int32), rng.integers(0, 4096, (N, 8, 16, L), dtype=np.int32), rng.integers(0, 64, (N, 8, 16, L), dtype=np.int32),
            rng.integers(0, 64, (N, 8, 16, 1), dtype=np.int32), rng.integers(45, 90, (N, 8, L), dtype=np.int32))
def stress(rng, mid):
    sh = (N, 8, 16, RO, L); kd = rng.integers(0, 3, (N, 8, 1, RO, L))
    near = mid + 18 * rng.standard_normal((N, 8, 1, RO, L)) + 12 * rng.standard_normal(sh)
    far = np.where(rng.random(sh) < 0.55, 200 + 56 * rng.random(sh), 40 * rng.random(sh))
    return np.clip(np.floor(np.where(kd == 0, near, np.where(kd == 1, 256 * rng.random(sh), far))), 0, 255).astype(np.int32)
def low(a):
    return np.asarray(a, np.float32).astype(BF)
def pack(x, c, s, y, wt, th):
    return {"x0": low(x.reshape(N, 128, W)), "c0": np.ascontiguousarray(c.reshape(N, 128, L)).astype(np.int32), "st": low(s.reshape(N, 128, RO * L)),
            "y0": low(y.reshape(N, 128, L)), "w": low(wt.reshape(N, 128, 1)), "th": low(th)}
def setup_inputs(rng):
    x, c, y, wt, th = plain(rng)
    return pack(x, c, stress(rng, 122), y, wt, th)
def setup_inputs_spread(rng):
    x, c, y, wt, th = plain(rng)
    x = np.minimum(np.floor(np.exp2(4 * rng.random((N, 8, 1, W), dtype=np.float32)) * rng.random((N, 8, 16, W), dtype=np.float32)), 15).astype(np.int32)
    c = np.floor(4096 * rng.random(c.shape) ** 3).astype(np.int32); y = np.floor(64 * rng.random(y.shape) ** 3).astype(np.int32)
    wt = np.floor(64 * rng.random(wt.shape) ** 2).astype(np.int32); th = np.floor(241 * rng.random(th.shape) ** 2).astype(np.int32)
    return pack(x, c, stress(rng, 15 + 40 * rng.random((N, 8, 1, 1, L))), y, wt, th)
def setup_inputs_ends(rng):
    sh = (N, 8, 16, RO, L); fz = (np.arange(N)[:, None] + np.arange(8)) & 1
    x = 15 * (rng.random((N, 8, 16, W), dtype=np.float32) < 0.5 * rng.integers(0, 3, (N, 8, 1, W))).astype(np.int32)
    c = 4095 * (rng.random((N, 8, 16, L)) < 0.5 * rng.integers(0, 3, (N, 8, 1, L))).astype(np.int32)
    y = 63 * (rng.random((N, 8, 16, L)) < 0.5 * rng.integers(0, 3, (N, 8, 1, L))).astype(np.int32)
    wt = 63 * (rng.random((N, 8, 16, 1)) < 0.6).astype(np.int32); wt[:, 7] = 63; wt[:, 0, 0] = 0; wt[:, :, 15] = 63
    th = 240 * rng.integers(0, 2, (N, 8, L))
    s = 255 * (rng.random(sh) < rng.choice(np.array([0.0, 0.45, 0.5, 0.55, 1.0]), (N, 8, 1, RO, L))).astype(np.int32)
    live = np.argsort(rng.random((N, 8, 1, L)), axis=-1) < 5 * L // 16; live[..., L - 4:] = False
    c = np.where(live, rng.integers(0, 4096, c.shape), c); s = np.where(live[:, :, :, None], stress(rng, 127), s)
    x[..., 0] = 15 * (1 - fz)[:, :, None]
    for u in (0, 1921): x[..., places(4095, u, 0)] = 15 * fz[:, :, None]
    x[..., 2:16] = 15; x[..., places(15, 1921, 0)] = 15
    full, none = 4095 * fz, 4095 * (1 - fz)
    y[..., L - 1] = 63; c[..., L - 1] = 0; s[:, :, :, 0, L - 1] = 255
    y[..., L - 4:L - 1] = 0; y[:, :, 15, L - 3] = 63
    for l in (L - 3, L - 2):
        c[..., l] = none[:, :, None]; c[:, :, 14, l] = full; c[:, :, 15, l] = 15; s[:, :, :, 0, l] = 30
    c[..., L - 4] = full[:, :, None]; c[:, :, 0, L - 4] = none; c[:, :, 2:, L - 4] = np.arange(2, 16); s[:, :, :, 0, L - 4] = 226
    return pack(x, c, s, y, wt, th)
def setup_inputs_corners(rng):
    x, c, y, wt, th = plain(rng); s = stress(rng, 150); n = np.arange(4096)
    typ = rng.integers(0, 4, (N, W)); p0 = int(places(4075, 2046, 0)); typ[:, p0] = 1; typ[:, (p0 + 1) & (W - 1)] = 0
    tb = typ[:, None, None, :]
    x = np.where(tb == 0, 0, np.where(tb == 1, 15, np.where(tb == 2, 13 + x % 3, x))).astype(np.int32)
    wt[:, :, 0] = 63; wt[:, :, 1] = 1; par = np.arange(L) & 1
    kd = np.stack([rng.permutation(L) % 8 for g in range(8)]); iu = rng.integers(0, 5, (8, L))
    top = (kd == 0) & (par == 1); fold = (kd == 0) & ((np.arange(L) & 3) == 0)
    iu = np.where(top, 3, np.where(fold, 2, iu)); ctl = (kd > 0) | top | fold
    y = np.where(ctl[:, None, :], 0, y); y[:, :, 0] = np.where(ctl, np.array([0, 0, 32, 32, 32])[iu], y[:, :, 0]); y[:, :, 1] = np.where(ctl, np.array([0, 1, 30, 31, 32])[iu], y[:, :, 1])
    c = np.where(top[:, None, :], 4095 - rng.integers(0, 3, c.shape), c)
    c = np.where(fold[:, None, :] & (rng.random(c.shape) < 0.5), 4075, c)
    th = rng.choice(np.array([0, 1, 60, 239, 240]), (N, 8, L)); th = np.where(kd == 7, rng.choice(np.array([0, 239]), (N, 8, L)), th)
    kb = kd[:, None, :]; a = rng.integers(8, 15, (8, 1, L)); b = np.minimum(15, a + 1 + rng.integers(0, 7, (8, 1, L))); z = np.zeros((8, 16, L), np.int64)
    want = np.select([kb == 1, (kb == 2) | (kb == 3), (kb == 4) | (kb == 7), kb == 5, kb == 6], [z + ((KS == a) | (KS == b)), z + (KS == b), z, z + 2, z + np.where(par == 1, KS > 0, True)], z - 1)
    eight = (7 * KS + np.arange(L)) % 16
    two = z + np.where((eight == 0) & (par == 1) & (b > a + 1), (225 + 15 * (16 - a)) >> 3, 30)
    s0 = np.select([kb == 1, kb == 2, kb == 3, kb == 4, kb == 5, kb == 6, kb == 7],
                   [two, z + 30 + (eight == 0) * par, z + 31, z + np.where(eight < 8 + par, 0, 255), 254 + rng.integers(0, 2, (8, 16, L)), z + np.where(par == 1, 226, 255), z + np.where(eight < 8, 0, 255)], z - 1)
    s[:, :, :, 0] = np.where(s0 < 0, s[:, :, :, 0], s0)
    us = np.array([0, 1, 2046, 2047, 0])
    for q in range(N):
        for i in range(5):
            kind = typ[q][places(n, us[i], 0)]
            for v in range(3):
                ix = np.flatnonzero(kind == v); ix = ix if len(ix) else n
                m = (iu == i)[:, None, :] & (want == v); c[q][m] = ix[rng.integers(0, len(ix), int(np.count_nonzero(m)))]
    for q in range(1, N, 2):
        s[q, :, :, 0] = np.where(kb == 7, 0, s[q, :, :, 0])
        for g, l in zip(*np.nonzero(kd == 7)):
            e = int(c[q - 1, g, 1, l]); kind = typ[q][(((n * e) >> 5) + n + 37 * e) & (W - 1)]; pos = (0, 14, 15, 16)[int(rng.integers(0, 4))]
            i0 = np.flatnonzero(kind == 0); i1 = np.flatnonzero(kind == 1); i0 = i0 if len(i0) else n; i1 = i1 if len(i1) else n
            zero = np.arange(16) >= pos; zero = zero & ((np.arange(16) == pos) | (rng.random(16) < 0.5))
            c[q, g, :, l] = np.where(zero, i0[rng.integers(0, len(i0), 16)], i1[rng.integers(0, len(i1), 16)])
    return pack(x, c, s, y, wt, th)
def setup_inputs_crowd(rng):
    x, c, y, wt, th = plain(rng); x = np.minimum(x, 14); s = stress(rng, 115)
    for q in range(N):
        for t in range(RO):
            kk = (q + t) % 4; g = (q + 3 * t + 7) % 8; l = (L - 1, 0)[t & 1]
            if kk < 2: s[q, :, :, t] = 255
            if kk == 1: s[q, g, :, t, l] = 0
            if kk == 3: s[q, :, :, t] = 0
            if kk == 3 and t != 1: s[q, g, :, t, l] = 255
    one = rng.integers(0, 4096, 8); one[2] = 4095; one[4] = 0
    for g in range(6):
        if g & 1: c[:, g, :, :L - 1] = one[g]
        else: c[:, g] = one[g]
    y[:, :4] = y[:, :4, :, :1].copy()
    th = np.where(rng.random(th.shape) < 0.5, th, 240 * rng.integers(0, 2, th.shape))
    return pack(x, c, s, y, wt, th)
def setup_inputs_ties(rng):
    x, c, y, wt, th = plain(rng); few = rng.integers(0, 16, (N, 8, 16, 40), dtype=np.int32); few[:, 1::2] = 8 * rng.integers(0, 2, (N, 4, 16, 40))
    x = np.ascontiguousarray(np.take_along_axis(few, rng.integers(0, 40, (N, 8, 1, W)), 3))
    c[:, 3] = rng.choice(np.array([0, 1, 2048, 4094, 4095]), (N, 16, L))
    u = np.add.reduce(wt * y, axis=2) & 2047; e, ek = score(pick(x, places(c, u[:, :, None], 0)))
    at = np.take_along_axis(ek, rng.integers(0, 16, (N, 8, 1, 1, L)), 3)[:, :, :, 0]
    s = stress(rng, 110); s[:, :, :, 0] = np.clip((at >> 3) + rng.integers(0, 2, (N, 8, 1, L)) * (rng.random(at.shape) < 0.4), 0, 255)
    th = rng.choice(np.array([0, 48, 56, 64]), (N, 8, L))
    return pack(x, c, s, y, wt, th)
def check_inputs(d):
    bad = []
    for k, hi in (("x0", 15), ("c0", 4095), ("st", 255), ("y0", 63), ("w", 63), ("th", 240)):
        v = np.asarray(d[k]).astype(np.float64)
        if not (np.min(v) >= 0 and np.max(v) <= hi): bad.append("range of " + k)
        elif np.any(v != np.floor(v)): bad.append("whole numbers in " + k)
    return bad
def reference(x0, c0, st, y0, w, th):
    x = x0.astype(np.int32).reshape(N, 8, 16, W); c = c0.astype(np.int32).reshape(N, 8, 16, L); y = y0.astype(np.int32).reshape(N, 8, 16, L)
    s = 8 * st.astype(np.int32).reshape(N, 8, 16, RO, L); wt = w.astype(np.int32).reshape(N, 8, 16, 1); bound = th.astype(np.int32)[:, :, None]
    a = np.zeros((N, 1, 1, 1), np.int64)
    for t in range(RO):
        u = (np.add.reduce(wt * y, axis=2) & 2047)[:, :, None]
        p = pick(x, places(c, u, a)); e, ek = score(p)
        g = np.add.reduce((ek >= s[:, :, :, t][:, :, :, None]).astype(np.int32), axis=2)
        best = 1 + np.argmax(g[:, :, 1:], axis=2)[:, :, None]
        g0 = g[:, :, :1]; gb = np.take_along_axis(g, best, 2)
        rest = g0 >= 9; move = ~rest & (gb > g0); go = ~rest & ~move
        name = np.take_along_axis(c, best, 2); v = np.take_along_axis(p, best[:, :, :, None], 3)[:, :, :, 0]
        fresh = (((name * u) >> 5) + u) & 4095
        down = np.concatenate([name, c[:, :, :15]], axis=2); up = np.concatenate([c[:, :, 1:], fresh], axis=2)
        c = np.where(move, np.where((KS <= best) | ((u & 1) == 1), down, c), np.where(go & (KS >= best), up, c))
        src = (np.arange(N) - 1 - t % (N - 1)) % N; ce, cv, come = name[src], v[src], go[src]
        h = (((c * ce) >> 5) + c + 37 * ce) & (W - 1)
        hit = np.add.reduce(np.abs(pick(x, h) - cv[:, :, :, None]), axis=2) <= bound
        pos = np.where(np.any(hit, axis=2), 1 + np.argmax(hit, axis=2), 0)[:, :, None]
        put = np.where(KS < pos, c, np.where(KS == pos, ce, np.concatenate([c[:, :, :1], c[:, :, :15]], axis=2)))
        c = np.where(come, put, c)
        y = e >> 5; a = np.add.reduce(go.reshape(N, -1).astype(np.int64), axis=1).reshape(N, 1, 1, 1)
        if t < LX:
            col = np.broadcast_to(M * np.arange(L) + (u & (M - 1)), (N, 8, 16, L))
            np.put_along_axis(x, col, ((np.take_along_axis(x, col, 3) + (e >> 7)) >> 1).astype(np.int32), 3)
    return {"yc": c.reshape(N, 128, L).astype(np.float32), "yy": y.reshape(N, 128, L).astype(np.float32).astype(BF)}

@@ -1,0 +1,723 @@
+from concourse.mybir import AluOpType as ALU, ActivationFunctionType as AF
+
+F, B, I, U = "float32", "bfloat16", "int32", "uint16"
+RO, PW = 5, 80
+SCRATCH = {}
+
+
+def _buf(name, n, dt, where="sbuf"):
+    SCRATCH[name] = (where, [128, n], dt)
+
+
+for _n, _w, _d in [
+    ("X0", 4096, B), ("X1", 4096, B), ("stb", 640, B), ("sT", 640, B), ("cin", 128, I), ("ct", 128, F),
+    ("yin", 128, B), ("wb", 16, B), ("th8", 128, B), ("thZ", 16, F), ("thm", 80, F),
+    ("pi", 8, I), ("pb", 8, I), ("pc", 16, F), ("iot", 160, F), ("kk8", 128, F), ("ii8", 128, F), ("kk16", 128, F),
+    ("ta", 128, F), ("tb", 128, F), ("I16", 128, B), ("Pf", 160, F), ("P0", 160, F), ("P1", 160, F),
+    ("W1", 144, B), ("WA", 144, B), ("Ww", 144, B), ("W8", 144, B), ("Wb", 128, B), ("Mx", 128, B), ("ME", 16, B),
+    ("sel", 1024, B), ("kc", 64, B), ("kap", 144, F), ("d0k", 64, F), ("lo4", 72, F), ("neg", 128, B), ("zer", 128, B),
+    ("c2k", 128, B), ("kc2", 64, B), ("o16", 128, F), ("ji", 16, I), ("jf", 16, F), ("jq", 16, I),
+    ("Lm", 16, U), ("Lc", 16, U), ("l32", 8, I), ("l32b", 8, I),
+    ("ui", 8, I), ("ub", 16, I), ("uI", 40, I), ("mU", 40, F), ("oU", 40, F), ("ob", 40, F), ("cx", 8, I), ("col", 40, U),
+    ("Acol", 16, F), ("cnt", 16, F), ("y128", 128, B), ("yo", 128, B), ("hx", 128, F), ("wv", 512, B),
+    ("ycs", 128, F), ("pay", 2 * RO * PW, F), ("land", 2 * RO * PW, F),
+]:
+    _buf(_n, _w, _d)
+for _h in "01":
+    for _n, _w, _d in [
+        ("A", 80, F), ("C", 64, F), ("t", 64, I), ("p", 64, I), ("off", 64, U), ("xa", 1024, B), ("xT", 1024, B),
+        ("ind", 1024, B), ("g2", 1024, B), ("ab", 1152, B), ("S", 64, F), ("Ki", 8, I), ("oi", 8, I), ("ei", 8, I),
+        ("fi", 8, I), ("ov", 8, U), ("nr", 16, F), ("TH", 8, F), ("oo", 8, F), ("mk", 144, F), ("Q", 80, F),
+        ("H", 80, F), ("Ms", 80, F), ("ep", 80, F), ("vT", 128, B), ("thb", 80, B),
+    ]:
+        _buf(_n + _h, _w, _d)
+PSUM = ["pB00", "pB01", "pB10", "pB11", "pS0", "pS1"]
+for _n in PSUM:
+    _buf(_n, 512, F, "psum")
+for _n in ("pX0", "pX1"):
+    _buf(_n, 1024, B, "psum")
+    PSUM.append(_n)
+DMAS = ["dc", "dy", "dw", "dx0", "dx1", "ds", "dt", "dyc0", "dyc1", "dyy"]
+SEMAPHORES = ["nV", "nA", "nP", "nG", "loc"] + DMAS + ["arr%d" % i for i in range(2 * RO)]
+CNT = {"V": "nV", "A": "nA", "P": "nP", "G": "nG"}
+BIG = 1.0e9
+GAM, SCA = 1.5, 3.5
+CFG = {"G1": "VAAA", "CP": "VVVV", "SG": "AVAV", "G2": "VAVA", "EP": "A", "ME": "VV", "X2": 0, "NR": "A", "BK": 1}
+LAT = {"x": 5000.0, "call": 900.0, "hop": 2600.0, "pe": 0.5}
+SAMEQ_WAR = True
+
+
+def s(b, lo=0, hi=None, st=1, p0=0, p1=128):
+    return (b, lo, SCRATCH[b][1][1] if hi is None else hi, st, p0, p1)
+
+
+def ind(w, o):
+    return ("*", w, o)
+
+
+def ap(T, x):
+    if x[0] == "*":
+        return ap(T, x[1]).indirect(ap(T, x[2]))
+    b, lo, hi, st, p0, p1 = x
+    return T[b][p0:p1, lo:hi:st] if st != 1 else T[b][p0:p1, lo:hi]
+
+
+def nel(x):
+    return 16 * nel(x[2]) if x[0] == "*" else (x[2] - x[1] + x[3] - 1) // x[3]
+
+
+def two(*xs):
+    return all(SCRATCH[x[0]][2] in (B, U) for x in xs)
+
+
+def program():
+    ops = []
+    half = [1]
+
+    def add(eng, fn, R, W, cost, sem=None, lat=0.0, grp=None):
+        rr, ww = [], []
+        for x in R:
+            if isinstance(x, tuple):
+                rr += [x[1], x[2]] if x[0] == "*" else [x]
+        for x in W:
+            if x[0] == "*":
+                ww.append(x[1]); rr.append(x[2])
+            else:
+                ww.append(x)
+        ops.append({"e": eng, "f": fn, "R": rr, "W": ww, "c": cost, "sem": sem, "lat": lat, "grp": grp, "h": half[0]})
+
+    def val(T, x):
+        return ap(T, x) if isinstance(x, tuple) else x
+
+    def vc(o, a, k):
+        if a[0] == "*":
+            return 55 + GAM * nel(a)
+        if o[0] == "*":
+            return 55 + SCA * nel(o)
+        return max(64, nel(a) * k)
+
+    def TS(o, a, s1, op0, s2=None, op1=None):
+        k = 0.5 if a[0] != "*" and two(o, a) else 1
+        if op1 is None:
+            add("V", lambda g, T, x: g.vector.tensor_scalar(ap(T, o), ap(T, a), val(T, s1), None, op0), [a, s1], [o], vc(o, a, k))
+        else:
+            add("V", lambda g, T, x: g.vector.tensor_scalar(ap(T, o), ap(T, a), val(T, s1), val(T, s2), op0, op1), [a, s1, s2], [o], vc(o, a, k))
+
+    def TT(o, a, b, op):
+        k = 1 if (a[0] in PSUM or b[0] in PSUM) else 2
+        add("V", lambda g, T, x: g.vector.tensor_tensor(ap(T, o), ap(T, a), ap(T, b), op), [a, b], [o], vc(o, a, k))
+
+    def CP(o, a):
+        k = 0.5 if a[0] != "*" and two(o, a) else 1
+        add("V", lambda g, T, x: g.vector.tensor_copy(ap(T, o), ap(T, a)), [a], [o], vc(o, a, k))
+
+    def MS(o, c):
+        add("V", lambda g, T, x: g.vector.memset(ap(T, o), c), [], [o], max(64, nel(o) * (0.5 if two(o) else 1)))
+
+    def SC(o, a, b, init, op0, op1):
+        add("V", lambda g, T, x: g.vector.tensor_tensor_scan(ap(T, o), ap(T, a), ap(T, b), init, op0, op1), [a, b], [o], max(64, nel(o)))
+
+    def VT(o, a):
+        add("V", lambda g, T, x: g.vector.transpose(ap(T, o), ap(T, a)), [a], [o], max(64, nel(o)))
+
+    def AC(o, a, fn=AF.Identity, bias=0.0, scale=1.0, acc=None):
+        c = 70 + GAM * nel(a) if a[0] == "*" else max(64, nel(a))
+        if acc is None:
+            add("A", lambda g, T, x: g.scalar.activation(ap(T, o), ap(T, a), fn, bias=val(T, bias), scale=val(T, scale)), [a, bias, scale], [o], c)
+        else:
+            add("A", lambda g, T, x: g.scalar.activation(ap(T, o), ap(T, a), fn, bias=val(T, bias), scale=val(T, scale), accum_out=ap(T, acc)),
+                [a, bias, scale], [o, acc], c + (20 if o[0] not in PSUM else 140))
+
+    def MM(o, l, r, start, stop):
+        c = LAT["pe"] * max(64, nel(r)) * (4 if SCRATCH[l[0]][2] == F else 1)
+        add("P", lambda g, T, x: g.tensor.matmul(ap(T, o), ap(T, l), ap(T, r), start, stop), [l, r], [o], c, grp=True)
+
+    def TR(o, a):
+        add("P", lambda g, T, x: g.tensor.transpose(ap(T, o), ap(T, a), ap(T, s("I16"))), [a, s("I16")], [o], 128 * LAT["pe"], grp=True)
+
+    def IO(o, pat, base, cm):
+        if SCRATCH[o[0]][2] == I:
+            add("G", lambda g, T, x: g.iota(ap(T, o), pat, base, cm), [], [o], 130 + 2 * nel(o))
+        else:
+            add("G", lambda g, T, x: g.iota(ap(T, o), pat, base, cm, allow_small_or_imprecise_dtypes=True), [], [o], 130 + 2 * nel(o))
+
+    def LD(q, o, name, sem, lat, after=()):
+        if q == "S":
+            add(q, lambda g, T, x: g.sync.dma_start(ap(T, o), T[name][:]), list(after), [o], 60, sem=(sem, 16), lat=lat)
+        else:
+            add(q, lambda g, T, x: g.scalar.dma_start(ap(T, o), T[name][:]), list(after), [o], 60, sem=(sem, 16), lat=lat)
+
+    def col(b, j):
+        return s(b, j, j + 1)
+
+    mul, ad, sub, mx, mn = ALU.mult, ALU.add, ALU.subtract, ALU.max, ALU.min
+    band, shr = ALU.bitwise_and, ALU.logical_shift_right
+    I32 = s("Pf", 16, 144)
+
+    LD("A", s("X0"), "x0", "dx0", LAT["x"])
+    LD("S", s("cin"), "c0", "dc", 2300)
+    LD("S", s("yin"), "y0", "dy", 2300)
+    LD("S", s("wb", 0, 1), "w", "dw", 2300)
+    LD("S", s("stb"), "st", "ds", 3000)
+    LD("S", s("th8", p1=8), "th", "dt", 2500)
+    X2 = CFG["X2"]
+    if X2:
+        LD("S", s("X1"), "x0", "dx1", 5500, after=[s("X0")])
+    IO(col("pi", 0), [[0, 1]], 0, 1)
+    IO(s("iot"), [[1, 160]], 0, 0)
+    TS(col("pb", 0), col("pi", 0), 4, shr)
+    TS(col("pb", 1), col("pi", 0), 15, band)
+    TS(col("pb", 2), col("pi", 0), 3, shr)
+    TS(col("pb", 3), col("pi", 0), 7, band)
+    TS(col("pb", 4), col("pi", 0), 4, shr, 1, band)
+    for j, (b, k, m_, a_) in enumerate([("pi", 0, 1, 0), ("pi", 0, 1, 16), ("pb", 0, 1, 0), ("pb", 0, 16, 15), ("pb", 1, 1, 2032), ("pb", 2, 1, 0),
+                                        ("pb", 3, 1, 0), ("pb", 4, 1, 0), ("pb", 4, -1, 1), ("pb", 2, -1, 16), ("pi", 0, 16, 15), ("pb", 0, -16, 0),
+                                        ("pb", 0, -512, 0)]):
+        TS(col("pc", j), col(b, k), float(m_), mul, float(a_), ad)
+    eq = ALU.is_equal
+    TS(s("P0"), s("iot"), col("pc", 1), eq, col("pc", 8), mul)
+    TS(s("P1"), s("iot"), col("pc", 1), eq, col("pc", 7), mul)
+    TS(s("Pf"), s("iot"), col("pc", 1), eq)
+    TS(s("I16"), s("iot", 0, 128), col("pc", 0), eq)
+    CP(col("pc", 13), col("wb", 0))
+    TS(s("Ww"), s("iot", 0, 144), col("pc", 3), eq, col("pc", 13), mul)
+    TS(s("W1"), s("iot", 0, 144), col("pc", 3), eq)
+    TS(s("WA"), s("iot", 0, 144), col("pc", 3), eq, float(2 ** 18), mul)
+    TS(s("W8"), s("iot", 0, 144), col("pc", 10), eq)
+    MS(s("zer"), 0.0)
+    MS(s("neg"), -192.0)
+    MS(s("c2k"), 4.0)
+    if "V" in CFG["SG"]:
+        MS(s("kc2"), 0.0)
+        for c in range(4):
+            if CFG["SG"][c] == "V":
+                MS(s("kc2", 16 * c, 16 * c + 16), -float(2 ** 22))
+    MS(s("o16"), 16.0)
+    IO(s("kk8"), [[1, 16], [0, 8]], 0, 0)
+    IO(s("ii8"), [[0, 16], [1, 8]], 0, 0)
+    TS(s("ta"), s("kk8"), col("pc", 5), eq, col("pc", 5), mul)
+    TS(s("tb"), s("kk8"), col("pc", 5), ALU.is_gt, col("pc", 9), sub)
+    TT(s("ta"), s("ta"), s("tb"), sub)
+    TS(s("tb"), s("ii8"), col("pc", 6), eq, 0.125, mul)
+    TT(s("Mx"), s("ta"), s("tb"), mul)
+    TS(s("ME", 0, 8), s("Mx", 0, 8), 1.0 / 32, mul)
+    MS(s("sel"), -1.0)
+    for h in range(2):
+        x_ = s("sel", p0=64 * h, p1=64 * h + 64)
+        add("G", lambda g, T, x, x_=x_: g.affine_select(ap(T, x_), ap(T, x_), [[-16, 4], [0, 16], [-1, 16]], eq, 0.0, 0, 1), [x_], [x_], 2200)
+    IO(s("kc"), [[-4096, 64]], 63 * 4096, 0)
+    IO(s("kap", 0, 72), [[-256, 4], [-16, 18]], 2048, 0)
+    IO(s("kap", 72, 144), [[-256, 4], [-16, 18]], -2063, 0)
+    IO(s("kk16"), [[1, 8], [0, 16]], 0, 0)
+    TS(s("Wb"), s("kk16"), col("pc", 2), eq, col("pc", 13), mul)
+    MS(s("d0k"), BIG)
+    MS(s("d0k", 0, 64, 16), -BIG)
+    MS(s("d0k", 1, 64, 16), -BIG)
+    MS(s("lo4"), 0.0)
+    MS(s("lo4", 0, 72, 18), 1.0)
+    MS(s("lo4", 17, 72, 18), -BIG)
+    MS(s("thm"), -1.0)
+    MS(s("thm", 17, 72, 18), 0.0)
+    MS(s("thZ"), 0.0)
+    IO(s("ji", 0, 10), [[16, 10]], 0, 1)
+    TS(s("jf", 0, 10), s("ji", 0, 10), col("pc", 11), ad)
+    TS(s("jq", 0, 10), s("jf", 0, 10), 1.0 / 18, mul, -0.47, ad)
+    CP(s("Lm", 0, 10), s("jq", 0, 10))
+    IO(s("ji", 12, 16), [[18, 4]], 1, 1)
+    TS(s("Lc", 0, 4), s("ji", 12, 16), col("pc", 11), ad)
+    IO(s("l32b"), [[512, 8]], 0, 32)
+    TS(s("l32"), s("l32b"), col("pc", 12), ad)
+    for h in "01":
+        MS(s("A" + h, 72, 80), 0.0)
+        MS(s("Ms" + h), 0.0)
+        MS(s("ab" + h), 0.0)
+        MS(s("pS" + h, 399, 400), 0.0)
+    TS(s("ycs"), s("cin"), -2048.0, ad)
+    VT(s("ct"), s("ycs"))
+    for h in range(2):
+        ps = "pB%d0" % h
+        MM(s(ps, 340, 412), s("zer"), s("zer", 0, 72), True, False)
+        for c in range(4):
+            for g2 in range(2):
+                o_ = 16 + 16 * (c & 1) - 16 * g2
+                k0 = 32 * (2 * h + (c >> 1)) + 16 * g2
+                MM(s(ps, 341 + 18 * c, 357 + 18 * c), s("P%d" % (c & 1), o_, o_ + 128), s("ct", k0, k0 + 16), False, c == 3 and g2 == 1)
+        AC(s("A%d" % h, 0, 72), s(ps, 340, 412))
+
+    def sums(t, ysrc):
+        a, b = 8 * t, 8 * t + 8
+        if t > 0:
+            MM(s("pS1", 472, 480), s("Wb"), s("neg", 0, 8), True, False)
+        for r in range(16):
+            MM(s("pS1", 472, 480), s("Ww", 15 - r, 143 - r), s(ysrc, r, 128, 16), t == 0 and r == 0, r == 15)
+        CP(s("ui"), s("pS1", 472, 480))
+        TS(s("uI", a, b), s("ui"), 2047, band)
+        TS(s("mU", a, b), s("uI", a, b), 2.0, mul, 33.0, ad)
+        if t == 0:
+            AC(s("oU", a, b), s("mU", a, b), scale=2048.0, bias=-float(2 ** 22))
+        else:
+            MM(s("pS1", 480, 482), s("o16"), s("cnt", 2 * t - 2, 2 * t), True, True)
+            AC(s("Acol", 8, 10), s("pS1", 480, 482), bias=float(8192 - 2 ** 21), acc=col("Acol", t))
+            AC(s("oU", a, b), s("mU", a, b), scale=2048.0, bias=col("Acol", t))
+        TS(s("ub", 0, 8), s("ui"), 1, band)
+        TS(s("ob", a, b), s("ub", 0, 8), 1024.0, mul, 4096.0, ad)
+        if t < RO - 1:
+            TS(s("ub", 8, 16), s("ui"), 31, band)
+            TT(s("cx"), s("ub", 8, 16), s("l32"), ad)
+            CP(s("col", a, b), s("cx"))
+
+    def bank(h, c):
+        if CFG["BK"]:
+            return "pB%d%d" % (c >> 1, c & 1), 0
+        return "pB%d%d" % (h, c & 1), 256 * (c >> 1)
+
+    def renew(t, into):
+        TT(ind(s("X%d" % into), s("col", 8 * t, 8 * t + 8)), s("wv", 128 * t, 128 * t + 128), s("neg"), ad)
+
+    def places(h, mb, m0, ob_, o0):
+        H = str(h)
+        for c in range(4):
+            TS(s("t" + H, 16 * c, 16 * c + 16), s("A" + H, 18 * c + 1, 18 * c + 17), col(mb, m0 + c), mul, col(ob_, o0 + c), ad)
+        TS(s("p" + H), s("t" + H), 0x1FFFF, band, 5, shr)
+        CP(s("off" + H), s("p" + H))
+
+    def gather(h, t, out, plan):
+        for c in range(4):
+            (CP if plan[c] == "V" else AC)(s(out, 256 * c, 256 * c + 256), ind(s("X%d" % (t & X2)), s("off%d" % h, 16 * c, 16 * c + 16)))
+
+    def front(t, h):
+        H = str(h); ps = "pS" + H; A = "A" + H; u0 = 8 * t + 4 * h; y0 = PW * (2 * t + h); v0 = 328
+        half[0] = 1 - h
+        places(h, "mU", u0, "oU", u0)
+        AC(s("C" + H), ind(s(A), s("Lc", 0, 4)), bias=float(2 ** 22 + 2 ** 18 + 2048))
+        gather(h, t, "xa" + H, CFG["G1"])
+        for c in range(4):
+            px, w = "pX%d" % (c & 1), 256 * (c >> 1)
+            pb, z = bank(h, c)
+            MM(s(pb, z, z + 256), s("sT", 128 * t, 128 * t + 128, 1, 64 * h, 64 * h + 64), s("sel", 256 * c, 256 * c + 256, 1, 64 * h, 64 * h + 64), True, False)
+            for b in range(2):
+                TR(s(px, w + 128 * b, w + 128 * b + 128), s("xa" + H, 256 * c + b, 256 * c + 256, 2))
+            (CP if CFG["CP"][c] == "V" else AC)(s("xT" + H, 256 * c, 256 * c + 256), s(px, w, w + 256))
+            for b in range(2):
+                MM(s(pb, z + b, z + 256, 2), s("xT" + H, 256 * c + 128 * b, 256 * c + 128 * b + 128), s("Mx"), False, b == 1)
+            if CFG["SG"][c] == "V":
+                TS(s("ind" + H, 256 * c, 256 * c + 256), s(pb, z, z + 256), 0.0, ALU.is_ge, 2.0, mul)
+            else:
+                AC(s("ind" + H, 256 * c, 256 * c + 256), s(pb, z, z + 256), AF.Sign, bias=0.0625)
+        for ch in range(8):
+            c, b = ch >> 1, ch & 1
+            MM(s(ps, 64 + 16 * c + b, 80 + 16 * c, 2), s("xT" + H, 128 * ch, 128 * ch + 128), s("ME", 0, 8), True, True)
+        MM(s(ps, 0, 64), I32, s("C" + H), True, False)
+        MM(s(ps, 0, 64), s("I16"), s("kc"), False, False)
+        if "V" in CFG["SG"]:
+            MM(s(ps, 0, 64), s("I16"), s("kc2"), False, False)
+        for r in range(16):
+            MM(s(ps, 0, 64), s("WA", 15 - r, 143 - r), s("ind" + H, r, 1024, 16), False, r == 15)
+        SC(s("S" + H), s("d0k"), s(ps, 0, 64), -BIG, mn, mx)
+        K0, KS = s("S" + H, 0, 64, 16), s("S" + H, 15, 64, 16)
+        q = lambda b, j=0: s(b + H, j, j + 4)
+        CP(q("Ki"), KS)
+        TS(q("oi"), q("Ki"), 8, shr, 0x7F0, band)
+        TS(q("ov"), q("oi"), -1.0, mul, col("pc", 4), ad)
+        AC(s("pay", y0, y0 + 64), ind(s("xa" + H), q("ov")))
+        TS(q("ei"), q("Ki"), 4095, band)
+        ee, me, oe, gs = [s("pay", y0 + 64 + 4 * j, y0 + 68 + 4 * j) for j in range(4)]
+        TS(ee, q("ei"), -2048.0, ad)
+        if CFG["ME"][0] == "V":
+            TS(me, q("ei"), 32.0, ad)
+        else:
+            AC(me, ee, bias=2080.0)
+        if CFG["ME"][1] == "V":
+            TS(oe, q("ei"), -2048.0, ad, 3232.0, mul)
+        else:
+            AC(oe, ee, scale=3232.0)
+        if CFG["NR"] == "V":
+            TS(q("nr"), K0, float(9 * 2 ** 19), ALU.is_lt, 65536.0, mul)
+        else:
+            AC(q("nr"), K0, AF.Relu, scale=-65536.0, bias=float(9 * 2 ** 35))
+        TT(q("nr", 4), K0, KS, sub)
+        TT(q("nr", 8), q("nr"), q("nr", 4), mul)
+        if t < RO - 1:
+            AC(gs, q("nr", 8), AF.Sign, bias=-1.0, acc=col("cnt", 2 * t + h))
+        else:
+            AC(gs, q("nr", 8), AF.Sign, bias=-1.0)
+        n = 2 * t + h
+        add("G", lambda g, T, x: x["send"](n), [s("pay", y0, y0 + PW)], [s("land", y0, y0 + PW)], LAT["call"],
+            sem=("arr%d" % n, 0), lat=LAT["hop"] if t & 1 else 2 * LAT["hop"] + LAT["call"])
+        AC(s("y128", 64 * h, 64 * h + 64), s(ps, 64, 128), scale=8.0, bias=192.0 - 31.0 / 64)
+        if t < RO - 1:
+            if h == 0:
+                AC(s("hx"), ind(s("X%d" % (t & X2)), s("col", 8 * t, 8 * t + 8)), scale=0.5, bias=192.0 - 255.0 / 512)
+            TT(s("wv", 128 * t + 64 * h, 128 * t + 64 * h + 64), s("hx", 64 * h, 64 * h + 64), s(ps, 64, 128), ad)
+        AC(s(A, 0, 72, 18), ee)
+        TT(q("fi"), me, s("uI", u0, u0 + 4), mul)
+        TS(q("fi", 4), q("fi"), 0x1FFFF, band, 5, shr)
+        TS(s(A, 17, 72, 18), q("fi", 4), -2048.0, ad)
+        TT(q("TH"), q("oi"), q("nr", 8), mn)
+        TT(q("oo"), q("oi"), s("ob", u0, u0 + 4), sub)
+        TT(q("TH", 4), q("oo"), q("nr", 8), mx)
+        TT(s("mk" + H), ind(s("TH" + H), s("Lm", 0, 9)), s("kap"), ALU.is_ge)
+        TT(s(ps, v0, v0 + 71), s(A, 1, 72), s(A, 0, 71), sub)
+        TT(s(ps, v0 + 72, v0 + 143), s("mk" + H, 72, 143), s(ps, v0, v0 + 71), mul)
+        TT(s(ps, v0, v0 + 71), s("mk" + H, 0, 71), s(ps, v0, v0 + 71), mul)
+        TT(s("Q" + H, 0, 70), s(A, 0, 70), s(ps, v0 + 72, v0 + 142), ad)
+        TT(s(A, 1, 71), s("Q" + H, 0, 70), s(ps, v0 + 1, v0 + 71), ad)
+
+    def back(t, h):
+        H = str(h); ps = "pS" + H; A = "A" + H; y0 = PW * (2 * t + h); w0 = 399
+        half[0] = 1 - h
+        places(h, "land", y0 + 68, "land", y0 + 72)
+        MM(s(ps, 200, 328, 1, 0, 64), s("land", y0, y0 + 64), I32, True, True)
+        AC(s("vT" + H, p1=64), s(ps, 200, 328, 1, 0, 64))
+        gather(h, t, "g2" + H, CFG["G2"])
+        if CFG["EP"] == "V":
+            ep = s("ep" + H, 1, 71)
+            TT(s("ep" + H), ind(s("land", y0 + 64, y0 + 80), s("Lm", 0, 5)), s(A), sub)
+        elif CFG["EP"] == "S":
+            ep = s("ep" + H, 1, 71)
+            for c in range(4):
+                AC(s("ep" + H, 1 + 18 * c, 19 + 18 * c), s(A, 18 * c + 1, 18 * c + 19), scale=-1.0, bias=col("land", y0 + 64 + c))
+        else:
+            ep = s(ps, 329, 399)
+            for c in range(4):
+                AC(s(ps, 329 + 18 * c, 345 + 18 * c), s(A, 18 * c + 1, 18 * c + 17), scale=-1.0, bias=col("land", y0 + 64 + c))
+        for c in range(4):
+            pb, z = bank(h, c)
+            o_ = s(pb, z, z + 256)
+            MM(o_, s("vT" + H, p1=64), s("sel", 256 * c, 256 * c + 256, 1, 0, 64), True, False)
+            MM(o_, s("I16"), s("g2" + H, 256 * c, 256 * c + 256), False, True)
+            AC(s("ab" + H, 288 * c + 16, 288 * c + 272), o_, AF.Abs)
+        MM(s(ps, 128, 200), s("I16"), s("thb" + H, 0, 72), True, False)
+        MM(s(ps, 145, 200, 18), I32, s("land", y0 + 76, y0 + 80), False, False)
+        for r in range(16):
+            MM(s(ps, 128, 200), s("W1", 15 - r, 143 - r), s("ab" + H, r, 1152, 16), False, r == 15)
+        SC(s("H" + H, 0, 72), s(ps, 128, 200), s("lo4"), 1.0, mn, mx)
+        for c in range(4):
+            TS(s("Ms" + H, 18 * c, 18 * c + 16), s("H" + H, 18 * c, 18 * c + 16), col("H" + H, 18 * c + 17), ALU.is_le)
+        TT(s(ps, w0 + 1, w0 + 71), s("Ms" + H, 0, 70), ep, mul)
+        TT(s("Q" + H, 1, 71), s(A, 1, 71), s(ps, w0 + 1, w0 + 71), ad)
+        TT(s(A, 1, 71), s("Q" + H, 1, 71), s(ps, w0, w0 + 70), sub)
+
+    def finish(h):
+        H = str(h); ps = "pS" + H
+        MM(s(ps, 0, 64), s("c2k"), s("c2k", 0, 64), True, False)
+        for cp in range(2):
+            for g2 in range(2):
+                for c2 in range(2):
+                    o_ = 16 + 16 * g2 - 16 * c2; k0 = 18 * (2 * cp + c2) + 1; w = 32 * cp + 16 * g2
+                    MM(s(ps, w, w + 16), s("P%d" % g2, o_, o_ + 128), s("A" + H, k0, k0 + 16), False, cp + g2 + c2 == 3)
+        VT(s("ycs", 64 * h, 64 * h + 64), s(ps, 0, 64))
+        x_ = s("ycs", 64 * h, 64 * h + 64)
+        add("S", lambda g, T, x: g.sync.dma_start(T.yc[:, 64 * h:64 * h + 64], ap(T, x_)), [x_], [], 60, sem=("dyc" + H, 16), lat=2000)
+
+    sums(0, "yin")
+    for t in range(RO):
+        TR(s("pX1", 128 * t, 128 * t + 128), s("stb", 128 * t, 128 * t + 128))
+    CP(s("sT"), s("pX1", 0, 640))
+    for r in range(16):
+        MM(s("pB11", 0, 8), s("W8", 15 - r, 143 - r, 1, 0, 8), s("th8", r, 128, 16, 0, 8), r == 0, r == 15)
+    for h in range(2):
+        AC(s("thZ", 8 * h, 8 * h + 4), s("pB11", 4 * h, 4 + 4 * h))
+        TT(s("thb%d" % h), ind(s("thZ", 8 * h, 8 * h + 8), s("Lm", 0, 5)), s("thm"), mul)
+    front(0, 0)
+    front(0, 1)
+    for t in range(RO):
+        if t < RO - 1:
+            sums(t + 1, "y128")
+            if X2:
+                renew(t, (t + 1) & 1)
+        else:
+            TS(s("yo"), s("y128"), -192.0, ad)
+            add("S", lambda g, T, x: g.sync.dma_start(T.yy[:], T["yo"][:]), [s("yo")], [], 60, sem=("dyy", 16), lat=2000)
+        back(t, 0)
+        if not X2:
+            back(t, 1)
+            if t < RO - 1:
+                renew(t, 0)
+            for h in range(2):
+                if t < RO - 1:
+                    front(t + 1, h)
+                else:
+                    finish(h)
+            continue
+        if t < RO - 1:
+            front(t + 1, 0)
+        else:
+            finish(0)
+        back(t, 1)
+        if t < RO - 2:
+            renew(t, t & 1)
+        if t < RO - 1:
+            front(t + 1, 1)
+        else:
+            finish(1)
+    return ops
+
+
+XLAT, QLAT = 120.0, 70.0
+TRY, SWEEPS = [(20.0, 0.0), (40.0, 0.0), (60.0, 1500.0)], 4
+CLIMB, SLACK, MODES = 3000, 0.0, [(1.0, 1.0), (1.5, 1.0), (0.75, 1.4)]
+
+
+def meets(a, b):
+    if not (a[0] == b[0] and a[1] < b[2] and b[1] < a[2] and a[4] < b[5] and b[4] < a[5]):
+        return False
+    return (a[3] == 1 and b[3] == 1) or not set(range(a[1], a[2], a[3])).isdisjoint(range(b[1], b[2], b[3]))
+
+
+def schedule():
+    ops = program()
+    n = len(ops)
+    hist, run = {}, {}
+    for i, o in enumerate(ops):
+        dep = {}
+        for kind in "RW":
+            for x in o[kind]:
+                for j, k2, y in hist.get(x[0], []):
+                    p = ops[j]
+                    same = p["e"] == o["e"] and p["sem"] is None and o["sem"] is None
+                    if x[0] in PSUM and not same:
+                        dep[j] = True
+                    elif x[0] in PSUM and o["grp"]:
+                        dep.setdefault(j, False)
+                    elif (kind == "W" or k2 == "W") and meets(x, y):
+                        if not same or k2 == "W" or SAMEQ_WAR:
+                            dep[j] = True
+                        else:
+                            dep.setdefault(j, False)
+        o["d"] = dep
+        for kind in "RW":
+            for x in o[kind]:
+                hs = hist.setdefault(x[0], [])
+                if x[0] in PSUM:
+                    if hs and ops[hs[-1][0]]["e"] != o["e"]:
+                        hs[:] = [z for z in hs if ops[z[0]]["e"] == ops[hs[-1][0]]["e"] and z[0] >= run.get(x[0], 0)]
+                        run[x[0]] = i
+                    elif o["grp"] and hs:
+                        hs[:] = [z for z in hs if z[0] < run.get(x[0], 0)]
+                elif kind == "W" and x[3] == 1:
+                    hs[:] = [z for z in hs if not (x[1] <= z[2][1] and z[2][2] <= x[2] and x[4] <= z[2][4] and z[2][5] <= x[5])]
+                hs.append((i, kind, x))
+    succ = [[] for _ in ops]
+    for i, o in enumerate(ops):
+        for j in o["d"]:
+            succ[j].append(i)
+
+    def gap(j, i):
+        if not ops[i]["d"][j]:
+            return 0.0
+        return ops[j]["lat"] + (QLAT if ops[j]["e"] == ops[i]["e"] and ops[j]["sem"] is None else XLAT)
+
+    level = [0.0] * n
+    for i in range(n - 1, -1, -1):
+        level[i] = ops[i]["c"] + max([gap(i, k) + level[k] for k in succ[i]] + [ops[i]["lat"]])
+    pred = [[(j, gap(j, i)) for j in o["d"]] for i, o in enumerate(ops)]
+    post = [[(k, gap(i, k)) for k in succ[i]] for i in range(n)]
+
+    def sweep(before, after, prio, first, win):
+        left = [len(b) for b in before]
+        ready = {e: {} for e in "VAPGS"}
+        for i in range(n):
+            if left[i] == 0:
+                ready[ops[i]["e"]][i] = first[i]
+        free = {e: 0.0 for e in "VAPGS"}
+        fin = [0.0] * n
+        order = []
+        while len(order) < n:
+            t0, e0 = min((max(min(r.values()), free[e]), e) for e, r in ready.items() if r)
+            i = max((i for i, r in ready[e0].items() if r <= t0 + win), key=lambda i: (prio[i], -i))
+            fin[i] = max(ready[e0].pop(i), free[e0]) + ops[i]["c"]
+            free[e0] = fin[i]
+            order.append(i)
+            for k, _ in after[i]:
+                left[k] -= 1
+                if left[k] == 0:
+                    ready[ops[k]["e"]][k] = max([first[k]] + [fin[j] + d for j, d in before[k]])
+        return order, fin
+
+    best = None
+    tail = [o["lat"] if not succ[i] else 0.0 for i, o in enumerate(ops)]
+    for win, bias in TRY:
+        prio = [level[i] + bias * ops[i]["h"] for i in range(n)]
+        for it in range(SWEEPS):
+            order, fin = sweep(pred, post, prio, [0.0] * n, win)
+            end = max(fin[i] + tail[i] for i in range(n))
+            if best is None or end < best[0]:
+                best = (end, order, fin)
+            prio = sweep(post, pred, fin, tail, win)[1]
+
+    eng, cost = [o["e"] for o in ops], [o["c"] for o in ops]
+    ends = [i for i in range(n) if not succ[i]]
+
+    def replay(order, k, pe, fin):
+        free = {e: 0.0 for e in "VAPGS"}
+        for i in order:
+            e = eng[i]
+            st = free[e]
+            for j, d in pred[i]:
+                x = fin[j] + d * k
+                if x > st:
+                    st = x
+            fin[i] = free[e] = st + (cost[i] * pe if e == "P" else cost[i])
+        return max(fin[i] + tail[i] for i in ends)
+
+    def worth(order):
+        return sum(replay(order, k, pe, fin) for k, pe in MODES)
+
+    order, fin = best[1], list(best[2])
+    top, seed, moved = worth(order), 12345, False
+    gold = (top, order)
+    for it in range(CLIMB):
+        seed = (seed * 1103515245 + 12345) % 2 ** 31
+        if it == 0 or moved:
+            k, pe = MODES[(seed >> 10) % 3]
+            at, lastq, f, why = {}, {}, [0.0] * n, [None] * n
+            for p, i in enumerate(order):
+                at[i] = p
+                q = lastq.get(eng[i])
+                st, why[i] = (f[q], (q, True)) if q is not None else (0.0, None)
+                for j, d in pred[i]:
+                    if f[j] + d * k >= st:
+                        st, why[i] = f[j] + d * k, (j, False)
+                f[i] = st + cost[i] * (pe if eng[i] == "P" else 1.0)
+                lastq[eng[i]] = i
+            i = max(range(n), key=lambda i: f[i] + tail[i])
+            arcs = []
+            while why[i] is not None:
+                if why[i][1]:
+                    arcs.append((why[i][0], i))
+                i = why[i][0]
+            byq = {e: [i for i in order if eng[i] == e] for e in "VAPGS"}
+        moved = False
+        a, b = arcs[(seed >> 8) % len(arcs)]
+        qa = byq[eng[a]]
+        pa = qa.index(a)
+        first = qa[max(0, pa - (0, 0, 1, 2, 3, 5)[(seed >> 20) % 6])]
+        late = set(i for i in qa[qa.index(first):pa + 1])
+        keep, push = [], []
+        for i in order[at[first]:at[b] + 1]:
+            if i in late or any(j in late for j, _ in pred[i]):
+                late.add(i); push.append(i)
+            else:
+                keep.append(i)
+        if b in late:
+            continue
+        o2 = order[:at[first]] + keep + push + order[at[b] + 1:]
+        w = worth(o2)
+        if w <= top + SLACK * (1.0 - it / CLIMB):
+            top, order, moved = w, o2, True
+            if w < gold[0]:
+                gold = (w, o2)
+    order = gold[1]
+    replay(order, 1.0, 1.0, fin)
+    for i in order:
+        ops[i]["t"] = fin[i] - ops[i]["c"]
+    pos, seen = {}, {e: 0 for e in "VAPGS"}
+    for i in order:
+        if ops[i]["sem"] is None:
+            seen[ops[i]["e"]] += 1
+            pos[i] = (ops[i]["e"], seen[ops[i]["e"]])
+        else:
+            pos[i] = (ops[i]["sem"][0], 1)
+    know = {e: {} for e in "VAPGS"}
+    clock = {}
+    need = set()
+    lastg = []
+    for i in order:
+        o = ops[i]; kn = know[o["e"]]
+        want = {}
+        if o["e"] == "G" and o["sem"] is None:
+            if lastg:
+                want["G"] = (pos[lastg[-1]][1], lastg[-1])
+            lastg.append(i)
+        for j, sem in o["d"].items():
+            if sem and pos[j][1] > want.get(pos[j][0], (0, 0))[0]:
+                want[pos[j][0]] = (pos[j][1], j)
+        o["w"] = []
+        for key, (v, j) in sorted(want.items(), key=lambda kv: -fin[kv[1][1]] - ops[kv[1][1]]["lat"]):
+            if kn.get(key, 0) < v:
+                o["w"].append(j); need.add(j)
+                for k2, v2 in clock[j].items():
+                    if kn.get(k2, 0) < v2:
+                        kn[k2] = v2
+        ck = {} if o["sem"] is not None and o["sem"][1] == 0 else dict(kn)
+        ck[pos[i][0]] = pos[i][1]
+        clock[i] = ck
+    count = {e: 0 for e in CNT}
+    for i in order:
+        if ops[i]["sem"] is None and i in need:
+            count[ops[i]["e"]] += 1
+            ops[i]["n"] = count[ops[i]["e"]]
+        else:
+            ops[i]["n"] = 0
+    return ops, order, max(fin[i] + ops[i]["lat"] for i in range(n))
+
+
+PLAN = []
+
+
+def route(T, topo, rank, t):
+    src = T.cores[rank]
+    dst = T.cores[(rank + 1 + t % (len(T.cores) - 1)) % len(T.cores)]
+    if topo.may_write(src, dst):
+        return dst, dst, topo.mask(src, dst)
+    via = [c for c in topo.cores_of(src) if c != src and topo.may_write(c, dst)]
+    via.sort(key=lambda c: (topo.die(c) != topo.die(src), c))
+    return via[0], dst, topo.mask(via[0], dst)
+
+
+def bits(m):
+    return bin(m).count("1")
+
+
+def rank_program(g, core, T, topo):
+    rank = T.rank_of(core)
+    N = len(T.cores)
+    if rank is None:
+        sent = 0
+        for r in range(N):
+            for t in range(RO):
+                via, dst, m = route(T, topo, r, t)
+                if via == core:
+                    rid, pid = topo.addr(dst, core)
+                    for n in (2 * t, 2 * t + 1):
+                        x = T["land"][:, PW * n:PW * n + PW]
+                        g.wait_ge(T.sem["arr%d" % n], bits(m))
+                        g.remote_dma(x, x, T.sem["arr%d" % n], T.sem.loc, pid, rid, m)
+                        sent += bits(m)
+        if sent:
+            g.wait_ge(T.sem.loc, sent)
+        return
+    if not PLAN:
+        PLAN.append(schedule())
+    ops, order, _ = PLAN[0]
+    sent = [0]
+
+    def send(n):
+        via, dst, m = route(T, topo, rank, n // 2)
+        rid, pid = topo.addr(via, core)
+        g.remote_dma(T["land"][:, PW * n:PW * n + PW], T["pay"][:, PW * n:PW * n + PW], T.sem["arr%d" % n], T.sem.loc, pid, rid, m)
+        sent[0] += bits(m)
+
+    def arrivals(n):
+        t = n // 2
+        return bits(route(T, topo, (rank - 1 - t % (N - 1)) % N, t)[2])
+
+    Q = {"V": g.vector, "A": g.scalar, "P": g.tensor, "G": g, "S": g.sync}
+    ctx = {"send": send}
+    for i in order:
+        o = ops[i]
+        for j in o["w"]:
+            p = ops[j]
+            if p["sem"] is None:
+                Q[o["e"]].wait_ge(T.sem[CNT[p["e"]]], p["n"])
+            else:
+                Q[o["e"]].wait_ge(T.sem[p["sem"][0]], p["sem"][1] or arrivals(int(p["sem"][0][3:])))
+        ins = o["f"](g, T, ctx)
+        if o["sem"] is not None and o["sem"][1]:
+            ins.then_inc(T.sem[o["sem"][0]], o["sem"][1])
+        elif o["n"]:
+            ins.then_inc(T.sem[CNT[o["e"]]], 1)
+    g.wait_ge(T.sem.loc, sent[0])
+    for name in ("dyy", "dyc0", "dyc1"):
+        g.sync.wait_ge(T.sem[name], 16)

@@ -1,54 +1,70 @@
 from concourse.mybir import AluOpType as ALU, ActivationFunctionType as AF
 
-F, B, I, U = "float32", "bfloat16", "int32", "uint16"
+F, B, I, U, H16 = "float32", "bfloat16", "int32", "uint16", "float16"
 RO, PW = 5, 80
 SCRATCH = {}
+CFG = {"G1": ["V01", "A12", "A23", "A34"], "G2": ["V01", "A12", "V23", "A34"], "UW": 1, "CP": "VVVV", "SG": "AAAV", "AB": "AAAA", "PL": "VV", "EP": "A",
+       "MS": "C", "ME": "VA", "NR": "A", "X2": 0, "NZ": 4, "NX": 2, "D3": 1, "MW": 1, "OR": 1, "OWN": "",
+       "BANK": {"K0": "pS0", "D0": "pS0", "K1": "pS0", "D1": "pS0", "E0": "pS0", "E1": "pS0", "U": "pS0", "V0": "pV", "V1": "pV", "P0": "pS0", "P1": "pS0"}}
 
 
 def _buf(name, n, dt, where="sbuf"):
-    SCRATCH[name] = (where, [128, n], dt)
+    SCRATCH[name] = (where, [128] + (n if isinstance(n, list) else [n]), dt)
 
 
-for _n, _w, _d in [
-    ("X0", 4096, B), ("X1", 4096, B), ("stb", 640, B), ("sT", 640, B), ("cin", 128, I), ("ct", 128, F),
-    ("yin", 128, B), ("wb", 16, B), ("th8", 128, B), ("thZ", 16, F), ("thm", 80, F),
-    ("pi", 8, I), ("pb", 8, I), ("pc", 16, F), ("iot", 160, F), ("kk8", 128, F), ("ii8", 128, F), ("kk16", 128, F),
-    ("ta", 128, F), ("tb", 128, F), ("I16", 128, B), ("Pf", 160, F), ("P0", 160, F), ("P1", 160, F),
-    ("W1", 144, B), ("WA", 144, B), ("Ww", 144, B), ("W8", 144, B), ("Wb", 128, B), ("Mx", 128, B), ("ME", 16, B),
-    ("sel", 1024, B), ("kc", 64, B), ("kap", 144, F), ("d0k", 64, F), ("lo4", 72, F), ("neg", 128, B), ("zer", 128, B),
-    ("c2k", 128, B), ("kc2", 64, B), ("o16", 128, F), ("ji", 16, I), ("jf", 16, F), ("jq", 16, I),
-    ("Lm", 16, U), ("Lc", 16, U), ("l32", 8, I), ("l32b", 8, I),
-    ("ui", 8, I), ("ub", 16, I), ("uI", 40, I), ("mU", 40, F), ("oU", 40, F), ("ob", 40, F), ("cx", 8, I), ("col", 40, U),
-    ("Acol", 16, F), ("cnt", 16, F), ("y128", 128, B), ("yo", 128, B), ("hx", 128, F), ("wv", 512, B),
-    ("ycs", 128, F), ("pay", 2 * RO * PW, F), ("land", 2 * RO * PW, F),
-]:
-    _buf(_n, _w, _d)
-for _h in "01":
-    for _n, _w, _d in [
-        ("A", 80, F), ("C", 64, F), ("t", 64, I), ("p", 64, I), ("off", 64, U), ("xa", 1024, B), ("xT", 1024, B),
-        ("ind", 1024, B), ("g2", 1024, B), ("ab", 1152, B), ("S", 64, F), ("Ki", 8, I), ("oi", 8, I), ("ei", 8, I),
-        ("fi", 8, I), ("ov", 8, U), ("nr", 16, F), ("TH", 8, F), ("oo", 8, F), ("mk", 144, F), ("Q", 80, F),
-        ("H", 80, F), ("Ms", 80, F), ("ep", 80, F), ("vT", 128, B), ("thb", 80, B),
+PSUM = []
+
+
+def declare():
+    SCRATCH.clear()
+    PSUM[:] = []
+    for n, w, d in [
+        ("X0", 4096, B), ("X1", 4096, B), ("stb", 640, B), ("sT", 640, B), ("cin", 128, I), ("ct", 128, H16), ("cf", 128, H16),
+        ("yin", 128, B), ("wb", 16, B), ("th8", 128, B), ("thZ", 16, F), ("thm", 80, F),
+        ("pi", 8, I), ("pb", 8, I), ("pc", 16, F), ("iot", 160, F), ("kk8", 128, F), ("ii8", 128, F), ("kk16", 128, F),
+        ("ta", 128, F), ("tb", 128, F), ("I16", 128, B), ("Pf", 160, F), ("P0", 160, H16), ("P1", 160, H16),
+        ("W1", 144, B), ("WA", 144, B), ("Ww", 144, B), ("W8", 144, B), ("Wb", 128, B), ("Mx", 128, B), ("ME", 16, B),
+        ("sel", 1024, B), ("kc", 72, B), ("kap", 144, F), ("d0k", 72, F), ("lo4", 72, F), ("neg", 128, B), ("zer", 128, B),
+        ("c2k", 128, B), ("o16", 128, F), ("ji", 16, I), ("jf", 16, F), ("jq", 16, I), ("jr", 16, F),
+        ("Lm", 16, U), ("Lh", 8, U), ("l32", 8, I), ("l32b", 8, I),
+        ("ui", 8, I), ("ub", 16, I), ("uI", 40, I), ("mU", 40, F), ("oU", 40, F), ("ob", 40, F), ("cx", 8, I), ("col", 40, U),
+        ("Acol", 16, F), ("cnt", 16, F), ("y128", 128, B), ("yo", 128, B), ("hx", 128, F), ("wv", 512, B),
+        ("ycs", 128, F), ("pay", 2 * RO * PW, F), ("land", 2 * RO * PW, F),
     ]:
-        _buf(_n + _h, _w, _d)
-PSUM = ["pB00", "pB01", "pB10", "pB11", "pS0", "pS1"]
-for _n in PSUM:
-    _buf(_n, 512, F, "psum")
-for _n in ("pX0", "pX1"):
-    _buf(_n, 1024, B, "psum")
-    PSUM.append(_n)
+        _buf(n, w, d)
+    wide = [4, 288] if CFG["D3"] else 1152
+    for h in "01":
+        for n, w, d in [
+            ("A", 80, F), ("Af", 80, H16), ("t", 64, I), ("tf", 64, F), ("p", 64, I), ("off", 64, U), ("xa", 1024, B), ("xT", 1024, B),
+            ("ind", wide, B), ("g2", 1024, B), ("ab", wide, B), ("S", 72, F), ("Ki", 8, I), ("oi", 8, I), ("ei", 8, I),
+            ("fi", 8, I), ("ov", 8, U), ("nr", 16, F), ("TH", 8, F), ("oo", 8, F), ("mk", 144, F), ("Q", 80, F),
+            ("H", 80, F), ("Ms", 80, F), ("ep", 80, F), ("vT", 128, B), ("thb", 80, B),
+        ]:
+            _buf(n + h, w, d)
+    for n in ["pZ%d" % j for j in range(CFG["NZ"])] + sorted(set(CFG["BANK"].values())):
+        _buf(n, 512, F, "psum")
+        PSUM.append(n)
+    for j in range(CFG["NX"]):
+        _buf("pX%d" % j, 1024, B, "psum")
+        PSUM.append("pX%d" % j)
+
+
+declare()
 DMAS = ["dc", "dy", "dw", "dx0", "dx1", "ds", "dt", "dyc0", "dyc1", "dyy"]
 SEMAPHORES = ["nV", "nA", "nP", "nG", "loc"] + DMAS + ["arr%d" % i for i in range(2 * RO)]
 CNT = {"V": "nV", "A": "nA", "P": "nP", "G": "nG"}
 BIG = 1.0e9
-GAM, SCA = 1.5, 3.5
-CFG = {"G1": "VAAA", "CP": "VVVV", "SG": "AVAV", "G2": "VAVA", "EP": "A", "ME": "VV", "X2": 0, "NR": "A", "BK": 1}
-LAT = {"x": 5000.0, "call": 900.0, "hop": 2600.0, "pe": 0.5}
-SAMEQ_WAR = True
+REG = {"K0": 72, "K1": 72, "D0": 72, "D1": 72, "E0": 64, "E1": 64, "U": 16, "V0": 216, "V1": 216, "P0": 72, "P1": 72}
 
 
-def s(b, lo=0, hi=None, st=1, p0=0, p1=128):
-    return (b, lo, SCRATCH[b][1][1] if hi is None else hi, st, p0, p1)
+def s(b, lo=0, hi=None, st=1, p0=0, p1=128, sg=None):
+    return (b, lo, SCRATCH[b][1][-1] if hi is None else hi, st, p0, p1, sg)
+
+
+def seg(b, c0, c1, lo, hi, st=1):
+    if CFG["D3"]:
+        return s(b, lo, hi, st, sg=(c0, c1))
+    return s(b, 288 * c0 + lo, 288 * (c1 - 1) + hi, st)
 
 
 def ind(w, o):
@@ -58,23 +74,38 @@ def ind(w, o):
 def ap(T, x):
     if x[0] == "*":
         return ap(T, x[1]).indirect(ap(T, x[2]))
-    b, lo, hi, st, p0, p1 = x
+    b, lo, hi, st, p0, p1, sg = x
+    if sg is not None:
+        return T[b][p0:p1, sg[0]:sg[1], lo:hi:st] if st != 1 else T[b][p0:p1, sg[0]:sg[1], lo:hi]
     return T[b][p0:p1, lo:hi:st] if st != 1 else T[b][p0:p1, lo:hi]
 
 
 def nel(x):
-    return 16 * nel(x[2]) if x[0] == "*" else (x[2] - x[1] + x[3] - 1) // x[3]
+    if x[0] == "*":
+        return 16 * nel(x[2])
+    return (x[2] - x[1] + x[3] - 1) // x[3] * (x[6][1] - x[6][0] if x[6] else 1)
 
 
 def two(*xs):
-    return all(SCRATCH[x[0]][2] in (B, U) for x in xs)
+    return all(SCRATCH[x[0]][2] in (B, U, H16) for x in xs)
 
 
 def program():
     ops = []
     half = [1]
+    at, used = {}, {}
+    for r_ in ("K0", "K1", "D0", "D1", "E0", "E1", "U", "V0", "V1", "P0", "P1"):
+        b_ = CFG["BANK"][r_]
+        at[r_] = (b_, used.get(b_, 0))
+        used[b_] = used.get(b_, 0) + REG[r_]
+        assert used[b_] <= 512 or (r_[0] == "P" and CFG["EP"] != "P")
 
-    def add(eng, fn, R, W, cost, sem=None, lat=0.0, grp=None):
+    def rg(r, lo, hi, st=1):
+        if r == "E":
+            r, lo, hi = ("E0", lo, hi) if lo < 64 else ("E1", lo - 64, hi - 64)
+        return s(at[r][0], at[r][1] + lo, at[r][1] + hi, st)
+
+    def add(eng, fn, R, W, kind, n, sem=None, grp=None):
         rr, ww = [], []
         for x in R:
             if isinstance(x, tuple):
@@ -84,68 +115,68 @@ def program():
                 ww.append(x[1]); rr.append(x[2])
             else:
                 ww.append(x)
-        ops.append({"e": eng, "f": fn, "R": rr, "W": ww, "c": cost, "sem": sem, "lat": lat, "grp": grp, "h": half[0]})
+        ops.append({"e": eng, "f": fn, "R": rr, "W": ww, "k": kind, "c": n, "sem": sem, "grp": grp, "h": half[0]})
 
     def val(T, x):
         return ap(T, x) if isinstance(x, tuple) else x
 
     def vc(o, a, k):
         if a[0] == "*":
-            return 55 + GAM * nel(a)
+            return "g", nel(a)
         if o[0] == "*":
-            return 55 + SCA * nel(o)
-        return max(64, nel(a) * k)
+            return "s", nel(o)
+        return "n", nel(a) * k
 
     def TS(o, a, s1, op0, s2=None, op1=None):
         k = 0.5 if a[0] != "*" and two(o, a) else 1
         if op1 is None:
-            add("V", lambda g, T, x: g.vector.tensor_scalar(ap(T, o), ap(T, a), val(T, s1), None, op0), [a, s1], [o], vc(o, a, k))
+            add("V", lambda g, T, x: g.vector.tensor_scalar(ap(T, o), ap(T, a), val(T, s1), None, op0), [a, s1], [o], *vc(o, a, k))
         else:
-            add("V", lambda g, T, x: g.vector.tensor_scalar(ap(T, o), ap(T, a), val(T, s1), val(T, s2), op0, op1), [a, s1, s2], [o], vc(o, a, k))
+            add("V", lambda g, T, x: g.vector.tensor_scalar(ap(T, o), ap(T, a), val(T, s1), val(T, s2), op0, op1), [a, s1, s2], [o], *vc(o, a, k))
 
     def TT(o, a, b, op):
         k = 1 if (a[0] in PSUM or b[0] in PSUM) else 2
-        add("V", lambda g, T, x: g.vector.tensor_tensor(ap(T, o), ap(T, a), ap(T, b), op), [a, b], [o], vc(o, a, k))
+        add("V", lambda g, T, x: g.vector.tensor_tensor(ap(T, o), ap(T, a), ap(T, b), op), [a, b], [o], *vc(o, a, k))
 
     def CP(o, a):
         k = 0.5 if a[0] != "*" and two(o, a) else 1
-        add("V", lambda g, T, x: g.vector.tensor_copy(ap(T, o), ap(T, a)), [a], [o], vc(o, a, k))
+        add("V", lambda g, T, x: g.vector.tensor_copy(ap(T, o), ap(T, a)), [a], [o], *vc(o, a, k))
 
     def MS(o, c):
-        add("V", lambda g, T, x: g.vector.memset(ap(T, o), c), [], [o], max(64, nel(o) * (0.5 if two(o) else 1)))
+        add("V", lambda g, T, x: g.vector.memset(ap(T, o), c), [], [o], "n", nel(o) * (0.5 if two(o) else 1))
 
     def SC(o, a, b, init, op0, op1):
-        add("V", lambda g, T, x: g.vector.tensor_tensor_scan(ap(T, o), ap(T, a), ap(T, b), init, op0, op1), [a, b], [o], max(64, nel(o)))
+        add("V", lambda g, T, x: g.vector.tensor_tensor_scan(ap(T, o), ap(T, a), ap(T, b), init, op0, op1), [a, b], [o], "n", nel(o))
 
     def VT(o, a):
-        add("V", lambda g, T, x: g.vector.transpose(ap(T, o), ap(T, a)), [a], [o], max(64, nel(o)))
+        add("V", lambda g, T, x: g.vector.transpose(ap(T, o), ap(T, a)), [a], [o], "n", nel(o))
 
     def AC(o, a, fn=AF.Identity, bias=0.0, scale=1.0, acc=None):
-        c = 70 + GAM * nel(a) if a[0] == "*" else max(64, nel(a))
+        k = "g" if a[0] == "*" else "n"
         if acc is None:
-            add("A", lambda g, T, x: g.scalar.activation(ap(T, o), ap(T, a), fn, bias=val(T, bias), scale=val(T, scale)), [a, bias, scale], [o], c)
+            add("A", lambda g, T, x: g.scalar.activation(ap(T, o), ap(T, a), fn, bias=val(T, bias), scale=val(T, scale)), [a, bias, scale], [o], k, nel(a))
         else:
             add("A", lambda g, T, x: g.scalar.activation(ap(T, o), ap(T, a), fn, bias=val(T, bias), scale=val(T, scale), accum_out=ap(T, acc)),
-                [a, bias, scale], [o, acc], c + (20 if o[0] not in PSUM else 140))
+                [a, bias, scale], [o, acc], k, max(64, nel(a)) + 20)
 
     def MM(o, l, r, start, stop):
-        c = LAT["pe"] * max(64, nel(r)) * (4 if SCRATCH[l[0]][2] == F else 1)
-        add("P", lambda g, T, x: g.tensor.matmul(ap(T, o), ap(T, l), ap(T, r), start, stop), [l, r], [o], c, grp=True)
+        c = max(min(64, nel(l)), nel(r)) * (4 if SCRATCH[l[0]][2] == F else 1)
+        add("P", lambda g, T, x: g.tensor.matmul(ap(T, o), ap(T, l), ap(T, r), start, stop), [l, r], [o], "p", c, grp=True)
 
     def TR(o, a):
-        add("P", lambda g, T, x: g.tensor.transpose(ap(T, o), ap(T, a), ap(T, s("I16"))), [a, s("I16")], [o], 128 * LAT["pe"], grp=True)
+        add("P", lambda g, T, x: g.tensor.transpose(ap(T, o), ap(T, a), ap(T, s("I16"))), [a, s("I16")], [o], "p", 128, grp=True)
 
     def IO(o, pat, base, cm):
         if SCRATCH[o[0]][2] == I:
-            add("G", lambda g, T, x: g.iota(ap(T, o), pat, base, cm), [], [o], 130 + 2 * nel(o))
+            add("G", lambda g, T, x: g.iota(ap(T, o), pat, base, cm), [], [o], "G", nel(o))
         else:
-            add("G", lambda g, T, x: g.iota(ap(T, o), pat, base, cm, allow_small_or_imprecise_dtypes=True), [], [o], 130 + 2 * nel(o))
+            add("G", lambda g, T, x: g.iota(ap(T, o), pat, base, cm, allow_small_or_imprecise_dtypes=True), [], [o], "G", nel(o))
 
     def LD(q, o, name, sem, lat, after=()):
         if q == "S":
-            add(q, lambda g, T, x: g.sync.dma_start(ap(T, o), T[name][:]), list(after), [o], 60, sem=(sem, 16), lat=lat)
+            add(q, lambda g, T, x: g.sync.dma_start(ap(T, o), T[name][:]), list(after), [o], "d", lat, sem=(sem, 16))
         else:
-            add(q, lambda g, T, x: g.scalar.dma_start(ap(T, o), T[name][:]), list(after), [o], 60, sem=(sem, 16), lat=lat)
+            add(q, lambda g, T, x: g.scalar.dma_start(ap(T, o), T[name][:]), list(after), [o], "d", lat, sem=(sem, 16))
 
     def col(b, j):
         return s(b, j, j + 1)
@@ -153,16 +184,25 @@ def program():
     mul, ad, sub, mx, mn = ALU.mult, ALU.add, ALU.subtract, ALU.max, ALU.min
     band, shr = ALU.bitwise_and, ALU.logical_shift_right
     I32 = s("Pf", 16, 144)
+    UW, X2 = CFG["UW"], CFG["X2"]
+    SW = UW if CFG["D3"] else 1
+    turn = {}
 
-    LD("A", s("X0"), "x0", "dx0", LAT["x"])
+    def nxt(k, h):
+        own = k in CFG["OWN"]
+        n = CFG["N" + k] // (2 if own else 1)
+        key = (k, h if own else 0)
+        turn[key] = turn.get(key, -1) + 1
+        return "p%s%d" % (k, turn[key] % n + (n * h if own else 0))
+
+    LD("A", s("X0"), "x0", "dx0", 5000)
     LD("S", s("cin"), "c0", "dc", 2300)
     LD("S", s("yin"), "y0", "dy", 2300)
     LD("S", s("wb", 0, 1), "w", "dw", 2300)
     LD("S", s("stb"), "st", "ds", 3000)
     LD("S", s("th8", p1=8), "th", "dt", 2500)
-    X2 = CFG["X2"]
     if X2:
-        LD("S", s("X1"), "x0", "dx1", 5500, after=[s("X0")])
+        LD("S", s("X1"), "x0", "dx1", 4500, after=[s("X0")])
     IO(col("pi", 0), [[0, 1]], 0, 1)
     IO(s("iot"), [[1, 160]], 0, 0)
     TS(col("pb", 0), col("pi", 0), 4, shr)
@@ -187,11 +227,6 @@ def program():
     MS(s("zer"), 0.0)
     MS(s("neg"), -192.0)
     MS(s("c2k"), 4.0)
-    if "V" in CFG["SG"]:
-        MS(s("kc2"), 0.0)
-        for c in range(4):
-            if CFG["SG"][c] == "V":
-                MS(s("kc2", 16 * c, 16 * c + 16), -float(2 ** 22))
     MS(s("o16"), 16.0)
     IO(s("kk8"), [[1, 16], [0, 8]], 0, 0)
     IO(s("ii8"), [[0, 16], [1, 8]], 0, 0)
@@ -204,15 +239,20 @@ def program():
     MS(s("sel"), -1.0)
     for h in range(2):
         x_ = s("sel", p0=64 * h, p1=64 * h + 64)
-        add("G", lambda g, T, x, x_=x_: g.affine_select(ap(T, x_), ap(T, x_), [[-16, 4], [0, 16], [-1, 16]], eq, 0.0, 0, 1), [x_], [x_], 2200)
-    IO(s("kc"), [[-4096, 64]], 63 * 4096, 0)
+        add("G", lambda g, T, x, x_=x_: g.affine_select(ap(T, x_), ap(T, x_), [[-16, 4], [0, 16], [-1, 16]], eq, 0.0, 0, 1), [x_], [x_], "G", 1040)
+    IO(s("kc", p1=32), [[-512, 4], [-32, 18]], 2048, 0)
+    IO(s("kc", p0=32, p1=64), [[0, 72]], 2064, 0)
+    MS(s("kc", p0=64), 0.0)
+    for c in range(4):
+        if CFG["SG"][c - c % SW] == "A":
+            MS(s("kc", 18 * c, 18 * c + 18, 1, 64, 96), float(2 ** 15))
     IO(s("kap", 0, 72), [[-256, 4], [-16, 18]], 2048, 0)
     IO(s("kap", 72, 144), [[-256, 4], [-16, 18]], -2063, 0)
     IO(s("kk16"), [[1, 8], [0, 16]], 0, 0)
     TS(s("Wb"), s("kk16"), col("pc", 2), eq, col("pc", 13), mul)
     MS(s("d0k"), BIG)
-    MS(s("d0k", 0, 64, 16), -BIG)
-    MS(s("d0k", 1, 64, 16), -BIG)
+    MS(s("d0k", 1, 72, 18), -BIG)
+    MS(s("d0k", 2, 72, 18), -BIG)
     MS(s("lo4"), 0.0)
     MS(s("lo4", 0, 72, 18), 1.0)
     MS(s("lo4", 17, 72, 18), -BIG)
@@ -223,19 +263,36 @@ def program():
     TS(s("jf", 0, 10), s("ji", 0, 10), col("pc", 11), ad)
     TS(s("jq", 0, 10), s("jf", 0, 10), 1.0 / 18, mul, -0.47, ad)
     CP(s("Lm", 0, 10), s("jq", 0, 10))
-    IO(s("ji", 12, 16), [[18, 4]], 1, 1)
-    TS(s("Lc", 0, 4), s("ji", 12, 16), col("pc", 11), ad)
+    if CFG["MS"] == "I":
+        TS(s("jr", 0, 6), s("jq", 0, 6), 18.0, mul, 17.0, ad)
+        if CFG["EP"] == "V":
+            TT(s("jr", 8, 14), s("jr", 0, 6), s("jf", 0, 6), sub)
+            TS(s("jr", 8, 14), s("jr", 8, 14), 1.5, ALU.is_lt, 99.0, mul)
+            TT(s("jr", 0, 6), s("jr", 0, 6), s("jr", 8, 14), ad)
+        TS(s("Lh", 0, 6), s("jr", 0, 6), 72.0, mn)
     IO(s("l32b"), [[512, 8]], 0, 32)
     TS(s("l32"), s("l32b"), col("pc", 12), ad)
     for h in "01":
         MS(s("A" + h, 72, 80), 0.0)
-        MS(s("Ms" + h), 0.0)
-        MS(s("ab" + h), 0.0)
-        MS(s("pS" + h, 399, 400), 0.0)
-    TS(s("ycs"), s("cin"), -2048.0, ad)
-    VT(s("ct"), s("ycs"))
+        MS(s("H" + h, 72, 80), -2.0)
+        MS(s("H" + h, 73, 80), 0.0)
+        for b in ("ab", "ind"):
+            if CFG["D3"]:
+                MS(seg(b + h, 0, 4, 0, 16), 0.0)
+                MS(seg(b + h, 0, 4, 272, 288), 0.0)
+            else:
+                MS(s(b + h), 0.0)
+        if CFG["EP"] == "A":
+            MS(s("ep" + h), 0.0)
+        elif CFG["EP"] == "P":
+            MS(rg("P" + h, 0, 72), 0.0)
+        MS(rg("V" + h, 144, 145), 0.0)
+        if CFG["MS"] == "C":
+            MS(rg("V" + h, 72, 144), 0.0)
+    TS(s("cf"), s("cin"), -2048.0, ad)
+    VT(s("ct"), s("cf"))
     for h in range(2):
-        ps = "pB%d0" % h
+        ps = "pZ%d" % h
         MM(s(ps, 340, 412), s("zer"), s("zer", 0, 72), True, False)
         for c in range(4):
             for g2 in range(2):
@@ -246,18 +303,19 @@ def program():
 
     def sums(t, ysrc):
         a, b = 8 * t, 8 * t + 8
+        pu = rg("U", 0, 8)
         if t > 0:
-            MM(s("pS1", 472, 480), s("Wb"), s("neg", 0, 8), True, False)
+            MM(pu, s("Wb"), s("neg", 0, 8), True, False)
         for r in range(16):
-            MM(s("pS1", 472, 480), s("Ww", 15 - r, 143 - r), s(ysrc, r, 128, 16), t == 0 and r == 0, r == 15)
-        CP(s("ui"), s("pS1", 472, 480))
+            MM(pu, s("Ww", 15 - r, 143 - r), s(ysrc, r, 128, 16), t == 0 and r == 0, r == 15)
+        CP(s("ui"), pu)
         TS(s("uI", a, b), s("ui"), 2047, band)
         TS(s("mU", a, b), s("uI", a, b), 2.0, mul, 33.0, ad)
         if t == 0:
             AC(s("oU", a, b), s("mU", a, b), scale=2048.0, bias=-float(2 ** 22))
         else:
-            MM(s("pS1", 480, 482), s("o16"), s("cnt", 2 * t - 2, 2 * t), True, True)
-            AC(s("Acol", 8, 10), s("pS1", 480, 482), bias=float(8192 - 2 ** 21), acc=col("Acol", t))
+            MM(rg("U", 8, 10), s("o16"), s("cnt", 2 * t - 2, 2 * t), True, True)
+            AC(s("Acol", 8, 10), rg("U", 8, 10), bias=float(8192 - 2 ** 21), acc=col("Acol", t))
             AC(s("oU", a, b), s("mU", a, b), scale=2048.0, bias=col("Acol", t))
         TS(s("ub", 0, 8), s("ui"), 1, band)
         TS(s("ob", a, b), s("ub", 0, 8), 1024.0, mul, 4096.0, ad)
@@ -266,55 +324,68 @@ def program():
             TT(s("cx"), s("ub", 8, 16), s("l32"), ad)
             CP(s("col", a, b), s("cx"))
 
-    def bank(h, c):
-        if CFG["BK"]:
-            return "pB%d%d" % (c >> 1, c & 1), 0
-        return "pB%d%d" % (h, c & 1), 256 * (c >> 1)
-
     def renew(t, into):
         TT(ind(s("X%d" % into), s("col", 8 * t, 8 * t + 8)), s("wv", 128 * t, 128 * t + 128), s("neg"), ad)
 
-    def places(h, mb, m0, ob_, o0):
+    def places(h, mb, m0, ob_, o0, eng):
         H = str(h)
         for c in range(4):
-            TS(s("t" + H, 16 * c, 16 * c + 16), s("A" + H, 18 * c + 1, 18 * c + 17), col(mb, m0 + c), mul, col(ob_, o0 + c), ad)
+            a_ = s("A" + H, 18 * c + 1, 18 * c + 17)
+            if eng == "V":
+                TS(s("t" + H, 16 * c, 16 * c + 16), a_, col(mb, m0 + c), mul, col(ob_, o0 + c), ad)
+            else:
+                AC(s("tf" + H, 16 * c, 16 * c + 16), a_, scale=col(mb, m0 + c), bias=col(ob_, o0 + c))
+        if eng != "V":
+            CP(s("t" + H), s("tf" + H))
         TS(s("p" + H), s("t" + H), 0x1FFFF, band, 5, shr)
         CP(s("off" + H), s("p" + H))
 
     def gather(h, t, out, plan):
-        for c in range(4):
-            (CP if plan[c] == "V" else AC)(s(out, 256 * c, 256 * c + 256), ind(s("X%d" % (t & X2)), s("off%d" % h, 16 * c, 16 * c + 16)))
+        for x in plan:
+            c0, c1 = int(x[1]), int(x[2])
+            (CP if x[0] == "V" else AC)(s(out, 256 * c0, 256 * c1), ind(s("X%d" % (t & X2)), s("off%d" % h, 16 * c0, 16 * c1)))
+
+    def values(t, lo, hi):
+        AC(s("y128", lo, hi), rg("E", lo, hi), scale=8.0, bias=192.0 - 31.0 / 64)
+        if t < RO - 1:
+            TT(s("wv", 128 * t + lo, 128 * t + hi), s("hx", lo, hi), rg("E", lo, hi), ad)
 
     def front(t, h):
-        H = str(h); ps = "pS" + H; A = "A" + H; u0 = 8 * t + 4 * h; y0 = PW * (2 * t + h); v0 = 328
+        H = str(h); A = "A" + H; u0 = 8 * t + 4 * h; y0 = PW * (2 * t + h); v0 = 232 * h
         half[0] = 1 - h
-        places(h, "mU", u0, "oU", u0)
-        AC(s("C" + H), ind(s(A), s("Lc", 0, 4)), bias=float(2 ** 22 + 2 ** 18 + 2048))
+        places(h, "mU", u0, "oU", u0, CFG["PL"][0])
         gather(h, t, "xa" + H, CFG["G1"])
-        for c in range(4):
-            px, w = "pX%d" % (c & 1), 256 * (c >> 1)
-            pb, z = bank(h, c)
-            MM(s(pb, z, z + 256), s("sT", 128 * t, 128 * t + 128, 1, 64 * h, 64 * h + 64), s("sel", 256 * c, 256 * c + 256, 1, 64 * h, 64 * h + 64), True, False)
-            for b in range(2):
-                TR(s(px, w + 128 * b, w + 128 * b + 128), s("xa" + H, 256 * c + b, 256 * c + 256, 2))
-            (CP if CFG["CP"][c] == "V" else AC)(s("xT" + H, 256 * c, 256 * c + 256), s(px, w, w + 256))
-            for b in range(2):
-                MM(s(pb, z + b, z + 256, 2), s("xT" + H, 256 * c + 128 * b, 256 * c + 128 * b + 128), s("Mx"), False, b == 1)
-            if CFG["SG"][c] == "V":
-                TS(s("ind" + H, 256 * c, 256 * c + 256), s(pb, z, z + 256), 0.0, ALU.is_ge, 2.0, mul)
-            else:
-                AC(s("ind" + H, 256 * c, 256 * c + 256), s(pb, z, z + 256), AF.Sign, bias=0.0625)
+        for c0 in range(0, 4, UW):
+            px, w = nxt("X", h), 256 * c0
+            pb = nxt("Z", h)
+            MM(s(pb, 0, 256 * UW), s("sT", 128 * t, 128 * t + 128, 1, 64 * h, 64 * h + 64),
+               s("sel", 256 * c0, 256 * (c0 + UW), 1, 64 * h, 64 * h + 64), True, False)
+            for c in range(c0, c0 + UW):
+                for b in range(2):
+                    z = 256 * (c - c0) + 128 * b
+                    TR(s(px, w + z, w + z + 128), s("xa" + H, 256 * c + b, 256 * c + 256, 2))
+            (CP if CFG["CP"][c0] == "V" else AC)(s("xT" + H, 256 * c0, 256 * (c0 + UW)), s(px, w, w + 256 * UW))
+            for c in range(c0, c0 + UW):
+                z = 256 * (c - c0)
+                for b in range(2):
+                    MM(s(pb, z + b, z + 256, 2), s("xT" + H, 256 * c + 128 * b, 256 * c + 128 * b + 128), s("Mx"), False, b == 1 and c == c0 + UW - 1)
+            for c in range(c0, c0 + UW, SW):
+                z = 256 * (c - c0)
+                o_, i_ = seg("ind" + H, c, c + SW, 16, 272), s(pb, z, z + 256 * SW)
+                if CFG["SG"][c] == "V":
+                    TS(o_, i_, 0.0, ALU.is_ge, 2.0, mul)
+                else:
+                    AC(o_, i_, AF.Sign, bias=0.0625)
         for ch in range(8):
             c, b = ch >> 1, ch & 1
-            MM(s(ps, 64 + 16 * c + b, 80 + 16 * c, 2), s("xT" + H, 128 * ch, 128 * ch + 128), s("ME", 0, 8), True, True)
-        MM(s(ps, 0, 64), I32, s("C" + H), True, False)
-        MM(s(ps, 0, 64), s("I16"), s("kc"), False, False)
-        if "V" in CFG["SG"]:
-            MM(s(ps, 0, 64), s("I16"), s("kc2"), False, False)
+            MM(rg("E", 64 * h + 16 * c + b, 64 * h + 16 * c + 16, 2), s("xT" + H, 128 * ch, 128 * ch + 128), s("ME", 0, 8), True, True)
+        pk = rg("K" + H, 0, 72)
+        MM(pk, I32, s(A, 0, 72), True, False)
+        MM(pk, s("c2k"), s("kc"), False, False)
         for r in range(16):
-            MM(s(ps, 0, 64), s("WA", 15 - r, 143 - r), s("ind" + H, r, 1024, 16), False, r == 15)
-        SC(s("S" + H), s("d0k"), s(ps, 0, 64), -BIG, mn, mx)
-        K0, KS = s("S" + H, 0, 64, 16), s("S" + H, 15, 64, 16)
+            MM(pk, s("WA", 15 - r, 143 - r), seg("ind" + H, 0, 4, r, 288, 16), False, r == 15)
+        SC(s("S" + H), s("d0k"), pk, -BIG, mn, mx)
+        K0, KS = s("S" + H, 1, 72, 18), s("S" + H, 16, 72, 18)
         q = lambda b, j=0: s(b + H, j, j + 4)
         CP(q("Ki"), KS)
         TS(q("oi"), q("Ki"), 8, shr, 0x7F0, band)
@@ -342,13 +413,13 @@ def program():
         else:
             AC(gs, q("nr", 8), AF.Sign, bias=-1.0)
         n = 2 * t + h
-        add("G", lambda g, T, x: x["send"](n), [s("pay", y0, y0 + PW)], [s("land", y0, y0 + PW)], LAT["call"],
-            sem=("arr%d" % n, 0), lat=LAT["hop"] if t & 1 else 2 * LAT["hop"] + LAT["call"])
-        AC(s("y128", 64 * h, 64 * h + 64), s(ps, 64, 128), scale=8.0, bias=192.0 - 31.0 / 64)
-        if t < RO - 1:
-            if h == 0:
-                AC(s("hx"), ind(s("X%d" % (t & X2)), s("col", 8 * t, 8 * t + 8)), scale=0.5, bias=192.0 - 255.0 / 512)
-            TT(s("wv", 128 * t + 64 * h, 128 * t + 64 * h + 64), s("hx", 64 * h, 64 * h + 64), s(ps, 64, 128), ad)
+        add("G", lambda g, T, x: x["send"](n), [s("pay", y0, y0 + PW)], [s("land", y0, y0 + PW)], "r", 1 if t & 1 else 2, sem=("arr%d" % n, 0))
+        if t < RO - 1 and h == 0:
+            AC(s("hx"), ind(s("X%d" % (t & X2)), s("col", 8 * t, 8 * t + 8)), scale=0.5, bias=192.0 - 255.0 / 512)
+        if not CFG["MW"]:
+            values(t, 64 * h, 64 * h + 64)
+        elif h == 1:
+            values(t, 0, 128)
         AC(s(A, 0, 72, 18), ee)
         TT(q("fi"), me, s("uI", u0, u0 + 4), mul)
         TS(q("fi", 4), q("fi"), 0x1FFFF, band, 5, shr)
@@ -357,67 +428,75 @@ def program():
         TT(q("oo"), q("oi"), s("ob", u0, u0 + 4), sub)
         TT(q("TH", 4), q("oo"), q("nr", 8), mx)
         TT(s("mk" + H), ind(s("TH" + H), s("Lm", 0, 9)), s("kap"), ALU.is_ge)
-        TT(s(ps, v0, v0 + 71), s(A, 1, 72), s(A, 0, 71), sub)
-        TT(s(ps, v0 + 72, v0 + 143), s("mk" + H, 72, 143), s(ps, v0, v0 + 71), mul)
-        TT(s(ps, v0, v0 + 71), s("mk" + H, 0, 71), s(ps, v0, v0 + 71), mul)
-        TT(s("Q" + H, 0, 70), s(A, 0, 70), s(ps, v0 + 72, v0 + 142), ad)
-        TT(s(A, 1, 71), s("Q" + H, 0, 70), s(ps, v0 + 1, v0 + 71), ad)
+        V = "V" + H
+        TT(rg(V, 0, 71), s(A, 1, 72), s(A, 0, 71), sub)
+        TT(rg(V, 72, 142), s("mk" + H, 72, 142), rg(V, 0, 70), mul)
+        TT(rg(V, 145, 215), s("mk" + H, 1, 71), rg(V, 1, 71), mul)
+        TT(s("Q" + H, 0, 70), s(A, 0, 70), rg(V, 72, 142), ad)
+        TT(s(A, 1, 71), s("Q" + H, 0, 70), rg(V, 145, 215), ad)
 
     def back(t, h):
-        H = str(h); ps = "pS" + H; A = "A" + H; y0 = PW * (2 * t + h); w0 = 399
+        H = str(h); A = "A" + H; y0 = PW * (2 * t + h); w0 = 144; V = "V" + H
         half[0] = 1 - h
-        places(h, "land", y0 + 68, "land", y0 + 72)
-        MM(s(ps, 200, 328, 1, 0, 64), s("land", y0, y0 + 64), I32, True, True)
-        AC(s("vT" + H, p1=64), s(ps, 200, 328, 1, 0, 64))
+        places(h, "land", y0 + 68, "land", y0 + 72, CFG["PL"][1])
+        pbs = [nxt("Z", h) for c0 in range(0, 4, UW)]
+        pv = s(pbs[0], 0, 128, 1, 0, 64)
+        MM(pv, s("land", y0, y0 + 64), I32, True, True)
+        AC(s("vT" + H, p1=64), pv)
         gather(h, t, "g2" + H, CFG["G2"])
         if CFG["EP"] == "V":
             ep = s("ep" + H, 1, 71)
             TT(s("ep" + H), ind(s("land", y0 + 64, y0 + 80), s("Lm", 0, 5)), s(A), sub)
-        elif CFG["EP"] == "S":
-            ep = s("ep" + H, 1, 71)
-            for c in range(4):
-                AC(s("ep" + H, 1 + 18 * c, 19 + 18 * c), s(A, 18 * c + 1, 18 * c + 19), scale=-1.0, bias=col("land", y0 + 64 + c))
         else:
-            ep = s(ps, 329, 399)
+            e_ = (lambda lo, hi: s("ep" + H, lo, hi)) if CFG["EP"] == "A" else (lambda lo, hi: rg("P" + H, lo, hi))
+            ep = e_(1, 71)
             for c in range(4):
-                AC(s(ps, 329 + 18 * c, 345 + 18 * c), s(A, 18 * c + 1, 18 * c + 17), scale=-1.0, bias=col("land", y0 + 64 + c))
-        for c in range(4):
-            pb, z = bank(h, c)
-            o_ = s(pb, z, z + 256)
-            MM(o_, s("vT" + H, p1=64), s("sel", 256 * c, 256 * c + 256, 1, 0, 64), True, False)
-            MM(o_, s("I16"), s("g2" + H, 256 * c, 256 * c + 256), False, True)
-            AC(s("ab" + H, 288 * c + 16, 288 * c + 272), o_, AF.Abs)
-        MM(s(ps, 128, 200), s("I16"), s("thb" + H, 0, 72), True, False)
-        MM(s(ps, 145, 200, 18), I32, s("land", y0 + 76, y0 + 80), False, False)
+                AC(e_(1 + 18 * c, 17 + 18 * c), s(A, 18 * c + 1, 18 * c + 17), scale=-1.0, bias=col("land", y0 + 64 + c))
+        for c0 in range(0, 4, UW):
+            pb = pbs[c0 // UW]
+            o_ = s(pb, 0, 256 * UW)
+            MM(o_, s("vT" + H, p1=64), s("sel", 256 * c0, 256 * (c0 + UW), 1, 0, 64), True, False)
+            MM(o_, s("I16"), s("g2" + H, 256 * c0, 256 * (c0 + UW)), False, True)
+            for c in range(c0, c0 + UW, SW):
+                z = 256 * (c - c0)
+                AC(seg("ab" + H, c, c + SW, 16, 272), s(pb, z, z + 256 * SW), AF.Abs)
+        pd = rg("D" + H, 0, 72)
+        MM(pd, s("I16"), s("thb" + H, 0, 72), True, False)
+        MM(rg("D" + H, 17, 72, 18), I32, s("land", y0 + 76, y0 + 80), False, False)
         for r in range(16):
-            MM(s(ps, 128, 200), s("W1", 15 - r, 143 - r), s("ab" + H, r, 1152, 16), False, r == 15)
-        SC(s("H" + H, 0, 72), s(ps, 128, 200), s("lo4"), 1.0, mn, mx)
-        for c in range(4):
-            TS(s("Ms" + H, 18 * c, 18 * c + 16), s("H" + H, 18 * c, 18 * c + 16), col("H" + H, 18 * c + 17), ALU.is_le)
-        TT(s(ps, w0 + 1, w0 + 71), s("Ms" + H, 0, 70), ep, mul)
-        TT(s("Q" + H, 1, 71), s(A, 1, 71), s(ps, w0 + 1, w0 + 71), ad)
-        TT(s(A, 1, 71), s("Q" + H, 1, 71), s(ps, w0, w0 + 70), sub)
+            MM(pd, s("W1", 15 - r, 143 - r), seg("ab" + H, 0, 4, r, 288, 16), False, r == 15)
+        SC(s("H" + H, 0, 72), pd, s("lo4"), 1.0, mn, mx)
+        if CFG["MS"] == "I":
+            TT(s("Ms" + H), ind(s("H" + H), s("Lh", 0, 5)), s("H" + H), ALU.is_ge)
+            ms = s("Ms" + H, 0, 70)
+        else:
+            for c in range(4):
+                TS(rg(V, 72 + 18 * c, 88 + 18 * c), s("H" + H, 18 * c, 18 * c + 16), col("H" + H, 18 * c + 17), ALU.is_le)
+            ms = rg(V, 72, 142)
+        TT(rg(V, w0 + 1, w0 + 71), ms, ep, mul)
+        TT(s("Q" + H, 1, 71), s(A, 1, 71), rg(V, w0 + 1, w0 + 71), ad)
+        TT(s(A if t < RO - 1 else "Af" + H, 1, 71), s("Q" + H, 1, 71), rg(V, w0, w0 + 70), sub)
 
     def finish(h):
-        H = str(h); ps = "pS" + H
+        H = str(h); ps = nxt("Z", h)
         MM(s(ps, 0, 64), s("c2k"), s("c2k", 0, 64), True, False)
         for cp in range(2):
             for g2 in range(2):
                 for c2 in range(2):
                     o_ = 16 + 16 * g2 - 16 * c2; k0 = 18 * (2 * cp + c2) + 1; w = 32 * cp + 16 * g2
-                    MM(s(ps, w, w + 16), s("P%d" % g2, o_, o_ + 128), s("A" + H, k0, k0 + 16), False, cp + g2 + c2 == 3)
+                    MM(s(ps, w, w + 16), s("P%d" % g2, o_, o_ + 128), s("Af" + H, k0, k0 + 16), False, cp + g2 + c2 == 3)
         VT(s("ycs", 64 * h, 64 * h + 64), s(ps, 0, 64))
         x_ = s("ycs", 64 * h, 64 * h + 64)
-        add("S", lambda g, T, x: g.sync.dma_start(T.yc[:, 64 * h:64 * h + 64], ap(T, x_)), [x_], [], 60, sem=("dyc" + H, 16), lat=2000)
+        add("S", lambda g, T, x: g.sync.dma_start(T.yc[:, 64 * h:64 * h + 64], ap(T, x_)), [x_], [], "d", 2000, sem=("dyc" + H, 16))
 
     sums(0, "yin")
     for t in range(RO):
-        TR(s("pX1", 128 * t, 128 * t + 128), s("stb", 128 * t, 128 * t + 128))
-    CP(s("sT"), s("pX1", 0, 640))
+        TR(s("pX0", 128 * t, 128 * t + 128), s("stb", 128 * t, 128 * t + 128))
+    CP(s("sT"), s("pX0", 0, 640))
     for r in range(16):
-        MM(s("pB11", 0, 8), s("W8", 15 - r, 143 - r, 1, 0, 8), s("th8", r, 128, 16, 0, 8), r == 0, r == 15)
+        MM(s("pZ2", 0, 8), s("W8", 15 - r, 143 - r, 1, 0, 8), s("th8", r, 128, 16, 0, 8), r == 0, r == 15)
     for h in range(2):
-        AC(s("thZ", 8 * h, 8 * h + 4), s("pB11", 4 * h, 4 + 4 * h))
+        AC(s("thZ", 8 * h, 8 * h + 4), s("pZ2", 4 * h, 4 + 4 * h))
         TT(s("thb%d" % h), ind(s("thZ", 8 * h, 8 * h + 8), s("Lm", 0, 5)), s("thm"), mul)
     front(0, 0)
     front(0, 1)
@@ -428,12 +507,12 @@ def program():
                 renew(t, (t + 1) & 1)
         else:
             TS(s("yo"), s("y128"), -192.0, ad)
-            add("S", lambda g, T, x: g.sync.dma_start(T.yy[:], T["yo"][:]), [s("yo")], [], 60, sem=("dyy", 16), lat=2000)
+            add("S", lambda g, T, x: g.sync.dma_start(T.yy[:], T["yo"][:]), [s("yo")], [], "d", 2000, sem=("dyy", 16))
         back(t, 0)
-        if not X2:
+        if not X2 or CFG["OR"]:
             back(t, 1)
-            if t < RO - 1:
-                renew(t, 0)
+            if t < RO - 1 - X2:
+                renew(t, t & X2)
             for h in range(2):
                 if t < RO - 1:
                     front(t + 1, h)
@@ -454,20 +533,38 @@ def program():
     return ops
 
 
-XLAT, QLAT = 120.0, 70.0
-TRY, SWEEPS = [(20.0, 0.0), (40.0, 0.0), (60.0, 1500.0)], 4
-CLIMB, SLACK, MODES = 3000, 0.0, [(1.0, 1.0), (1.5, 1.0), (0.75, 1.4)]
+MODES = [(1.04, 0, 64, 0.52, 180, 170, 1300, 500, 1.5, 3.5), (1.2, 0, 64, 0.6, 130, 110, 1500, 600, 1.5, 3.5),
+         (1.04, 55, 0, 0.52, 130, 80, 1300, 500, 1.5, 3.5), (1.04, 0, 64, 0.52, 200, 120, 2600, 900, 1.5, 3.5)]
+TRY, SWEEPS, CLIMB = [(20.0, 0.0), (60.0, 0.0), (60.0, 1500.0)], 3, 2500
+
+
+def prices(ops, m):
+    cv, fix, least, pe, xl, ql, hop, call, gam, sca = m
+    cost, lat = [], []
+    for o in ops:
+        k, n = o["k"], o["c"]
+        cost.append({"n": cv * max(least, fix + n), "g": (55 if o["e"] == "V" else 70) + cv * gam * n, "s": 55 + cv * sca * n,
+                     "p": pe * n, "G": 130 + 2 * cv * n, "d": 60, "r": call}[k])
+        lat.append(n if k == "d" else (n * hop + (n - 1) * call if k == "r" else 0.0))
+    pred = [[(j, 0.0 if not sem else lat[j] + (ql if ops[j]["e"] == o["e"] and ops[j]["sem"] is None else xl)) for j, sem in o["d"].items()] for o in ops]
+    return cost, lat, pred
+
+
+def cells(x, memo={}):
+    if x not in memo:
+        m = 0
+        for c in range(*(x[6] or (0, 1))):
+            for j in range(x[1], x[2], x[3]):
+                m |= 1 << (c * SCRATCH[x[0]][1][-1] + j)
+        memo[x] = m
+    return memo[x]
 
 
 def meets(a, b):
-    if not (a[0] == b[0] and a[1] < b[2] and b[1] < a[2] and a[4] < b[5] and b[4] < a[5]):
-        return False
-    return (a[3] == 1 and b[3] == 1) or not set(range(a[1], a[2], a[3])).isdisjoint(range(b[1], b[2], b[3]))
+    return a[4] < b[5] and b[4] < a[5] and cells(a) & cells(b) != 0
 
 
-def schedule():
-    ops = program()
-    n = len(ops)
+def depend(ops):
     hist, run = {}, {}
     for i, o in enumerate(ops):
         dep = {}
@@ -481,107 +578,110 @@ def schedule():
                     elif x[0] in PSUM and o["grp"]:
                         dep.setdefault(j, False)
                     elif (kind == "W" or k2 == "W") and meets(x, y):
-                        if not same or k2 == "W" or SAMEQ_WAR:
-                            dep[j] = True
-                        else:
-                            dep.setdefault(j, False)
+                        dep[j] = True
         o["d"] = dep
         for kind in "RW":
             for x in o[kind]:
                 hs = hist.setdefault(x[0], [])
-                if x[0] in PSUM:
-                    if hs and ops[hs[-1][0]]["e"] != o["e"]:
-                        hs[:] = [z for z in hs if ops[z[0]]["e"] == ops[hs[-1][0]]["e"] and z[0] >= run.get(x[0], 0)]
-                        run[x[0]] = i
-                    elif o["grp"] and hs:
-                        hs[:] = [z for z in hs if z[0] < run.get(x[0], 0)]
-                elif kind == "W" and x[3] == 1:
-                    hs[:] = [z for z in hs if not (x[1] <= z[2][1] and z[2][2] <= x[2] and x[4] <= z[2][4] and z[2][5] <= x[5])]
+                if x[0] in PSUM and hs and ops[hs[-1][0]]["e"] != o["e"]:
+                    hs[:] = [z for z in hs if ops[z[0]]["e"] == ops[hs[-1][0]]["e"] and z[0] >= run.get(x[0], 0)]
+                    run[x[0]] = i
+                elif x[0] in PSUM and o["grp"]:
+                    hs[:] = [z for z in hs if z[0] < run.get(x[0], 0)]
+                elif kind == "W":
+                    hs[:] = [z for z in hs if z[0] < run.get(x[0], 0) or
+                             not (x[4] <= z[2][4] and z[2][5] <= x[5] and cells(z[2]) & ~cells(x) == 0)]
                 hs.append((i, kind, x))
+
+
+def schedule():
+    ops = program()
+    n = len(ops)
+    depend(ops)
+    price = [prices(ops, m) for m in MODES]
+    eng = [o["e"] for o in ops]
     succ = [[] for _ in ops]
     for i, o in enumerate(ops):
         for j in o["d"]:
             succ[j].append(i)
-
-    def gap(j, i):
-        if not ops[i]["d"][j]:
-            return 0.0
-        return ops[j]["lat"] + (QLAT if ops[j]["e"] == ops[i]["e"] and ops[j]["sem"] is None else XLAT)
-
-    level = [0.0] * n
-    for i in range(n - 1, -1, -1):
-        level[i] = ops[i]["c"] + max([gap(i, k) + level[k] for k in succ[i]] + [ops[i]["lat"]])
-    pred = [[(j, gap(j, i)) for j in o["d"]] for i, o in enumerate(ops)]
-    post = [[(k, gap(i, k)) for k in succ[i]] for i in range(n)]
-
-    def sweep(before, after, prio, first, win):
-        left = [len(b) for b in before]
-        ready = {e: {} for e in "VAPGS"}
-        for i in range(n):
-            if left[i] == 0:
-                ready[ops[i]["e"]][i] = first[i]
-        free = {e: 0.0 for e in "VAPGS"}
-        fin = [0.0] * n
-        order = []
-        while len(order) < n:
-            t0, e0 = min((max(min(r.values()), free[e]), e) for e, r in ready.items() if r)
-            i = max((i for i, r in ready[e0].items() if r <= t0 + win), key=lambda i: (prio[i], -i))
-            fin[i] = max(ready[e0].pop(i), free[e0]) + ops[i]["c"]
-            free[e0] = fin[i]
-            order.append(i)
-            for k, _ in after[i]:
-                left[k] -= 1
-                if left[k] == 0:
-                    ready[ops[k]["e"]][k] = max([first[k]] + [fin[j] + d for j, d in before[k]])
-        return order, fin
-
-    best = None
-    tail = [o["lat"] if not succ[i] else 0.0 for i, o in enumerate(ops)]
-    for win, bias in TRY:
-        prio = [level[i] + bias * ops[i]["h"] for i in range(n)]
-        for it in range(SWEEPS):
-            order, fin = sweep(pred, post, prio, [0.0] * n, win)
-            end = max(fin[i] + tail[i] for i in range(n))
-            if best is None or end < best[0]:
-                best = (end, order, fin)
-            prio = sweep(post, pred, fin, tail, win)[1]
-
-    eng, cost = [o["e"] for o in ops], [o["c"] for o in ops]
     ends = [i for i in range(n) if not succ[i]]
 
-    def replay(order, k, pe, fin):
+    def replay(order, m, fin):
+        cost, lat, pred = price[m]
         free = {e: 0.0 for e in "VAPGS"}
         for i in order:
             e = eng[i]
             st = free[e]
             for j, d in pred[i]:
-                x = fin[j] + d * k
+                x = fin[j] + d
                 if x > st:
                     st = x
-            fin[i] = free[e] = st + (cost[i] * pe if e == "P" else cost[i])
-        return max(fin[i] + tail[i] for i in ends)
+            fin[i] = free[e] = st + cost[i]
+        return max(fin[i] + lat[i] for i in ends)
+
+    fin = [0.0] * n
 
     def worth(order):
-        return sum(replay(order, k, pe, fin) for k, pe in MODES)
+        return sum(replay(order, m, fin) for m in range(len(MODES)))
 
-    order, fin = best[1], list(best[2])
-    top, seed, moved = worth(order), 12345, False
-    gold = (top, order)
+    def sweep(cost, before, after, prio, first, win):
+        left = [len(b) for b in before]
+        ready = {e: {} for e in "VAPGS"}
+        for i in range(n):
+            if left[i] == 0:
+                ready[eng[i]][i] = first[i]
+        free = {e: 0.0 for e in "VAPGS"}
+        f = [0.0] * n
+        order = []
+        while len(order) < n:
+            t0, e0 = min((max(min(r.values()), free[e]), e) for e, r in ready.items() if r)
+            i = max((i for i, r in ready[e0].items() if r <= t0 + win), key=lambda i: (prio[i], -i))
+            f[i] = max(ready[e0].pop(i), free[e0]) + cost[i]
+            free[e0] = f[i]
+            order.append(i)
+            for k, _ in after[i]:
+                left[k] -= 1
+                if left[k] == 0:
+                    ready[eng[k]][k] = max([first[k]] + [f[j] + d for j, d in before[k]])
+        return order, f
+
+    best = None
+    for cost, lat, pred in price:
+        post = [[] for _ in ops]
+        for i in range(n):
+            for j, d in pred[i]:
+                post[j].append((i, d))
+        level = [0.0] * n
+        for i in range(n - 1, -1, -1):
+            level[i] = cost[i] + max([d + level[k] for k, d in post[i]] + [lat[i]])
+        tail = [lat[i] if not succ[i] else 0.0 for i in range(n)]
+        for win, bias in TRY:
+            prio = [level[i] + bias * ops[i]["h"] for i in range(n)]
+            for it in range(SWEEPS):
+                order, f = sweep(cost, pred, post, prio, [0.0] * n, win)
+                w = worth(order)
+                if best is None or w < best[0]:
+                    best = (w, order)
+                if it < SWEEPS - 1:
+                    prio = sweep(cost, post, pred, f, tail, win)[1]
+
+    top, order = best
+    seed, moved = 12345, False
     for it in range(CLIMB):
         seed = (seed * 1103515245 + 12345) % 2 ** 31
-        if it == 0 or moved:
-            k, pe = MODES[(seed >> 10) % 3]
+        if it == 0 or moved or it % 40 == 0:
+            cost, lat, pred = price[(seed >> 10) % len(MODES)]
             at, lastq, f, why = {}, {}, [0.0] * n, [None] * n
             for p, i in enumerate(order):
                 at[i] = p
                 q = lastq.get(eng[i])
                 st, why[i] = (f[q], (q, True)) if q is not None else (0.0, None)
                 for j, d in pred[i]:
-                    if f[j] + d * k >= st:
-                        st, why[i] = f[j] + d * k, (j, False)
-                f[i] = st + cost[i] * (pe if eng[i] == "P" else 1.0)
+                    if f[j] + d >= st:
+                        st, why[i] = f[j] + d, (j, False)
+                f[i] = st + cost[i]
                 lastq[eng[i]] = i
-            i = max(range(n), key=lambda i: f[i] + tail[i])
+            i = max(ends, key=lambda i: f[i] + lat[i])
             arcs = []
             while why[i] is not None:
                 if why[i][1]:
@@ -596,7 +696,7 @@ def schedule():
         late = set(i for i in qa[qa.index(first):pa + 1])
         keep, push = [], []
         for i in order[at[first]:at[b] + 1]:
-            if i in late or any(j in late for j, _ in pred[i]):
+            if i in late or any(j in late for j in ops[i]["d"]):
                 late.add(i); push.append(i)
             else:
                 keep.append(i)
@@ -604,14 +704,12 @@ def schedule():
             continue
         o2 = order[:at[first]] + keep + push + order[at[b] + 1:]
         w = worth(o2)
-        if w <= top + SLACK * (1.0 - it / CLIMB):
+        if w <= top:
             top, order, moved = w, o2, True
-            if w < gold[0]:
-                gold = (w, o2)
-    order = gold[1]
-    replay(order, 1.0, 1.0, fin)
+    times = [replay(order, m, fin) for m in range(len(MODES) - 1, -1, -1)][::-1]
+    cost, lat, pred = price[0]
     for i in order:
-        ops[i]["t"] = fin[i] - ops[i]["c"]
+        ops[i]["t"] = fin[i] - cost[i]
     pos, seen = {}, {e: 0 for e in "VAPGS"}
     for i in order:
         if ops[i]["sem"] is None:
@@ -634,7 +732,7 @@ def schedule():
             if sem and pos[j][1] > want.get(pos[j][0], (0, 0))[0]:
                 want[pos[j][0]] = (pos[j][1], j)
         o["w"] = []
-        for key, (v, j) in sorted(want.items(), key=lambda kv: -fin[kv[1][1]] - ops[kv[1][1]]["lat"]):
+        for key, (v, j) in sorted(want.items(), key=lambda kv: -fin[kv[1][1]] - lat[kv[1][1]]):
             if kn.get(key, 0) < v:
                 o["w"].append(j); need.add(j)
                 for k2, v2 in clock[j].items():
@@ -650,7 +748,7 @@ def schedule():
             ops[i]["n"] = count[ops[i]["e"]]
         else:
             ops[i]["n"] = 0
-    return ops, order, max(fin[i] + ops[i]["lat"] for i in range(n))
+    return ops, order, times
 
 
 PLAN = []

@@ -3,15 +3,8 @@ from concourse.mybir import AluOpType as ALU, ActivationFunctionType as AF
 F, B, I, U, H16 = "float32", "bfloat16", "int32", "uint16", "float16"
 RO, PW = 5, 80
 SCRATCH = {}
-CFG = {"G1": ["V01", "A12", "A23", "A34"], "G2": ["V01", "A12", "V23", "A34"], "UW": 1, "CP": "VVVV", "SG": "AAAV", "AB": "AAAA", "PL": "VV", "EP": "A",
-       "MS": "C", "ME": "VA", "NR": "A", "X2": 0, "NZ": 4, "NX": 2, "D3": 1, "MW": 1, "OR": 1, "OWN": "",
-       "BANK": {"K0": "pS0", "D0": "pS0", "K1": "pS0", "D1": "pS0", "E0": "pS0", "E1": "pS0", "U": "pS0", "V0": "pV", "V1": "pV", "P0": "pS0", "P1": "pS0"}}
-
-
-def _buf(name, n, dt, where="sbuf"):
-    SCRATCH[name] = (where, [128] + (n if isinstance(n, list) else [n]), dt)
-
-
+CFG = {"G1": "AVAAAVAA", "G2": "VAVAVAVA", "CP": "VVVV", "SG": "AAAVAAAV", "ME": "VVA", "MS": "VVVV",
+       "TN": "V", "VC": "V", "X2": 0, "NZ": 4, "NX": 2, "PU": 1, "SM": 1, "VB": 1, "ML": 1, "MV": 0}
 PSUM = []
 
 
@@ -24,47 +17,48 @@ def declare():
         ("pi", 8, I), ("pb", 8, I), ("pc", 16, F), ("iot", 160, F), ("kk8", 128, F), ("ii8", 128, F), ("kk16", 128, F),
         ("ta", 128, F), ("tb", 128, F), ("I16", 128, B), ("Pf", 160, F), ("P0", 160, H16), ("P1", 160, H16),
         ("W1", 144, B), ("WA", 144, B), ("Ww", 144, B), ("W8", 144, B), ("Wb", 128, B), ("Mx", 128, B), ("ME", 16, B),
-        ("sel", 1024, B), ("kc", 72, B), ("kap", 144, F), ("d0k", 72, F), ("lo4", 72, F), ("neg", 128, B), ("zer", 128, B),
-        ("c2k", 128, B), ("o16", 128, F), ("ji", 16, I), ("jf", 16, F), ("jq", 16, I), ("jr", 16, F),
-        ("Lm", 16, U), ("Lh", 8, U), ("l32", 8, I), ("l32b", 8, I),
+        ("sel", 1024, B), ("kc", 128, B), ("kap", 256, F), ("d0k", 64, F), ("lo4", 72, F), ("neg", 128, B), ("zer", 128, B),
+        ("c2k", 128, B), ("o16", 128, F), ("ji", 16, I), ("jf", 16, F), ("jq", 16, I), ("jk", 16, I),
+        ("Lm", 16, U), ("Lk", 16, U), ("l32", 8, I), ("l32b", 8, I),
         ("ui", 8, I), ("ub", 16, I), ("uI", 40, I), ("mU", 40, F), ("oU", 40, F), ("ob", 40, F), ("cx", 8, I), ("col", 40, U),
         ("Acol", 16, F), ("cnt", 16, F), ("y128", 128, B), ("yo", 128, B), ("hx", 128, F), ("wv", 512, B),
-        ("ycs", 128, F), ("pay", 2 * RO * PW, F), ("land", 2 * RO * PW, F),
+        ("ycs", 128, F), ("pay", [2 * RO, PW], F), ("land", [2 * RO, PW], F), ("payv", [2 * RO, 64], B), ("landv", [2 * RO, 64], B),
+        ("A", [8, 18], F), ("Af", [8, 18], H16), ("S", 128, F), ("H", 144, F), ("Ki", 8, I), ("oi", 8, I), ("ei", 8, I),
+        ("fi", 16, I), ("ov", 8, U), ("nr", 24, F), ("TH", 16, F), ("oo", 8, F), ("mk", 256, F), ("Q", 128, F), ("ep", 128, F),
+        ("tn", [8, 18], I), ("tf", [8, 18], F), ("tp", [8, 18], I), ("pf", [8, 18], F), ("dp", 128, F), ("Qp", 128, F), ("pn", 128, F), ("Ms", 128, F),
     ]:
-        _buf(n, w, d)
-    wide = [4, 288] if CFG["D3"] else 1152
+        SCRATCH[n] = ("sbuf", [128] + (w if isinstance(w, list) else [w]), d)
     for h in "01":
-        for n, w, d in [
-            ("A", 80, F), ("Af", 80, H16), ("t", 64, I), ("tf", 64, F), ("p", 64, I), ("off", 64, U), ("xa", 1024, B), ("xT", 1024, B),
-            ("ind", wide, B), ("g2", 1024, B), ("ab", wide, B), ("S", 72, F), ("Ki", 8, I), ("oi", 8, I), ("ei", 8, I),
-            ("fi", 8, I), ("ov", 8, U), ("nr", 16, F), ("TH", 8, F), ("oo", 8, F), ("mk", 144, F), ("Q", 80, F),
-            ("H", 80, F), ("Ms", 80, F), ("ep", 80, F), ("vT", 128, B), ("thb", 80, B),
-        ]:
-            _buf(n + h, w, d)
-    for n in ["pZ%d" % j for j in range(CFG["NZ"])] + sorted(set(CFG["BANK"].values())):
-        _buf(n, 512, F, "psum")
+        for n, w, d in [("t", 128, I), ("off", 64, U), ("xa", 1024, B), ("xT", 1024, B), ("ind", 1024, B), ("g2", 1024, B), ("ab", [4, 288], B),
+                        ("vT", 128, B), ("thb", 80, B)]:
+            SCRATCH[n + h] = ("sbuf", [128] + (w if isinstance(w, list) else [w]), d)
+    for n, w, d in ([("pZ%d" % j, [512], F) for j in range(CFG["NZ"])] + [("pX%d" % j, [1024], B) for j in range(CFG["NX"])]
+                    + [("pS", [512], F), ("pV", [8, 64], F)]):
+        SCRATCH[n] = ("psum", [128] + w, d)
         PSUM.append(n)
-    for j in range(CFG["NX"]):
-        _buf("pX%d" % j, 1024, B, "psum")
-        PSUM.append("pX%d" % j)
 
 
 declare()
 DMAS = ["dc", "dy", "dw", "dx0", "dx1", "ds", "dt", "dyc0", "dyc1", "dyy"]
-SEMAPHORES = ["nV", "nA", "nP", "nG", "loc"] + DMAS + ["arr%d" % i for i in range(2 * RO)]
+
+
+def writes():
+    parts = ([("", 64, PW), ("v", 0, 64)] if CFG["VB"] else [("", 68, PW), ("", 0, 68)]) if CFG["SM"] else [("", 0, PW)]
+    return [(len(parts) * n + j, n // 2, n, v, lo, hi) for n in range(2 * RO) for j, (v, lo, hi) in enumerate(parts)]
+
+
+SEMAPHORES = ["nV", "nA", "nP", "nG", "loc"] + DMAS + ["arr%d" % w[0] for w in writes()]
 CNT = {"V": "nV", "A": "nA", "P": "nP", "G": "nG"}
 BIG = 1.0e9
-REG = {"K0": 72, "K1": 72, "D0": 72, "D1": 72, "E0": 64, "E1": 64, "U": 16, "V0": 216, "V1": 216, "P0": 72, "P1": 72}
+RUN = 4
 
 
 def s(b, lo=0, hi=None, st=1, p0=0, p1=128, sg=None):
     return (b, lo, SCRATCH[b][1][-1] if hi is None else hi, st, p0, p1, sg)
 
 
-def seg(b, c0, c1, lo, hi, st=1):
-    if CFG["D3"]:
-        return s(b, lo, hi, st, sg=(c0, c1))
-    return s(b, 288 * c0 + lo, 288 * (c1 - 1) + hi, st)
+def z(b, a0, a1, lo, hi, st=1):
+    return s(b, lo, hi, st, sg=(a0, a1))
 
 
 def ind(w, o):
@@ -75,9 +69,14 @@ def ap(T, x):
     if x[0] == "*":
         return ap(T, x[1]).indirect(ap(T, x[2]))
     b, lo, hi, st, p0, p1, sg = x
-    if sg is not None:
-        return T[b][p0:p1, sg[0]:sg[1], lo:hi:st] if st != 1 else T[b][p0:p1, sg[0]:sg[1], lo:hi]
-    return T[b][p0:p1, lo:hi:st] if st != 1 else T[b][p0:p1, lo:hi]
+    cols = slice(lo, hi, st) if st != 1 else slice(lo, hi)
+    if sg is None:
+        return T[b][p0:p1, cols]
+    if sg[1] - sg[0] == 1:
+        return T[b][p0:p1, sg[0], cols]
+    if hi - lo == 1:
+        return T[b][p0:p1, sg[0]:sg[1], lo]
+    return T[b][p0:p1, sg[0]:sg[1], cols]
 
 
 def nel(x):
@@ -93,19 +92,8 @@ def two(*xs):
 def program():
     ops = []
     half = [1]
-    at, used = {}, {}
-    for r_ in ("K0", "K1", "D0", "D1", "E0", "E1", "U", "V0", "V1", "P0", "P1"):
-        b_ = CFG["BANK"][r_]
-        at[r_] = (b_, used.get(b_, 0))
-        used[b_] = used.get(b_, 0) + REG[r_]
-        assert used[b_] <= 512 or (r_[0] == "P" and CFG["EP"] != "P")
 
-    def rg(r, lo, hi, st=1):
-        if r == "E":
-            r, lo, hi = ("E0", lo, hi) if lo < 64 else ("E1", lo - 64, hi - 64)
-        return s(at[r][0], at[r][1] + lo, at[r][1] + hi, st)
-
-    def add(eng, fn, R, W, kind, n, sem=None, grp=None):
+    def add(eng, fn, R, W, kind, n, sem=None, grp=None, join=False):
         rr, ww = [], []
         for x in R:
             if isinstance(x, tuple):
@@ -115,6 +103,10 @@ def program():
                 ww.append(x[1]); rr.append(x[2])
             else:
                 ww.append(x)
+        if join:
+            o, f0 = ops[-1], ops[-1]["f"]
+            o.update(f=lambda g, T, x: (f0(g, T, x), fn(g, T, x))[1], R=o["R"] + rr, W=o["W"] + ww, c=o["c"] + n)
+            return
         ops.append({"e": eng, "f": fn, "R": rr, "W": ww, "k": kind, "c": n, "sem": sem, "grp": grp, "h": half[0]})
 
     def val(T, x):
@@ -159,12 +151,12 @@ def program():
             add("A", lambda g, T, x: g.scalar.activation(ap(T, o), ap(T, a), fn, bias=val(T, bias), scale=val(T, scale), accum_out=ap(T, acc)),
                 [a, bias, scale], [o, acc], k, max(64, nel(a)) + 20)
 
-    def MM(o, l, r, start, stop):
+    def MM(o, l, r, start, stop, join=False):
         c = max(min(64, nel(l)), nel(r)) * (4 if SCRATCH[l[0]][2] == F else 1)
-        add("P", lambda g, T, x: g.tensor.matmul(ap(T, o), ap(T, l), ap(T, r), start, stop), [l, r], [o], "p", c, grp=True)
+        add("P", lambda g, T, x: g.tensor.matmul(ap(T, o), ap(T, l), ap(T, r), start, stop), [l, r], [o], "p", c, grp=True, join=join)
 
-    def TR(o, a):
-        add("P", lambda g, T, x: g.tensor.transpose(ap(T, o), ap(T, a), ap(T, s("I16"))), [a, s("I16")], [o], "p", 128, grp=True)
+    def TR(o, a, join=False):
+        add("P", lambda g, T, x: g.tensor.transpose(ap(T, o), ap(T, a), ap(T, s("I16"))), [a, s("I16")], [o], "p", 128, grp=True, join=join)
 
     def IO(o, pat, base, cm):
         if SCRATCH[o[0]][2] == I:
@@ -178,22 +170,18 @@ def program():
         else:
             add(q, lambda g, T, x: g.scalar.dma_start(ap(T, o), T[name][:]), list(after), [o], "d", lat, sem=(sem, 16))
 
-    def col(b, j):
-        return s(b, j, j + 1)
+    def col(b, j, n=None):
+        return s(b, j, j + 1) if n is None else z(b, n, n + 1, j, j + 1)
 
     mul, ad, sub, mx, mn = ALU.mult, ALU.add, ALU.subtract, ALU.max, ALU.min
     band, shr = ALU.bitwise_and, ALU.logical_shift_right
     I32 = s("Pf", 16, 144)
-    UW, X2 = CFG["UW"], CFG["X2"]
-    SW = UW if CFG["D3"] else 1
-    turn = {}
+    X2, MV = CFG["X2"], CFG["MV"]
+    turn = {"Z": -1, "X": -1}
 
-    def nxt(k, h):
-        own = k in CFG["OWN"]
-        n = CFG["N" + k] // (2 if own else 1)
-        key = (k, h if own else 0)
-        turn[key] = turn.get(key, -1) + 1
-        return "p%s%d" % (k, turn[key] % n + (n * h if own else 0))
+    def nxt(k):
+        turn[k] += 1
+        return "p%s%d" % (k, turn[k] % CFG["N" + k])
 
     LD("A", s("X0"), "x0", "dx0", 5000)
     LD("S", s("cin"), "c0", "dc", 2300)
@@ -240,82 +228,67 @@ def program():
     for h in range(2):
         x_ = s("sel", p0=64 * h, p1=64 * h + 64)
         add("G", lambda g, T, x, x_=x_: g.affine_select(ap(T, x_), ap(T, x_), [[-16, 4], [0, 16], [-1, 16]], eq, 0.0, 0, 1), [x_], [x_], "G", 1040)
-    IO(s("kc", p1=32), [[-512, 4], [-32, 18]], 2048, 0)
-    IO(s("kc", p0=32, p1=64), [[0, 72]], 2064, 0)
-    MS(s("kc", p0=64), 0.0)
-    for c in range(4):
-        if CFG["SG"][c - c % SW] == "A":
-            MS(s("kc", 18 * c, 18 * c + 18, 1, 64, 96), float(2 ** 15))
-    IO(s("kap", 0, 72), [[-256, 4], [-16, 18]], 2048, 0)
-    IO(s("kap", 72, 144), [[-256, 4], [-16, 18]], -2063, 0)
+    IO(s("kc", p1=32), [[0, 2], [-32, 64]], 2016, 0)
+    IO(s("kc", p0=32, p1=64), [[0, 128]], 2064, 0)
+    MS(s("kc", p0=96), 0.0)
+    MS(s("kc", p0=64, p1=96), float(2 ** 15))
+    for c in range(8):
+        if CFG["SG"][c] == "V":
+            MS(s("kc", 16 * c, 16 * c + 16, 1, 64, 96), 0.0)
+    nh = 2 if MV else 1
+    IO(s("kap", 0, 64 * nh), [[0, nh], [-16, 64]], 2032, 0)
+    IO(s("kap", 64 * nh, 128 * nh), [[0, nh], [-16, 64]], -2063, 0)
     IO(s("kk16"), [[1, 8], [0, 16]], 0, 0)
     TS(s("Wb"), s("kk16"), col("pc", 2), eq, col("pc", 13), mul)
     MS(s("d0k"), BIG)
-    MS(s("d0k", 1, 72, 18), -BIG)
-    MS(s("d0k", 2, 72, 18), -BIG)
+    MS(s("d0k", 0, 64, 16), -BIG)
+    MS(s("d0k", 1, 64, 16), -BIG)
     MS(s("lo4"), 0.0)
     MS(s("lo4", 0, 72, 18), 1.0)
     MS(s("lo4", 17, 72, 18), -BIG)
     MS(s("thm"), -1.0)
     MS(s("thm", 17, 72, 18), 0.0)
     MS(s("thZ"), 0.0)
-    IO(s("ji", 0, 10), [[16, 10]], 0, 1)
-    TS(s("jf", 0, 10), s("ji", 0, 10), col("pc", 11), ad)
-    TS(s("jq", 0, 10), s("jf", 0, 10), 1.0 / 18, mul, -0.47, ad)
-    CP(s("Lm", 0, 10), s("jq", 0, 10))
-    if CFG["MS"] == "I":
-        TS(s("jr", 0, 6), s("jq", 0, 6), 18.0, mul, 17.0, ad)
-        if CFG["EP"] == "V":
-            TT(s("jr", 8, 14), s("jr", 0, 6), s("jf", 0, 6), sub)
-            TS(s("jr", 8, 14), s("jr", 8, 14), 1.5, ALU.is_lt, 99.0, mul)
-            TT(s("jr", 0, 6), s("jr", 0, 6), s("jr", 8, 14), ad)
-        TS(s("Lh", 0, 6), s("jr", 0, 6), 72.0, mn)
+    IO(s("ji", 0, 6), [[16, 6]], 0, 1)
+    TS(s("jf", 0, 6), s("ji", 0, 6), col("pc", 11), ad)
+    TS(s("jq", 0, 6), s("jf", 0, 6), 1.0 / 18, mul, -0.47, ad)
+    CP(s("Lm", 0, 6), s("jq", 0, 6))
+    IO(s("jk"), [[1, 16]] if MV else [[4, 2], [8, 2], [1, 4]], 0, 0)
+    CP(s("Lk"), s("jk"))
+    MS(s("TH"), 0.0)
     IO(s("l32b"), [[512, 8]], 0, 32)
     TS(s("l32"), s("l32b"), col("pc", 12), ad)
+    MS(z("pV", 0, 8, 0, 18, 17), 0.0)
     for h in "01":
-        MS(s("A" + h, 72, 80), 0.0)
-        MS(s("H" + h, 72, 80), -2.0)
-        MS(s("H" + h, 73, 80), 0.0)
-        for b in ("ab", "ind"):
-            if CFG["D3"]:
-                MS(seg(b + h, 0, 4, 0, 16), 0.0)
-                MS(seg(b + h, 0, 4, 272, 288), 0.0)
-            else:
-                MS(s(b + h), 0.0)
-        if CFG["EP"] == "A":
-            MS(s("ep" + h), 0.0)
-        elif CFG["EP"] == "P":
-            MS(rg("P" + h, 0, 72), 0.0)
-        MS(rg("V" + h, 144, 145), 0.0)
-        if CFG["MS"] == "C":
-            MS(rg("V" + h, 72, 144), 0.0)
+        MS(z("ab" + h, 0, 4, 0, 16), 0.0)
+        MS(z("ab" + h, 0, 4, 272, 288), 0.0)
     TS(s("cf"), s("cin"), -2048.0, ad)
     VT(s("ct"), s("cf"))
     for h in range(2):
         ps = "pZ%d" % h
-        MM(s(ps, 340, 412), s("zer"), s("zer", 0, 72), True, False)
+        MM(s(ps, 0, 64), s("zer"), s("zer", 0, 64), True, False)
         for c in range(4):
             for g2 in range(2):
                 o_ = 16 + 16 * (c & 1) - 16 * g2
                 k0 = 32 * (2 * h + (c >> 1)) + 16 * g2
-                MM(s(ps, 341 + 18 * c, 357 + 18 * c), s("P%d" % (c & 1), o_, o_ + 128), s("ct", k0, k0 + 16), False, c == 3 and g2 == 1)
-        AC(s("A%d" % h, 0, 72), s(ps, 340, 412))
+                MM(s(ps, 16 * c, 16 * c + 16), s("P%d" % (c & 1), o_, o_ + 128), s("ct", k0, k0 + 16), False, c == 3 and g2 == 1, True)
+        AC(z("A", 4 * h, 4 * h + 4, 1, 17), s(ps, 0, 64))
 
     def sums(t, ysrc):
         a, b = 8 * t, 8 * t + 8
-        pu = rg("U", 0, 8)
+        pu = s("pS", 400, 408)
         if t > 0:
             MM(pu, s("Wb"), s("neg", 0, 8), True, False)
         for r in range(16):
-            MM(pu, s("Ww", 15 - r, 143 - r), s(ysrc, r, 128, 16), t == 0 and r == 0, r == 15)
+            MM(pu, s("Ww", 15 - r, 143 - r), s(ysrc, r, 128, 16), t == 0 and r == 0, r == 15, r % RUN > 0)
         CP(s("ui"), pu)
         TS(s("uI", a, b), s("ui"), 2047, band)
         TS(s("mU", a, b), s("uI", a, b), 2.0, mul, 33.0, ad)
         if t == 0:
             AC(s("oU", a, b), s("mU", a, b), scale=2048.0, bias=-float(2 ** 22))
         else:
-            MM(rg("U", 8, 10), s("o16"), s("cnt", 2 * t - 2, 2 * t), True, True)
-            AC(s("Acol", 8, 10), rg("U", 8, 10), bias=float(8192 - 2 ** 21), acc=col("Acol", t))
+            MM(s("pS", 408, 410), s("o16"), s("cnt", 2 * t - 2, 2 * t), True, True)
+            AC(s("Acol", 8, 10), s("pS", 408, 410), bias=float(8192 - 2 ** 21), acc=col("Acol", t))
             AC(s("oU", a, b), s("mU", a, b), scale=2048.0, bias=col("Acol", t))
         TS(s("ub", 0, 8), s("ui"), 1, band)
         TS(s("ob", a, b), s("ub", 0, 8), 1024.0, mul, 4096.0, ad)
@@ -327,174 +300,196 @@ def program():
     def renew(t, into):
         TT(ind(s("X%d" % into), s("col", 8 * t, 8 * t + 8)), s("wv", 128 * t, 128 * t + 128), s("neg"), ad)
 
-    def places(h, mb, m0, ob_, o0, eng):
+    def places(h, m, o):
         H = str(h)
         for c in range(4):
-            a_ = s("A" + H, 18 * c + 1, 18 * c + 17)
-            if eng == "V":
-                TS(s("t" + H, 16 * c, 16 * c + 16), a_, col(mb, m0 + c), mul, col(ob_, o0 + c), ad)
-            else:
-                AC(s("tf" + H, 16 * c, 16 * c + 16), a_, scale=col(mb, m0 + c), bias=col(ob_, o0 + c))
-        if eng != "V":
-            CP(s("t" + H), s("tf" + H))
-        TS(s("p" + H), s("t" + H), 0x1FFFF, band, 5, shr)
-        CP(s("off" + H), s("p" + H))
+            TS(s("t" + H, 16 * c, 16 * c + 16), z("A", 4 * h + c, 4 * h + c + 1, 1, 17), m(c), mul, o(c), ad)
+        TS(s("t" + H, 64, 128), s("t" + H, 0, 64), 0x1FFFF, band, 5, shr)
+        CP(s("off" + H), s("t" + H, 64, 128))
 
     def gather(h, t, out, plan):
-        for x in plan:
-            c0, c1 = int(x[1]), int(x[2])
-            (CP if x[0] == "V" else AC)(s(out, 256 * c0, 256 * c1), ind(s("X%d" % (t & X2)), s("off%d" % h, 16 * c0, 16 * c1)))
+        for c in range(4):
+            e = plan[4 * h + c]
+            if e in "VA":
+                c1 = c + 1
+                while c1 < 4 and plan[4 * h + c1] not in "VA":
+                    c1 += 1
+                (CP if e == "V" else AC)(s(out, 256 * c, 256 * c1), ind(s("X%d" % (t & X2)), s("off%d" % h, 16 * c, 16 * c1)))
 
-    def values(t, lo, hi):
-        AC(s("y128", lo, hi), rg("E", lo, hi), scale=8.0, bias=192.0 - 31.0 / 64)
-        if t < RO - 1:
-            TT(s("wv", 128 * t + lo, 128 * t + hi), s("hx", lo, hi), rg("E", lo, hi), ad)
-
-    def front(t, h):
-        H = str(h); A = "A" + H; u0 = 8 * t + 4 * h; y0 = PW * (2 * t + h); v0 = 232 * h
-        half[0] = 1 - h
-        places(h, "mU", u0, "oU", u0, CFG["PL"][0])
-        gather(h, t, "xa" + H, CFG["G1"])
-        for c0 in range(0, 4, UW):
-            px, w = nxt("X", h), 256 * c0
-            pb = nxt("Z", h)
-            MM(s(pb, 0, 256 * UW), s("sT", 128 * t, 128 * t + 128, 1, 64 * h, 64 * h + 64),
-               s("sel", 256 * c0, 256 * (c0 + UW), 1, 64 * h, 64 * h + 64), True, False)
-            for c in range(c0, c0 + UW):
-                for b in range(2):
-                    z = 256 * (c - c0) + 128 * b
-                    TR(s(px, w + z, w + z + 128), s("xa" + H, 256 * c + b, 256 * c + 256, 2))
-            (CP if CFG["CP"][c0] == "V" else AC)(s("xT" + H, 256 * c0, 256 * (c0 + UW)), s(px, w, w + 256 * UW))
-            for c in range(c0, c0 + UW):
-                z = 256 * (c - c0)
-                for b in range(2):
-                    MM(s(pb, z + b, z + 256, 2), s("xT" + H, 256 * c + 128 * b, 256 * c + 128 * b + 128), s("Mx"), False, b == 1 and c == c0 + UW - 1)
-            for c in range(c0, c0 + UW, SW):
-                z = 256 * (c - c0)
-                o_, i_ = seg("ind" + H, c, c + SW, 16, 272), s(pb, z, z + 256 * SW)
-                if CFG["SG"][c] == "V":
-                    TS(o_, i_, 0.0, ALU.is_ge, 2.0, mul)
-                else:
-                    AC(o_, i_, AF.Sign, bias=0.0625)
+    def total(h):
         for ch in range(8):
             c, b = ch >> 1, ch & 1
-            MM(rg("E", 64 * h + 16 * c + b, 64 * h + 16 * c + 16, 2), s("xT" + H, 128 * ch, 128 * ch + 128), s("ME", 0, 8), True, True)
-        pk = rg("K" + H, 0, 72)
-        MM(pk, I32, s(A, 0, 72), True, False)
-        MM(pk, s("c2k"), s("kc"), False, False)
+            MM(s("pS", 272 + 64 * h + 16 * c + b, 288 + 64 * h + 16 * c, 2), s("xT%d" % h, 128 * ch, 128 * ch + 128), s("ME", 0, 8), True, True, ch % RUN > 0)
+
+    def front(t, h):
+        H = str(h); u0 = 8 * t + 4 * h; n = 2 * t + h; a0, a1 = 4 * h, 4 * h + 4
+        half[0] = 1 - h
+        if t == 0 or not CFG["PU"]:
+            places(h, lambda c: col("mU", u0 + c), lambda c: col("oU", u0 + c))
+        gather(h, t, "xa" + H, CFG["G1"])
+        for c in range(4):
+            px, w, pb = nxt("X"), 256 * c, nxt("Z")
+            MM(s(pb, 0, 256), s("sT", 128 * t, 128 * t + 128, 1, 64 * h, 64 * h + 64), s("sel", w, w + 256, 1, 64 * h, 64 * h + 64), True, False)
+            for b in range(2):
+                TR(s(px, w + 128 * b, w + 128 * b + 128), s("xa" + H, w + b, w + 256, 2), b == 1)
+            (CP if CFG["CP"][c] == "V" else AC)(s("xT" + H, w, w + 256), s(px, w, w + 256))
+            for b in range(2):
+                MM(s(pb, b, 256, 2), s("xT" + H, w + 128 * b, w + 128 * b + 128), s("Mx"), False, b == 1, b == 1)
+            if CFG["SG"][a0 + c] == "V":
+                TS(s("ind" + H, w, w + 256), s(pb, 0, 256), 0.0, ALU.is_ge, 2.0, mul)
+            else:
+                AC(s("ind" + H, w, w + 256), s(pb, 0, 256), AF.Sign, bias=0.0625)
+        if CFG["ML"] == 0:
+            total(h)
+        pk = s("pS", 64 * h, 64 * h + 64)
+        MM(pk, I32, z("A", a0, a1, 1, 17), True, False)
+        MM(pk, s("c2k"), s("kc", 64 * h, 64 * h + 64), False, False, True)
         for r in range(16):
-            MM(pk, s("WA", 15 - r, 143 - r), seg("ind" + H, 0, 4, r, 288, 16), False, r == 15)
-        SC(s("S" + H), s("d0k"), pk, -BIG, mn, mx)
-        K0, KS = s("S" + H, 1, 72, 18), s("S" + H, 16, 72, 18)
-        q = lambda b, j=0: s(b + H, j, j + 4)
+            MM(pk, s("WA", 15 - r, 143 - r), s("ind" + H, r, 1024, 16), False, r == 15, r % RUN > 0)
+        SC(s("S", 64 * h, 64 * h + 64), s("d0k"), pk, -BIG, mn, mx)
+        if CFG["ML"] == 1:
+            total(h)
+        if CFG["ML"] == 2 and h == 1:
+            total(0)
+            total(1)
+        K0, KS = s("S", 64 * h, 64 * h + 64, 16), s("S", 64 * h + 15, 64 * h + 64, 16)
+        q = lambda b, j=0: s(b, j + a0, j + a1)
         CP(q("Ki"), KS)
         TS(q("oi"), q("Ki"), 8, shr, 0x7F0, band)
         TS(q("ov"), q("oi"), -1.0, mul, col("pc", 4), ad)
-        AC(s("pay", y0, y0 + 64), ind(s("xa" + H), q("ov")))
+        AC(z("payv" if CFG["VB"] else "pay", n, n + 1, 0, 64), ind(s("xa" + H), q("ov")))
         TS(q("ei"), q("Ki"), 4095, band)
-        ee, me, oe, gs = [s("pay", y0 + 64 + 4 * j, y0 + 68 + 4 * j) for j in range(4)]
-        TS(ee, q("ei"), -2048.0, ad)
-        if CFG["ME"][0] == "V":
-            TS(me, q("ei"), 32.0, ad)
-        else:
-            AC(me, ee, bias=2080.0)
+        gs, ee, me, oe = [z("pay", n, n + 1, 64 + 4 * j, 68 + 4 * j) for j in range(4)]
+        TS(me, q("ei"), 32.0, ad)
         if CFG["ME"][1] == "V":
+            TS(ee, q("ei"), -2048.0, ad)
+        else:
+            AC(ee, me, bias=-2080.0)
+        if CFG["ME"][2] == "V":
             TS(oe, q("ei"), -2048.0, ad, 3232.0, mul)
         else:
-            AC(oe, ee, scale=3232.0)
-        if CFG["NR"] == "V":
-            TS(q("nr"), K0, float(9 * 2 ** 19), ALU.is_lt, 65536.0, mul)
-        else:
-            AC(q("nr"), K0, AF.Relu, scale=-65536.0, bias=float(9 * 2 ** 35))
-        TT(q("nr", 4), K0, KS, sub)
-        TT(q("nr", 8), q("nr"), q("nr", 4), mul)
+            AC(oe, me, scale=3232.0, bias=-3232.0 * 2080)
+        AC(q("nr"), K0, AF.Relu, scale=-65536.0, bias=float(9 * 2 ** 35))
+        TT(q("nr", 8), K0, KS, sub)
+        TT(q("nr", 16), q("nr"), q("nr", 8), mul)
         if t < RO - 1:
-            AC(gs, q("nr", 8), AF.Sign, bias=-1.0, acc=col("cnt", 2 * t + h))
+            AC(gs, q("nr", 16), AF.Sign, bias=-1.0, acc=col("cnt", n))
         else:
-            AC(gs, q("nr", 8), AF.Sign, bias=-1.0)
-        n = 2 * t + h
-        add("G", lambda g, T, x: x["send"](n), [s("pay", y0, y0 + PW)], [s("land", y0, y0 + PW)], "r", 1 if t & 1 else 2, sem=("arr%d" % n, 0))
-        if t < RO - 1 and h == 0:
+            AC(gs, q("nr", 16), AF.Sign, bias=-1.0)
+        for m_, t_, n_, v, lo, hi in writes():
+            if n_ == n:
+                add("G", lambda g, T, x, m_=m_: x["send"](m_), [z("pay" + v, n, n + 1, lo, hi)], [z("land" + v, n, n + 1, lo, hi)], "r",
+                    (1 if t & 1 else 2, (hi - lo) * (2 if v else 4)), sem=("arr%d" % m_, 0))
+        if h == 0 and t < RO - 1:
             AC(s("hx"), ind(s("X%d" % (t & X2)), s("col", 8 * t, 8 * t + 8)), scale=0.5, bias=192.0 - 255.0 / 512)
-        if not CFG["MW"]:
-            values(t, 64 * h, 64 * h + 64)
+        if h == 1:
+            pe = s("pS", 272, 400)
+            AC(s("y128"), pe, scale=8.0, bias=192.0 - 31.0 / 64)
+            if t < RO - 1:
+                TT(s("wv", 128 * t, 128 * t + 128), s("hx"), pe, ad)
+        if not MV:
+            moves(t, h, h + 1)
         elif h == 1:
-            values(t, 0, 128)
-        AC(s(A, 0, 72, 18), ee)
-        TT(q("fi"), me, s("uI", u0, u0 + 4), mul)
-        TS(q("fi", 4), q("fi"), 0x1FFFF, band, 5, shr)
-        TS(s(A, 17, 72, 18), q("fi", 4), -2048.0, ad)
-        TT(q("TH"), q("oi"), q("nr", 8), mn)
-        TT(q("oo"), q("oi"), s("ob", u0, u0 + 4), sub)
-        TT(q("TH", 4), q("oo"), q("nr", 8), mx)
-        TT(s("mk" + H), ind(s("TH" + H), s("Lm", 0, 9)), s("kap"), ALU.is_ge)
-        V = "V" + H
-        TT(rg(V, 0, 71), s(A, 1, 72), s(A, 0, 71), sub)
-        TT(rg(V, 72, 142), s("mk" + H, 72, 142), rg(V, 0, 70), mul)
-        TT(rg(V, 145, 215), s("mk" + H, 1, 71), rg(V, 1, 71), mul)
-        TT(s("Q" + H, 0, 70), s(A, 0, 70), rg(V, 72, 142), ad)
-        TT(s(A, 1, 71), s("Q" + H, 0, 70), rg(V, 145, 215), ad)
+            moves(t, 0, 2)
+
+    def moves(t, h0, h1):
+        a0, a1 = 4 * h0, 4 * h1
+        w, m0 = 16 * (a1 - a0), 128 * h0
+        me = z("pay", 2 * t + h0, 2 * t + h1, 72, 76)
+        q = lambda b, j=0: s(b, j + a0, j + a1)
+        AC(z("A", a0, a1, 0, 1), me, bias=-2080.0)
+        TT(q("fi"), me, s("uI", 8 * t + a0, 8 * t + a1), mul)
+        TS(q("fi", 8), q("fi"), 0x1FFFF, band, 5, shr)
+        TS(z("A", a0, a1, 17, 18), q("fi", 8), -2048.0, ad)
+        TT(q("TH"), q("oi"), q("nr", 16), mn)
+        TT(q("oo"), q("oi"), s("ob", 8 * t + a0, 8 * t + a1), sub)
+        TT(q("TH", 8), q("oo"), q("nr", 16), mx)
+        TT(s("mk", m0, m0 + 2 * w), ind(s("TH"), s("Lk", 2 * a0, 2 * a1)), s("kap", 0, 2 * w), ALU.is_ge)
+        TT(z("pV", a0, a1, 34, 51), z("A", a0, a1, 1, 18), z("A", a0, a1, 0, 17), sub)
+        TT(z("pV", a0, a1, 1, 17), s("mk", m0 + w, m0 + 2 * w), z("pV", a0, a1, 34, 50), mul)
+        TT(z("pV", a0, a1, 18, 34), s("mk", m0, m0 + w), z("pV", a0, a1, 35, 51), mul)
+        TT(s("Q", 16 * a0, 16 * a1), z("A", a0, a1, 0, 16), z("pV", a0, a1, 1, 17), ad)
+        TT(z("A", a0, a1, 1, 17), s("Q", 16 * a0, 16 * a1), z("pV", a0, a1, 18, 34), ad)
 
     def back(t, h):
-        H = str(h); A = "A" + H; y0 = PW * (2 * t + h); w0 = 144; V = "V" + H
+        H = str(h); n = 2 * t + h; a0, a1 = 4 * h, 4 * h + 4
         half[0] = 1 - h
-        places(h, "land", y0 + 68, "land", y0 + 72, CFG["PL"][1])
-        pbs = [nxt("Z", h) for c0 in range(0, 4, UW)]
-        pv = s(pbs[0], 0, 128, 1, 0, 64)
-        MM(pv, s("land", y0, y0 + 64), I32, True, True)
-        AC(s("vT" + H, p1=64), pv)
+        q = lambda b: s(b, 64 * h, 64 * h + 64)
+        places(h, lambda c: col("land", 72 + c, n), lambda c: col("land", 76 + c, n))
+        AC(z("A", a0, a1, 0, 1), z("land", n, n + 1, 68, 72))
+        ahead = CFG["PU"] and t < RO - 1
+        if ahead:
+            u1 = 8 * (t + 1) + a0
+            for c in range(4):
+                a_ = z("A", a0 + c, a0 + c + 1, 0, 17)
+                if CFG["TN"] == "V":
+                    TS(z("tn", a0 + c, a0 + c + 1, 0, 17), a_, col("mU", u1 + c), mul, col("oU", u1 + c), ad)
+                else:
+                    AC(z("tf", a0 + c, a0 + c + 1, 0, 17), a_, scale=col("mU", u1 + c), bias=col("oU", u1 + c))
+            if CFG["TN"] != "V":
+                CP(z("tn", a0, a1, 0, 17), z("tf", a0, a1, 0, 17))
+            TS(z("tp", a0, a1, 0, 17), z("tn", a0, a1, 0, 17), 0x1FFFF, band, 5, shr)
+            CP(z("pf", a0, a1, 0, 17), z("tp", a0, a1, 0, 17))
+            for c in range(a0, a1):
+                AC(s("dp", 16 * c, 16 * c + 16), z("pf", c, c + 1, 1, 17), scale=-1.0, bias=col("pf", 0, c))
+        pbs = [nxt("Z") for c in range(4)]
+        if CFG["VB"]:
+            pv = s(nxt("X"), 0, 128, 1, 0, 64)
+            TR(pv, z("landv", n, n + 1, 0, 64))
+        else:
+            pv = s(pbs[0], 0, 128, 1, 0, 64)
+            MM(pv, z("land", n, n + 1, 0, 64), I32, True, True)
+        (AC if CFG["VC"] == "A" else CP)(s("vT" + H, p1=64), pv)
         gather(h, t, "g2" + H, CFG["G2"])
-        if CFG["EP"] == "V":
-            ep = s("ep" + H, 1, 71)
-            TT(s("ep" + H), ind(s("land", y0 + 64, y0 + 80), s("Lm", 0, 5)), s(A), sub)
-        else:
-            e_ = (lambda lo, hi: s("ep" + H, lo, hi)) if CFG["EP"] == "A" else (lambda lo, hi: rg("P" + H, lo, hi))
-            ep = e_(1, 71)
-            for c in range(4):
-                AC(e_(1 + 18 * c, 17 + 18 * c), s(A, 18 * c + 1, 18 * c + 17), scale=-1.0, bias=col("land", y0 + 64 + c))
-        for c0 in range(0, 4, UW):
-            pb = pbs[c0 // UW]
-            o_ = s(pb, 0, 256 * UW)
-            MM(o_, s("vT" + H, p1=64), s("sel", 256 * c0, 256 * (c0 + UW), 1, 0, 64), True, False)
-            MM(o_, s("I16"), s("g2" + H, 256 * c0, 256 * (c0 + UW)), False, True)
-            for c in range(c0, c0 + UW, SW):
-                z = 256 * (c - c0)
-                AC(seg("ab" + H, c, c + SW, 16, 272), s(pb, z, z + 256 * SW), AF.Abs)
-        pd = rg("D" + H, 0, 72)
+        for c in range(4):
+            AC(s("ep", 64 * h + 16 * c, 64 * h + 16 * c + 16), z("A", a0 + c, a0 + c + 1, 1, 17), scale=-1.0, bias=col("land", 68 + c, n))
+        for c in range(4):
+            o_, w = s(pbs[c], 0, 256), 256 * c
+            MM(o_, s("vT" + H, p1=64), s("sel", w, w + 256, 1, 0, 64), True, False)
+            MM(o_, s("I16"), s("g2" + H, w, w + 256), False, True)
+            AC(z("ab" + H, c, c + 1, 16, 272), o_, AF.Abs)
+        d0 = 128 + 72 * h
+        pd = s("pS", d0, d0 + 72)
         MM(pd, s("I16"), s("thb" + H, 0, 72), True, False)
-        MM(rg("D" + H, 17, 72, 18), I32, s("land", y0 + 76, y0 + 80), False, False)
+        MM(s("pS", d0 + 17, d0 + 72, 18), I32, z("land", n, n + 1, 64, 68), False, False)
         for r in range(16):
-            MM(pd, s("W1", 15 - r, 143 - r), seg("ab" + H, 0, 4, r, 288, 16), False, r == 15)
-        SC(s("H" + H, 0, 72), pd, s("lo4"), 1.0, mn, mx)
-        if CFG["MS"] == "I":
-            TT(s("Ms" + H), ind(s("H" + H), s("Lh", 0, 5)), s("H" + H), ALU.is_ge)
-            ms = s("Ms" + H, 0, 70)
-        else:
-            for c in range(4):
-                TS(rg(V, 72 + 18 * c, 88 + 18 * c), s("H" + H, 18 * c, 18 * c + 16), col("H" + H, 18 * c + 17), ALU.is_le)
-            ms = rg(V, 72, 142)
-        TT(rg(V, w0 + 1, w0 + 71), ms, ep, mul)
-        TT(s("Q" + H, 1, 71), s(A, 1, 71), rg(V, w0 + 1, w0 + 71), ad)
-        TT(s(A if t < RO - 1 else "Af" + H, 1, 71), s("Q" + H, 1, 71), rg(V, w0, w0 + 70), sub)
+            MM(pd, s("W1", 15 - r, 143 - r), z("ab" + H, 0, 4, r, 288, 16), False, r == 15, r % RUN > 0)
+        SC(s("H", 72 * h, 72 * h + 72), pd, s("lo4"), 1.0, mn, mx)
+        inp = "A" not in CFG["MS"]
+        for c in range(a0, a1):
+            o_ = z("pV", c, c + 1, 34, 50) if inp else s("Ms", 16 * c, 16 * c + 16)
+            if CFG["MS"][c - a0] == "V":
+                TS(o_, s("H", 18 * c, 18 * c + 16), col("H", 18 * c + 17), ALU.is_gt, -1.0, mul)
+            else:
+                AC(o_, s("H", 18 * c, 18 * c + 16), AF.Sign, scale=-1.0, bias=col("H", 18 * c + 17))
+        ms = z("pV", a0, a1, 34, 50) if inp else q("Ms")
+        if ahead:
+            TT(z("pV", a0, a1, 1, 17), ms, q("dp"), mul)
+            TT(q("Qp"), z("pf", a0, a1, 0, 16), z("pV", a0, a1, 1, 17), ad)
+            TT(q("pn"), q("Qp"), z("pV", a0, a1, 0, 16), sub)
+            CP(s("off" + H), q("pn"))
+        TT(z("pV", a0, a1, 18, 34), ms, q("ep"), mul)
+        TT(q("Q"), z("A", a0, a1, 0, 16), z("pV", a0, a1, 18, 34), ad)
+        TT(z("A" if t < RO - 1 else "Af", a0, a1, 1, 17), q("Q"), z("pV", a0, a1, 17, 33), sub)
 
     def finish(h):
-        H = str(h); ps = nxt("Z", h)
+        H = str(h); ps = nxt("Z")
         MM(s(ps, 0, 64), s("c2k"), s("c2k", 0, 64), True, False)
         for cp in range(2):
             for g2 in range(2):
                 for c2 in range(2):
-                    o_ = 16 + 16 * g2 - 16 * c2; k0 = 18 * (2 * cp + c2) + 1; w = 32 * cp + 16 * g2
-                    MM(s(ps, w, w + 16), s("P%d" % g2, o_, o_ + 128), s("Af" + H, k0, k0 + 16), False, cp + g2 + c2 == 3)
+                    o_ = 16 + 16 * g2 - 16 * c2; c = 4 * h + 2 * cp + c2; w = 32 * cp + 16 * g2
+                    MM(s(ps, w, w + 16), s("P%d" % g2, o_, o_ + 128), z("Af", c, c + 1, 1, 17), False, cp + g2 + c2 == 3, cp + g2 + c2 > 0)
         VT(s("ycs", 64 * h, 64 * h + 64), s(ps, 0, 64))
         x_ = s("ycs", 64 * h, 64 * h + 64)
         add("S", lambda g, T, x: g.sync.dma_start(T.yc[:, 64 * h:64 * h + 64], ap(T, x_)), [x_], [], "d", 2000, sem=("dyc" + H, 16))
 
     sums(0, "yin")
     for t in range(RO):
-        TR(s("pX0", 128 * t, 128 * t + 128), s("stb", 128 * t, 128 * t + 128))
+        TR(s("pX0", 128 * t, 128 * t + 128), s("stb", 128 * t, 128 * t + 128), t > 0)
     CP(s("sT"), s("pX0", 0, 640))
     for r in range(16):
-        MM(s("pZ2", 0, 8), s("W8", 15 - r, 143 - r, 1, 0, 8), s("th8", r, 128, 16, 0, 8), r == 0, r == 15)
+        MM(s("pZ2", 0, 8), s("W8", 15 - r, 143 - r, 1, 0, 8), s("th8", r, 128, 16, 0, 8), r == 0, r == 15, r % RUN > 0)
     for h in range(2):
         AC(s("thZ", 8 * h, 8 * h + 4), s("pZ2", 4 * h, 4 + 4 * h))
         TT(s("thb%d" % h), ind(s("thZ", 8 * h, 8 * h + 8), s("Lm", 0, 5)), s("thm"), mul)
@@ -509,33 +504,21 @@ def program():
             TS(s("yo"), s("y128"), -192.0, ad)
             add("S", lambda g, T, x: g.sync.dma_start(T.yy[:], T["yo"][:]), [s("yo")], [], "d", 2000, sem=("dyy", 16))
         back(t, 0)
-        if not X2 or CFG["OR"]:
-            back(t, 1)
-            if t < RO - 1 - X2:
-                renew(t, t & X2)
-            for h in range(2):
-                if t < RO - 1:
-                    front(t + 1, h)
-                else:
-                    finish(h)
-            continue
-        if t < RO - 1:
-            front(t + 1, 0)
-        else:
-            finish(0)
         back(t, 1)
-        if t < RO - 2:
-            renew(t, t & 1)
-        if t < RO - 1:
-            front(t + 1, 1)
-        else:
-            finish(1)
+        if t < RO - 1 - X2:
+            renew(t, t & X2)
+        for h in range(2):
+            if t < RO - 1:
+                front(t + 1, h)
+            else:
+                finish(h)
     return ops
 
 
-MODES = [(1.04, 0, 64, 0.52, 180, 170, 1300, 500, 1.5, 3.5), (1.2, 0, 64, 0.6, 130, 110, 1500, 600, 1.5, 3.5),
-         (1.04, 55, 0, 0.52, 130, 80, 1300, 500, 1.5, 3.5), (1.04, 0, 64, 0.52, 200, 120, 2600, 900, 1.5, 3.5)]
-TRY, SWEEPS, CLIMB = [(20.0, 0.0), (60.0, 0.0), (60.0, 1500.0)], 3, 2500
+MODES = [(1.04, 0, 64, 0.52, 180, 170, 1300, 500, 1.5, 3.5), (1.2, 0, 64, 0.6, 190, 180, 1800, 700, 1.8, 4.5),
+         (0.95, 0, 64, 0.48, 200, 190, 1500, 500, 1.3, 3.0)]
+TRY, SWEEPS, CLIMB = [(20.0, 0.0), (60.0, 0.0), (20.0, 1000.0), (60.0, 1500.0)], 3, 2500
+SHAKE, SPAN, NOISE = 500, 2000.0, 600.0
 
 
 def prices(ops, m):
@@ -543,9 +526,9 @@ def prices(ops, m):
     cost, lat = [], []
     for o in ops:
         k, n = o["k"], o["c"]
-        cost.append({"n": cv * max(least, fix + n), "g": (55 if o["e"] == "V" else 70) + cv * gam * n, "s": 55 + cv * sca * n,
-                     "p": pe * n, "G": 130 + 2 * cv * n, "d": 60, "r": call}[k])
-        lat.append(n if k == "d" else (n * hop + (n - 1) * call if k == "r" else 0.0))
+        cost.append(call if k == "r" else {"n": cv * max(least, fix + n), "g": (55 if o["e"] == "V" else 70) + cv * gam * n, "s": 55 + cv * sca * n,
+                                           "p": pe * n, "G": 130 + 2 * cv * n, "d": 60}[k])
+        lat.append(n if k == "d" else (n[0] * hop * (0.7 + n[1] / 1000.0) + (n[0] - 1) * call if k == "r" else 0.0))
     pred = [[(j, 0.0 if not sem else lat[j] + (ql if ops[j]["e"] == o["e"] and ops[j]["sem"] is None else xl)) for j, sem in o["d"].items()] for o in ops]
     return cost, lat, pred
 
@@ -584,13 +567,13 @@ def depend(ops):
             for x in o[kind]:
                 hs = hist.setdefault(x[0], [])
                 if x[0] in PSUM and hs and ops[hs[-1][0]]["e"] != o["e"]:
-                    hs[:] = [z for z in hs if ops[z[0]]["e"] == ops[hs[-1][0]]["e"] and z[0] >= run.get(x[0], 0)]
+                    hs[:] = [y for y in hs if ops[y[0]]["e"] == ops[hs[-1][0]]["e"] and y[0] >= run.get(x[0], 0)]
                     run[x[0]] = i
                 elif x[0] in PSUM and o["grp"]:
-                    hs[:] = [z for z in hs if z[0] < run.get(x[0], 0)]
+                    hs[:] = [y for y in hs if y[0] < run.get(x[0], 0)]
                 elif kind == "W":
-                    hs[:] = [z for z in hs if z[0] < run.get(x[0], 0) or
-                             not (x[4] <= z[2][4] and z[2][5] <= x[5] and cells(z[2]) & ~cells(x) == 0)]
+                    hs[:] = [y for y in hs if y[0] < run.get(x[0], 0) or
+                             not (x[4] <= y[2][4] and y[2][5] <= x[5] and cells(y[2]) & ~cells(x) == 0)]
                 hs.append((i, kind, x))
 
 
@@ -661,11 +644,24 @@ def schedule():
                 order, f = sweep(cost, pred, post, prio, [0.0] * n, win)
                 w = worth(order)
                 if best is None or w < best[0]:
-                    best = (w, order)
+                    best = (w, order, prio, cost, pred, post, win)
                 if it < SWEEPS - 1:
                     prio = sweep(cost, post, pred, f, tail, win)[1]
+    seed = 4321
+    for it in range(SHAKE):
+        w0, _, prio, cost, pred, post, win = best
+        seed = (seed * 1103515245 + 12345) % 2 ** 31
+        mid, p2 = max(prio) * (seed >> 8) / 2 ** 23, list(prio)
+        for i in range(n):
+            if abs(prio[i] - mid) < SPAN:
+                seed = (seed * 1103515245 + 12345) % 2 ** 31
+                p2[i] += NOISE * ((seed >> 8) / 2 ** 22 - 1.0)
+        order = sweep(cost, pred, post, p2, [0.0] * n, win)[0]
+        w = worth(order)
+        if w <= w0:
+            best = (w, order, p2, cost, pred, post, win)
 
-    top, order = best
+    top, order = best[:2]
     seed, moved = 12345, False
     for it in range(CLIMB):
         seed = (seed * 1103515245 + 12345) % 2 ** 31
@@ -754,14 +750,15 @@ def schedule():
 PLAN = []
 
 
-def route(T, topo, rank, t):
+def route(T, topo, rank, m_):
+    t = writes()[m_][1]
     src = T.cores[rank]
     dst = T.cores[(rank + 1 + t % (len(T.cores) - 1)) % len(T.cores)]
     if topo.may_write(src, dst):
         return dst, dst, topo.mask(src, dst)
-    via = [c for c in topo.cores_of(src) if c != src and topo.may_write(c, dst)]
-    via.sort(key=lambda c: (topo.die(c) != topo.die(src), c))
-    return via[0], dst, topo.mask(via[0], dst)
+    via = [c for c in topo.cores_of(src) if c != src and topo.may_write(c, dst) and topo.die(c) == topo.die(src)]
+    c = via[m_ % len(via)]
+    return c, dst, topo.mask(c, dst)
 
 
 def bits(m):
@@ -771,35 +768,36 @@ def bits(m):
 def rank_program(g, core, T, topo):
     rank = T.rank_of(core)
     N = len(T.cores)
-    if rank is None:
-        sent = 0
-        for r in range(N):
-            for t in range(RO):
-                via, dst, m = route(T, topo, r, t)
-                if via == core:
-                    rid, pid = topo.addr(dst, core)
-                    for n in (2 * t, 2 * t + 1):
-                        x = T["land"][:, PW * n:PW * n + PW]
-                        g.wait_ge(T.sem["arr%d" % n], bits(m))
-                        g.remote_dma(x, x, T.sem["arr%d" % n], T.sem.loc, pid, rid, m)
-                        sent += bits(m)
-        if sent:
-            g.wait_ge(T.sem.loc, sent)
-        return
     if not PLAN:
         PLAN.append(schedule())
     ops, order, _ = PLAN[0]
+    if rank is None:
+        sent = 0
+        for m_ in [int(ops[i]["sem"][0][3:]) for i in order if ops[i]["k"] == "r"]:
+            _, t, n, v, lo, hi = writes()[m_]
+            for r in range(N):
+                via, dst, m = route(T, topo, r, m_)
+                if via == core:
+                    rid, pid = topo.addr(dst, core)
+                    x = T["land" + v][:, n, lo:hi]
+                    g.wait_ge(T.sem["arr%d" % m_], bits(m))
+                    g.remote_dma(x, x, T.sem["arr%d" % m_], T.sem.loc, pid, rid, m)
+                    sent += bits(m)
+        if sent:
+            g.wait_ge(T.sem.loc, sent)
+        return
     sent = [0]
 
-    def send(n):
-        via, dst, m = route(T, topo, rank, n // 2)
+    def send(m_):
+        _, t, n, v, lo, hi = writes()[m_]
+        via, dst, m = route(T, topo, rank, m_)
         rid, pid = topo.addr(via, core)
-        g.remote_dma(T["land"][:, PW * n:PW * n + PW], T["pay"][:, PW * n:PW * n + PW], T.sem["arr%d" % n], T.sem.loc, pid, rid, m)
+        g.remote_dma(T["land" + v][:, n, lo:hi], T["pay" + v][:, n, lo:hi], T.sem["arr%d" % m_], T.sem.loc, pid, rid, m)
         sent[0] += bits(m)
 
-    def arrivals(n):
-        t = n // 2
-        return bits(route(T, topo, (rank - 1 - t % (N - 1)) % N, t)[2])
+    def arrivals(m_):
+        t = writes()[m_][1]
+        return bits(route(T, topo, (rank - 1 - t % (N - 1)) % N, m_)[2])
 
     Q = {"V": g.vector, "A": g.scalar, "P": g.tensor, "G": g, "S": g.sync}
     ctx = {"send": send}

from concourse.mybir import AluOpType as ALU, ActivationFunctionType as AF

F, B, I, U, H16 = "float32", "bfloat16", "int32", "uint16", "float16"
RO, PW = 5, 80
SCRATCH = {}
CFG = {"G1": "AVAAAVAA", "G2": "VAVAVAVA", "CP": "VVVV", "SG": "AAAVAAAV", "ME": "VVA", "MS": "VVVV",
       "TN": "V", "VC": "V", "X2": 0, "NZ": 4, "NX": 2, "PU": 1, "SM": 1, "VB": 1, "ML": 1, "MV": 0}
PSUM = []


def declare():
    SCRATCH.clear()
    PSUM[:] = []
    for n, w, d in [
        ("X0", 4096, B), ("X1", 4096, B), ("stb", 640, B), ("sT", 640, B), ("cin", 128, I), ("ct", 128, H16), ("cf", 128, H16),
        ("yin", 128, B), ("wb", 16, B), ("th8", 128, B), ("thZ", 16, F), ("thm", 80, F),
        ("pi", 8, I), ("pb", 8, I), ("pc", 16, F), ("iot", 160, F), ("kk8", 128, F), ("ii8", 128, F), ("kk16", 128, F),
        ("ta", 128, F), ("tb", 128, F), ("I16", 128, B), ("Pf", 160, F), ("P0", 160, H16), ("P1", 160, H16),
        ("W1", 144, B), ("WA", 144, B), ("Ww", 144, B), ("W8", 144, B), ("Wb", 128, B), ("Mx", 128, B), ("ME", 16, B),
        ("sel", 1024, B), ("kc", 128, B), ("kap", 256, F), ("d0k", 64, F), ("lo4", 72, F), ("neg", 128, B), ("zer", 128, B),
        ("c2k", 128, B), ("o16", 128, F), ("ji", 16, I), ("jf", 16, F), ("jq", 16, I), ("jk", 16, I),
        ("Lm", 16, U), ("Lk", 16, U), ("l32", 8, I), ("l32b", 8, I),
        ("ui", 8, I), ("ub", 16, I), ("uI", 40, I), ("mU", 40, F), ("oU", 40, F), ("ob", 40, F), ("cx", 8, I), ("col", 40, U),
        ("Acol", 16, F), ("cnt", 16, F), ("y128", 128, B), ("yo", 128, B), ("hx", 128, F), ("wv", 512, B),
        ("ycs", 128, F), ("pay", [2 * RO, PW], F), ("land", [2 * RO, PW], F), ("payv", [2 * RO, 64], B), ("landv", [2 * RO, 64], B),
        ("A", [8, 18], F), ("Af", [8, 18], H16), ("S", 128, F), ("H", 144, F), ("Ki", 8, I), ("oi", 8, I), ("ei", 8, I),
        ("fi", 16, I), ("ov", 8, U), ("nr", 24, F), ("TH", 16, F), ("oo", 8, F), ("mk", 256, F), ("Q", 128, F), ("ep", 128, F),
        ("tn", [8, 18], I), ("tf", [8, 18], F), ("tp", [8, 18], I), ("pf", [8, 18], F), ("dp", 128, F), ("Qp", 128, F), ("pn", 128, F), ("Ms", 128, F),
    ]:
        SCRATCH[n] = ("sbuf", [128] + (w if isinstance(w, list) else [w]), d)
    for h in "01":
        for n, w, d in [("t", 128, I), ("off", 64, U), ("xa", 1024, B), ("xT", 1024, B), ("ind", 1024, B), ("g2", 1024, B), ("ab", [4, 288], B),
                        ("vT", 128, B), ("thb", 80, B)]:
            SCRATCH[n + h] = ("sbuf", [128] + (w if isinstance(w, list) else [w]), d)
    for n, w, d in ([("pZ%d" % j, [512], F) for j in range(CFG["NZ"])] + [("pX%d" % j, [1024], B) for j in range(CFG["NX"])]
                    + [("pS", [512], F), ("pV", [8, 64], F)]):
        SCRATCH[n] = ("psum", [128] + w, d)
        PSUM.append(n)


declare()
DMAS = ["dc", "dy", "dw", "dx0", "dx1", "ds", "dt", "dyc0", "dyc1", "dyy"]


def writes():
    parts = ([("", 64, PW), ("v", 0, 64)] if CFG["VB"] else [("", 68, PW), ("", 0, 68)]) if CFG["SM"] else [("", 0, PW)]
    return [(len(parts) * n + j, n // 2, n, v, lo, hi) for n in range(2 * RO) for j, (v, lo, hi) in enumerate(parts)]


SEMAPHORES = ["nV", "nA", "nP", "nG", "loc"] + DMAS + ["arr%d" % w[0] for w in writes()]
CNT = {"V": "nV", "A": "nA", "P": "nP", "G": "nG"}
BIG = 1.0e9
RUN = 4


def s(b, lo=0, hi=None, st=1, p0=0, p1=128, sg=None):
    return (b, lo, SCRATCH[b][1][-1] if hi is None else hi, st, p0, p1, sg)


def z(b, a0, a1, lo, hi, st=1):
    return s(b, lo, hi, st, sg=(a0, a1))


def ind(w, o):
    return ("*", w, o)


def ap(T, x):
    if x[0] == "*":
        return ap(T, x[1]).indirect(ap(T, x[2]))
    b, lo, hi, st, p0, p1, sg = x
    cols = slice(lo, hi, st) if st != 1 else slice(lo, hi)
    if sg is None:
        return T[b][p0:p1, cols]
    if sg[1] - sg[0] == 1:
        return T[b][p0:p1, sg[0], cols]
    if hi - lo == 1:
        return T[b][p0:p1, sg[0]:sg[1], lo]
    return T[b][p0:p1, sg[0]:sg[1], cols]


def nel(x):
    if x[0] == "*":
        return 16 * nel(x[2])
    return (x[2] - x[1] + x[3] - 1) // x[3] * (x[6][1] - x[6][0] if x[6] else 1)


def two(*xs):
    return all(SCRATCH[x[0]][2] in (B, U, H16) for x in xs)


def program():
    ops = []
    half = [1]

    def add(eng, fn, R, W, kind, n, sem=None, grp=None, join=False):
        rr, ww = [], []
        for x in R:
            if isinstance(x, tuple):
                rr += [x[1], x[2]] if x[0] == "*" else [x]
        for x in W:
            if x[0] == "*":
                ww.append(x[1]); rr.append(x[2])
            else:
                ww.append(x)
        if join:
            o, f0 = ops[-1], ops[-1]["f"]
            o.update(f=lambda g, T, x: (f0(g, T, x), fn(g, T, x))[1], R=o["R"] + rr, W=o["W"] + ww, c=o["c"] + n)
            return
        ops.append({"e": eng, "f": fn, "R": rr, "W": ww, "k": kind, "c": n, "sem": sem, "grp": grp, "h": half[0]})

    def val(T, x):
        return ap(T, x) if isinstance(x, tuple) else x

    def vc(o, a, k):
        if a[0] == "*":
            return "g", nel(a)
        if o[0] == "*":
            return "s", nel(o)
        return "n", nel(a) * k

    def TS(o, a, s1, op0, s2=None, op1=None):
        k = 0.5 if a[0] != "*" and two(o, a) else 1
        if op1 is None:
            add("V", lambda g, T, x: g.vector.tensor_scalar(ap(T, o), ap(T, a), val(T, s1), None, op0), [a, s1], [o], *vc(o, a, k))
        else:
            add("V", lambda g, T, x: g.vector.tensor_scalar(ap(T, o), ap(T, a), val(T, s1), val(T, s2), op0, op1), [a, s1, s2], [o], *vc(o, a, k))

    def TT(o, a, b, op):
        k = 1 if (a[0] in PSUM or b[0] in PSUM) else 2
        add("V", lambda g, T, x: g.vector.tensor_tensor(ap(T, o), ap(T, a), ap(T, b), op), [a, b], [o], *vc(o, a, k))

    def CP(o, a):
        k = 0.5 if a[0] != "*" and two(o, a) else 1
        add("V", lambda g, T, x: g.vector.tensor_copy(ap(T, o), ap(T, a)), [a], [o], *vc(o, a, k))

    def MS(o, c):
        add("V", lambda g, T, x: g.vector.memset(ap(T, o), c), [], [o], "n", nel(o) * (0.5 if two(o) else 1))

    def SC(o, a, b, init, op0, op1):
        add("V", lambda g, T, x: g.vector.tensor_tensor_scan(ap(T, o), ap(T, a), ap(T, b), init, op0, op1), [a, b], [o], "n", nel(o))

    def VT(o, a):
        add("V", lambda g, T, x: g.vector.transpose(ap(T, o), ap(T, a)), [a], [o], "n", nel(o))

    def AC(o, a, fn=AF.Identity, bias=0.0, scale=1.0, acc=None):
        k = "g" if a[0] == "*" else "n"
        if acc is None:
            add("A", lambda g, T, x: g.scalar.activation(ap(T, o), ap(T, a), fn, bias=val(T, bias), scale=val(T, scale)), [a, bias, scale], [o], k, nel(a))
        else:
            add("A", lambda g, T, x: g.scalar.activation(ap(T, o), ap(T, a), fn, bias=val(T, bias), scale=val(T, scale), accum_out=ap(T, acc)),
                [a, bias, scale], [o, acc], k, max(64, nel(a)) + 20)

    def MM(o, l, r, start, stop, join=False):
        c = max(min(64, nel(l)), nel(r)) * (4 if SCRATCH[l[0]][2] == F else 1)
        add("P", lambda g, T, x: g.tensor.matmul(ap(T, o), ap(T, l), ap(T, r), start, stop), [l, r], [o], "p", c, grp=True, join=join)

    def TR(o, a, join=False):
        add("P", lambda g, T, x: g.tensor.transpose(ap(T, o), ap(T, a), ap(T, s("I16"))), [a, s("I16")], [o], "p", 128, grp=True, join=join)

    def IO(o, pat, base, cm):
        if SCRATCH[o[0]][2] == I:
            add("G", lambda g, T, x: g.iota(ap(T, o), pat, base, cm), [], [o], "G", nel(o))
        else:
            add("G", lambda g, T, x: g.iota(ap(T, o), pat, base, cm, allow_small_or_imprecise_dtypes=True), [], [o], "G", nel(o))

    def LD(q, o, name, sem, lat, after=()):
        if q == "S":
            add(q, lambda g, T, x: g.sync.dma_start(ap(T, o), T[name][:]), list(after), [o], "d", lat, sem=(sem, 16))
        else:
            add(q, lambda g, T, x: g.scalar.dma_start(ap(T, o), T[name][:]), list(after), [o], "d", lat, sem=(sem, 16))

    def col(b, j, n=None):
        return s(b, j, j + 1) if n is None else z(b, n, n + 1, j, j + 1)

    mul, ad, sub, mx, mn = ALU.mult, ALU.add, ALU.subtract, ALU.max, ALU.min
    band, shr = ALU.bitwise_and, ALU.logical_shift_right
    I32 = s("Pf", 16, 144)
    X2, MV = CFG["X2"], CFG["MV"]
    turn = {"Z": -1, "X": -1}

    def nxt(k):
        turn[k] += 1
        return "p%s%d" % (k, turn[k] % CFG["N" + k])

    LD("A", s("X0"), "x0", "dx0", 5000)
    LD("S", s("cin"), "c0", "dc", 2300)
    LD("S", s("yin"), "y0", "dy", 2300)
    LD("S", s("wb", 0, 1), "w", "dw", 2300)
    LD("S", s("stb"), "st", "ds", 3000)
    LD("S", s("th8", p1=8), "th", "dt", 2500)
    if X2:
        LD("S", s("X1"), "x0", "dx1", 4500, after=[s("X0")])
    IO(col("pi", 0), [[0, 1]], 0, 1)
    IO(s("iot"), [[1, 160]], 0, 0)
    TS(col("pb", 0), col("pi", 0), 4, shr)
    TS(col("pb", 1), col("pi", 0), 15, band)
    TS(col("pb", 2), col("pi", 0), 3, shr)
    TS(col("pb", 3), col("pi", 0), 7, band)
    TS(col("pb", 4), col("pi", 0), 4, shr, 1, band)
    for j, (b, k, m_, a_) in enumerate([("pi", 0, 1, 0), ("pi", 0, 1, 16), ("pb", 0, 1, 0), ("pb", 0, 16, 15), ("pb", 1, 1, 2032), ("pb", 2, 1, 0),
                                        ("pb", 3, 1, 0), ("pb", 4, 1, 0), ("pb", 4, -1, 1), ("pb", 2, -1, 16), ("pi", 0, 16, 15), ("pb", 0, -16, 0),
                                        ("pb", 0, -512, 0)]):
        TS(col("pc", j), col(b, k), float(m_), mul, float(a_), ad)
    eq = ALU.is_equal
    TS(s("P0"), s("iot"), col("pc", 1), eq, col("pc", 8), mul)
    TS(s("P1"), s("iot"), col("pc", 1), eq, col("pc", 7), mul)
    TS(s("Pf"), s("iot"), col("pc", 1), eq)
    TS(s("I16"), s("iot", 0, 128), col("pc", 0), eq)
    CP(col("pc", 13), col("wb", 0))
    TS(s("Ww"), s("iot", 0, 144), col("pc", 3), eq, col("pc", 13), mul)
    TS(s("W1"), s("iot", 0, 144), col("pc", 3), eq)
    TS(s("WA"), s("iot", 0, 144), col("pc", 3), eq, float(2 ** 18), mul)
    TS(s("W8"), s("iot", 0, 144), col("pc", 10), eq)
    MS(s("zer"), 0.0)
    MS(s("neg"), -192.0)
    MS(s("c2k"), 4.0)
    MS(s("o16"), 16.0)
    IO(s("kk8"), [[1, 16], [0, 8]], 0, 0)
    IO(s("ii8"), [[0, 16], [1, 8]], 0, 0)
    TS(s("ta"), s("kk8"), col("pc", 5), eq, col("pc", 5), mul)
    TS(s("tb"), s("kk8"), col("pc", 5), ALU.is_gt, col("pc", 9), sub)
    TT(s("ta"), s("ta"), s("tb"), sub)
    TS(s("tb"), s("ii8"), col("pc", 6), eq, 0.125, mul)
    TT(s("Mx"), s("ta"), s("tb"), mul)
    TS(s("ME", 0, 8), s("Mx", 0, 8), 1.0 / 32, mul)
    MS(s("sel"), -1.0)
    for h in range(2):
        x_ = s("sel", p0=64 * h, p1=64 * h + 64)
        add("G", lambda g, T, x, x_=x_: g.affine_select(ap(T, x_), ap(T, x_), [[-16, 4], [0, 16], [-1, 16]], eq, 0.0, 0, 1), [x_], [x_], "G", 1040)
    IO(s("kc", p1=32), [[0, 2], [-32, 64]], 2016, 0)
    IO(s("kc", p0=32, p1=64), [[0, 128]], 2064, 0)
    MS(s("kc", p0=96), 0.0)
    MS(s("kc", p0=64, p1=96), float(2 ** 15))
    for c in range(8):
        if CFG["SG"][c] == "V":
            MS(s("kc", 16 * c, 16 * c + 16, 1, 64, 96), 0.0)
    nh = 2 if MV else 1
    IO(s("kap", 0, 64 * nh), [[0, nh], [-16, 64]], 2032, 0)
    IO(s("kap", 64 * nh, 128 * nh), [[0, nh], [-16, 64]], -2063, 0)
    IO(s("kk16"), [[1, 8], [0, 16]], 0, 0)
    TS(s("Wb"), s("kk16"), col("pc", 2), eq, col("pc", 13), mul)
    MS(s("d0k"), BIG)
    MS(s("d0k", 0, 64, 16), -BIG)
    MS(s("d0k", 1, 64, 16), -BIG)
    MS(s("lo4"), 0.0)
    MS(s("lo4", 0, 72, 18), 1.0)
    MS(s("lo4", 17, 72, 18), -BIG)
    MS(s("thm"), -1.0)
    MS(s("thm", 17, 72, 18), 0.0)
    MS(s("thZ"), 0.0)
    IO(s("ji", 0, 6), [[16, 6]], 0, 1)
    TS(s("jf", 0, 6), s("ji", 0, 6), col("pc", 11), ad)
    TS(s("jq", 0, 6), s("jf", 0, 6), 1.0 / 18, mul, -0.47, ad)
    CP(s("Lm", 0, 6), s("jq", 0, 6))
    IO(s("jk"), [[1, 16]] if MV else [[4, 2], [8, 2], [1, 4]], 0, 0)
    CP(s("Lk"), s("jk"))
    MS(s("TH"), 0.0)
    IO(s("l32b"), [[512, 8]], 0, 32)
    TS(s("l32"), s("l32b"), col("pc", 12), ad)
    MS(z("pV", 0, 8, 0, 18, 17), 0.0)
    for h in "01":
        MS(z("ab" + h, 0, 4, 0, 16), 0.0)
        MS(z("ab" + h, 0, 4, 272, 288), 0.0)
    TS(s("cf"), s("cin"), -2048.0, ad)
    VT(s("ct"), s("cf"))
    for h in range(2):
        ps = "pZ%d" % h
        MM(s(ps, 0, 64), s("zer"), s("zer", 0, 64), True, False)
        for c in range(4):
            for g2 in range(2):
                o_ = 16 + 16 * (c & 1) - 16 * g2
                k0 = 32 * (2 * h + (c >> 1)) + 16 * g2
                MM(s(ps, 16 * c, 16 * c + 16), s("P%d" % (c & 1), o_, o_ + 128), s("ct", k0, k0 + 16), False, c == 3 and g2 == 1, True)
        AC(z("A", 4 * h, 4 * h + 4, 1, 17), s(ps, 0, 64))

    def sums(t, ysrc):
        a, b = 8 * t, 8 * t + 8
        pu = s("pS", 400, 408)
        if t > 0:
            MM(pu, s("Wb"), s("neg", 0, 8), True, False)
        for r in range(16):
            MM(pu, s("Ww", 15 - r, 143 - r), s(ysrc, r, 128, 16), t == 0 and r == 0, r == 15, r % RUN > 0)
        CP(s("ui"), pu)
        TS(s("uI", a, b), s("ui"), 2047, band)
        TS(s("mU", a, b), s("uI", a, b), 2.0, mul, 33.0, ad)
        if t == 0:
            AC(s("oU", a, b), s("mU", a, b), scale=2048.0, bias=-float(2 ** 22))
        else:
            MM(s("pS", 408, 410), s("o16"), s("cnt", 2 * t - 2, 2 * t), True, True)
            AC(s("Acol", 8, 10), s("pS", 408, 410), bias=float(8192 - 2 ** 21), acc=col("Acol", t))
            AC(s("oU", a, b), s("mU", a, b), scale=2048.0, bias=col("Acol", t))
        TS(s("ub", 0, 8), s("ui"), 1, band)
        TS(s("ob", a, b), s("ub", 0, 8), 1024.0, mul, 4096.0, ad)
        if t < RO - 1:
            TS(s("ub", 8, 16), s("ui"), 31, band)
            TT(s("cx"), s("ub", 8, 16), s("l32"), ad)
            CP(s("col", a, b), s("cx"))

    def renew(t, into):
        TT(ind(s("X%d" % into), s("col", 8 * t, 8 * t + 8)), s("wv", 128 * t, 128 * t + 128), s("neg"), ad)

    def places(h, m, o):
        H = str(h)
        for c in range(4):
            TS(s("t" + H, 16 * c, 16 * c + 16), z("A", 4 * h + c, 4 * h + c + 1, 1, 17), m(c), mul, o(c), ad)
        TS(s("t" + H, 64, 128), s("t" + H, 0, 64), 0x1FFFF, band, 5, shr)
        CP(s("off" + H), s("t" + H, 64, 128))

    def gather(h, t, out, plan):
        for c in range(4):
            e = plan[4 * h + c]
            if e in "VA":
                c1 = c + 1
                while c1 < 4 and plan[4 * h + c1] not in "VA":
                    c1 += 1
                (CP if e == "V" else AC)(s(out, 256 * c, 256 * c1), ind(s("X%d" % (t & X2)), s("off%d" % h, 16 * c, 16 * c1)))

    def total(h):
        for ch in range(8):
            c, b = ch >> 1, ch & 1
            MM(s("pS", 272 + 64 * h + 16 * c + b, 288 + 64 * h + 16 * c, 2), s("xT%d" % h, 128 * ch, 128 * ch + 128), s("ME", 0, 8), True, True, ch % RUN > 0)

    def front(t, h):
        H = str(h); u0 = 8 * t + 4 * h; n = 2 * t + h; a0, a1 = 4 * h, 4 * h + 4
        half[0] = 1 - h
        if t == 0 or not CFG["PU"]:
            places(h, lambda c: col("mU", u0 + c), lambda c: col("oU", u0 + c))
        gather(h, t, "xa" + H, CFG["G1"])
        for c in range(4):
            px, w, pb = nxt("X"), 256 * c, nxt("Z")
            MM(s(pb, 0, 256), s("sT", 128 * t, 128 * t + 128, 1, 64 * h, 64 * h + 64), s("sel", w, w + 256, 1, 64 * h, 64 * h + 64), True, False)
            for b in range(2):
                TR(s(px, w + 128 * b, w + 128 * b + 128), s("xa" + H, w + b, w + 256, 2), b == 1)
            (CP if CFG["CP"][c] == "V" else AC)(s("xT" + H, w, w + 256), s(px, w, w + 256))
            for b in range(2):
                MM(s(pb, b, 256, 2), s("xT" + H, w + 128 * b, w + 128 * b + 128), s("Mx"), False, b == 1, b == 1)
            if CFG["SG"][a0 + c] == "V":
                TS(s("ind" + H, w, w + 256), s(pb, 0, 256), 0.0, ALU.is_ge, 2.0, mul)
            else:
                AC(s("ind" + H, w, w + 256), s(pb, 0, 256), AF.Sign, bias=0.0625)
        if CFG["ML"] == 0:
            total(h)
        pk = s("pS", 64 * h, 64 * h + 64)
        MM(pk, I32, z("A", a0, a1, 1, 17), True, False)
        MM(pk, s("c2k"), s("kc", 64 * h, 64 * h + 64), False, False, True)
        for r in range(16):
            MM(pk, s("WA", 15 - r, 143 - r), s("ind" + H, r, 1024, 16), False, r == 15, r % RUN > 0)
        SC(s("S", 64 * h, 64 * h + 64), s("d0k"), pk, -BIG, mn, mx)
        if CFG["ML"] == 1:
            total(h)
        if CFG["ML"] == 2 and h == 1:
            total(0)
            total(1)
        K0, KS = s("S", 64 * h, 64 * h + 64, 16), s("S", 64 * h + 15, 64 * h + 64, 16)
        q = lambda b, j=0: s(b, j + a0, j + a1)
        CP(q("Ki"), KS)
        TS(q("oi"), q("Ki"), 8, shr, 0x7F0, band)
        TS(q("ov"), q("oi"), -1.0, mul, col("pc", 4), ad)
        AC(z("payv" if CFG["VB"] else "pay", n, n + 1, 0, 64), ind(s("xa" + H), q("ov")))
        TS(q("ei"), q("Ki"), 4095, band)
        gs, ee, me, oe = [z("pay", n, n + 1, 64 + 4 * j, 68 + 4 * j) for j in range(4)]
        TS(me, q("ei"), 32.0, ad)
        if CFG["ME"][1] == "V":
            TS(ee, q("ei"), -2048.0, ad)
        else:
            AC(ee, me, bias=-2080.0)
        if CFG["ME"][2] == "V":
            TS(oe, q("ei"), -2048.0, ad, 3232.0, mul)
        else:
            AC(oe, me, scale=3232.0, bias=-3232.0 * 2080)
        AC(q("nr"), K0, AF.Relu, scale=-65536.0, bias=float(9 * 2 ** 35))
        TT(q("nr", 8), K0, KS, sub)
        TT(q("nr", 16), q("nr"), q("nr", 8), mul)
        if t < RO - 1:
            AC(gs, q("nr", 16), AF.Sign, bias=-1.0, acc=col("cnt", n))
        else:
            AC(gs, q("nr", 16), AF.Sign, bias=-1.0)
        for m_, t_, n_, v, lo, hi in writes():
            if n_ == n:
                add("G", lambda g, T, x, m_=m_: x["send"](m_), [z("pay" + v, n, n + 1, lo, hi)], [z("land" + v, n, n + 1, lo, hi)], "r",
                    (1 if t & 1 else 2, (hi - lo) * (2 if v else 4)), sem=("arr%d" % m_, 0))
        if h == 0 and t < RO - 1:
            AC(s("hx"), ind(s("X%d" % (t & X2)), s("col", 8 * t, 8 * t + 8)), scale=0.5, bias=192.0 - 255.0 / 512)
        if h == 1:
            pe = s("pS", 272, 400)
            AC(s("y128"), pe, scale=8.0, bias=192.0 - 31.0 / 64)
            if t < RO - 1:
                TT(s("wv", 128 * t, 128 * t + 128), s("hx"), pe, ad)
        if not MV:
            moves(t, h, h + 1)
        elif h == 1:
            moves(t, 0, 2)

    def moves(t, h0, h1):
        a0, a1 = 4 * h0, 4 * h1
        w, m0 = 16 * (a1 - a0), 128 * h0
        me = z("pay", 2 * t + h0, 2 * t + h1, 72, 76)
        q = lambda b, j=0: s(b, j + a0, j + a1)
        AC(z("A", a0, a1, 0, 1), me, bias=-2080.0)
        TT(q("fi"), me, s("uI", 8 * t + a0, 8 * t + a1), mul)
        TS(q("fi", 8), q("fi"), 0x1FFFF, band, 5, shr)
        TS(z("A", a0, a1, 17, 18), q("fi", 8), -2048.0, ad)
        TT(q("TH"), q("oi"), q("nr", 16), mn)
        TT(q("oo"), q("oi"), s("ob", 8 * t + a0, 8 * t + a1), sub)
        TT(q("TH", 8), q("oo"), q("nr", 16), mx)
        TT(s("mk", m0, m0 + 2 * w), ind(s("TH"), s("Lk", 2 * a0, 2 * a1)), s("kap", 0, 2 * w), ALU.is_ge)
        TT(z("pV", a0, a1, 34, 51), z("A", a0, a1, 1, 18), z("A", a0, a1, 0, 17), sub)
        TT(z("pV", a0, a1, 1, 17), s("mk", m0 + w, m0 + 2 * w), z("pV", a0, a1, 34, 50), mul)
        TT(z("pV", a0, a1, 18, 34), s("mk", m0, m0 + w), z("pV", a0, a1, 35, 51), mul)
        TT(s("Q", 16 * a0, 16 * a1), z("A", a0, a1, 0, 16), z("pV", a0, a1, 1, 17), ad)
        TT(z("A", a0, a1, 1, 17), s("Q", 16 * a0, 16 * a1), z("pV", a0, a1, 18, 34), ad)

    def back(t, h):
        H = str(h); n = 2 * t + h; a0, a1 = 4 * h, 4 * h + 4
        half[0] = 1 - h
        q = lambda b: s(b, 64 * h, 64 * h + 64)
        places(h, lambda c: col("land", 72 + c, n), lambda c: col("land", 76 + c, n))
        AC(z("A", a0, a1, 0, 1), z("land", n, n + 1, 68, 72))
        ahead = CFG["PU"] and t < RO - 1
        if ahead:
            u1 = 8 * (t + 1) + a0
            for c in range(4):
                a_ = z("A", a0 + c, a0 + c + 1, 0, 17)
                if CFG["TN"] == "V":
                    TS(z("tn", a0 + c, a0 + c + 1, 0, 17), a_, col("mU", u1 + c), mul, col("oU", u1 + c), ad)
                else:
                    AC(z("tf", a0 + c, a0 + c + 1, 0, 17), a_, scale=col("mU", u1 + c), bias=col("oU", u1 + c))
            if CFG["TN"] != "V":
                CP(z("tn", a0, a1, 0, 17), z("tf", a0, a1, 0, 17))
            TS(z("tp", a0, a1, 0, 17), z("tn", a0, a1, 0, 17), 0x1FFFF, band, 5, shr)
            CP(z("pf", a0, a1, 0, 17), z("tp", a0, a1, 0, 17))
            for c in range(a0, a1):
                AC(s("dp", 16 * c, 16 * c + 16), z("pf", c, c + 1, 1, 17), scale=-1.0, bias=col("pf", 0, c))
        pbs = [nxt("Z") for c in range(4)]
        if CFG["VB"]:
            pv = s(nxt("X"), 0, 128, 1, 0, 64)
            TR(pv, z("landv", n, n + 1, 0, 64))
        else:
            pv = s(pbs[0], 0, 128, 1, 0, 64)
            MM(pv, z("land", n, n + 1, 0, 64), I32, True, True)
        (AC if CFG["VC"] == "A" else CP)(s("vT" + H, p1=64), pv)
        gather(h, t, "g2" + H, CFG["G2"])
        for c in range(4):
            AC(s("ep", 64 * h + 16 * c, 64 * h + 16 * c + 16), z("A", a0 + c, a0 + c + 1, 1, 17), scale=-1.0, bias=col("land", 68 + c, n))
        for c in range(4):
            o_, w = s(pbs[c], 0, 256), 256 * c
            MM(o_, s("vT" + H, p1=64), s("sel", w, w + 256, 1, 0, 64), True, False)
            MM(o_, s("I16"), s("g2" + H, w, w + 256), False, True)
            AC(z("ab" + H, c, c + 1, 16, 272), o_, AF.Abs)
        d0 = 128 + 72 * h
        pd = s("pS", d0, d0 + 72)
        MM(pd, s("I16"), s("thb" + H, 0, 72), True, False)
        MM(s("pS", d0 + 17, d0 + 72, 18), I32, z("land", n, n + 1, 64, 68), False, False)
        for r in range(16):
            MM(pd, s("W1", 15 - r, 143 - r), z("ab" + H, 0, 4, r, 288, 16), False, r == 15, r % RUN > 0)
        SC(s("H", 72 * h, 72 * h + 72), pd, s("lo4"), 1.0, mn, mx)
        inp = "A" not in CFG["MS"]
        for c in range(a0, a1):
            o_ = z("pV", c, c + 1, 34, 50) if inp else s("Ms", 16 * c, 16 * c + 16)
            if CFG["MS"][c - a0] == "V":
                TS(o_, s("H", 18 * c, 18 * c + 16), col("H", 18 * c + 17), ALU.is_gt, -1.0, mul)
            else:
                AC(o_, s("H", 18 * c, 18 * c + 16), AF.Sign, scale=-1.0, bias=col("H", 18 * c + 17))
        ms = z("pV", a0, a1, 34, 50) if inp else q("Ms")
        if ahead:
            TT(z("pV", a0, a1, 1, 17), ms, q("dp"), mul)
            TT(q("Qp"), z("pf", a0, a1, 0, 16), z("pV", a0, a1, 1, 17), ad)
            TT(q("pn"), q("Qp"), z("pV", a0, a1, 0, 16), sub)
            CP(s("off" + H), q("pn"))
        TT(z("pV", a0, a1, 18, 34), ms, q("ep"), mul)
        TT(q("Q"), z("A", a0, a1, 0, 16), z("pV", a0, a1, 18, 34), ad)
        TT(z("A" if t < RO - 1 else "Af", a0, a1, 1, 17), q("Q"), z("pV", a0, a1, 17, 33), sub)

    def finish(h):
        H = str(h); ps = nxt("Z")
        MM(s(ps, 0, 64), s("c2k"), s("c2k", 0, 64), True, False)
        for cp in range(2):
            for g2 in range(2):
                for c2 in range(2):
                    o_ = 16 + 16 * g2 - 16 * c2; c = 4 * h + 2 * cp + c2; w = 32 * cp + 16 * g2
                    MM(s(ps, w, w + 16), s("P%d" % g2, o_, o_ + 128), z("Af", c, c + 1, 1, 17), False, cp + g2 + c2 == 3, cp + g2 + c2 > 0)
        VT(s("ycs", 64 * h, 64 * h + 64), s(ps, 0, 64))
        x_ = s("ycs", 64 * h, 64 * h + 64)
        add("S", lambda g, T, x: g.sync.dma_start(T.yc[:, 64 * h:64 * h + 64], ap(T, x_)), [x_], [], "d", 2000, sem=("dyc" + H, 16))

    sums(0, "yin")
    for t in range(RO):
        TR(s("pX0", 128 * t, 128 * t + 128), s("stb", 128 * t, 128 * t + 128), t > 0)
    CP(s("sT"), s("pX0", 0, 640))
    for r in range(16):
        MM(s("pZ2", 0, 8), s("W8", 15 - r, 143 - r, 1, 0, 8), s("th8", r, 128, 16, 0, 8), r == 0, r == 15, r % RUN > 0)
    for h in range(2):
        AC(s("thZ", 8 * h, 8 * h + 4), s("pZ2", 4 * h, 4 + 4 * h))
        TT(s("thb%d" % h), ind(s("thZ", 8 * h, 8 * h + 8), s("Lm", 0, 5)), s("thm"), mul)
    front(0, 0)
    front(0, 1)
    for t in range(RO):
        if t < RO - 1:
            sums(t + 1, "y128")
            if X2:
                renew(t, (t + 1) & 1)
        else:
            TS(s("yo"), s("y128"), -192.0, ad)
            add("S", lambda g, T, x: g.sync.dma_start(T.yy[:], T["yo"][:]), [s("yo")], [], "d", 2000, sem=("dyy", 16))
        back(t, 0)
        back(t, 1)
        if t < RO - 1 - X2:
            renew(t, t & X2)
        for h in range(2):
            if t < RO - 1:
                front(t + 1, h)
            else:
                finish(h)
    return ops


MODES = [(1.04, 0, 64, 0.52, 180, 170, 1300, 500, 1.5, 3.5), (1.2, 0, 64, 0.6, 190, 180, 1800, 700, 1.8, 4.5),
         (0.95, 0, 64, 0.48, 200, 190, 1500, 500, 1.3, 3.0)]
TRY, SWEEPS, CLIMB = [(20.0, 0.0), (60.0, 0.0), (20.0, 1000.0), (60.0, 1500.0)], 3, 2500
SHAKE, SPAN, NOISE = 500, 2000.0, 600.0


def prices(ops, m):
    cv, fix, least, pe, xl, ql, hop, call, gam, sca = m
    cost, lat = [], []
    for o in ops:
        k, n = o["k"], o["c"]
        cost.append(call if k == "r" else {"n": cv * max(least, fix + n), "g": (55 if o["e"] == "V" else 70) + cv * gam * n, "s": 55 + cv * sca * n,
                                           "p": pe * n, "G": 130 + 2 * cv * n, "d": 60}[k])
        lat.append(n if k == "d" else (n[0] * hop * (0.7 + n[1] / 1000.0) + (n[0] - 1) * call if k == "r" else 0.0))
    pred = [[(j, 0.0 if not sem else lat[j] + (ql if ops[j]["e"] == o["e"] and ops[j]["sem"] is None else xl)) for j, sem in o["d"].items()] for o in ops]
    return cost, lat, pred


def cells(x, memo={}):
    if x not in memo:
        m = 0
        for c in range(*(x[6] or (0, 1))):
            for j in range(x[1], x[2], x[3]):
                m |= 1 << (c * SCRATCH[x[0]][1][-1] + j)
        memo[x] = m
    return memo[x]


def meets(a, b):
    return a[4] < b[5] and b[4] < a[5] and cells(a) & cells(b) != 0


def depend(ops):
    hist, run = {}, {}
    for i, o in enumerate(ops):
        dep = {}
        for kind in "RW":
            for x in o[kind]:
                for j, k2, y in hist.get(x[0], []):
                    p = ops[j]
                    same = p["e"] == o["e"] and p["sem"] is None and o["sem"] is None
                    if x[0] in PSUM and not same:
                        dep[j] = True
                    elif x[0] in PSUM and o["grp"]:
                        dep.setdefault(j, False)
                    elif (kind == "W" or k2 == "W") and meets(x, y):
                        dep[j] = True
        o["d"] = dep
        for kind in "RW":
            for x in o[kind]:
                hs = hist.setdefault(x[0], [])
                if x[0] in PSUM and hs and ops[hs[-1][0]]["e"] != o["e"]:
                    hs[:] = [y for y in hs if ops[y[0]]["e"] == ops[hs[-1][0]]["e"] and y[0] >= run.get(x[0], 0)]
                    run[x[0]] = i
                elif x[0] in PSUM and o["grp"]:
                    hs[:] = [y for y in hs if y[0] < run.get(x[0], 0)]
                elif kind == "W":
                    hs[:] = [y for y in hs if y[0] < run.get(x[0], 0) or
                             not (x[4] <= y[2][4] and y[2][5] <= x[5] and cells(y[2]) & ~cells(x) == 0)]
                hs.append((i, kind, x))


def schedule():
    ops = program()
    n = len(ops)
    depend(ops)
    price = [prices(ops, m) for m in MODES]
    eng = [o["e"] for o in ops]
    succ = [[] for _ in ops]
    for i, o in enumerate(ops):
        for j in o["d"]:
            succ[j].append(i)
    ends = [i for i in range(n) if not succ[i]]

    def replay(order, m, fin):
        cost, lat, pred = price[m]
        free = {e: 0.0 for e in "VAPGS"}
        for i in order:
            e = eng[i]
            st = free[e]
            for j, d in pred[i]:
                x = fin[j] + d
                if x > st:
                    st = x
            fin[i] = free[e] = st + cost[i]
        return max(fin[i] + lat[i] for i in ends)

    fin = [0.0] * n

    def worth(order):
        return sum(replay(order, m, fin) for m in range(len(MODES)))

    def sweep(cost, before, after, prio, first, win):
        left = [len(b) for b in before]
        ready = {e: {} for e in "VAPGS"}
        for i in range(n):
            if left[i] == 0:
                ready[eng[i]][i] = first[i]
        free = {e: 0.0 for e in "VAPGS"}
        f = [0.0] * n
        order = []
        while len(order) < n:
            t0, e0 = min((max(min(r.values()), free[e]), e) for e, r in ready.items() if r)
            i = max((i for i, r in ready[e0].items() if r <= t0 + win), key=lambda i: (prio[i], -i))
            f[i] = max(ready[e0].pop(i), free[e0]) + cost[i]
            free[e0] = f[i]
            order.append(i)
            for k, _ in after[i]:
                left[k] -= 1
                if left[k] == 0:
                    ready[eng[k]][k] = max([first[k]] + [f[j] + d for j, d in before[k]])
        return order, f

    best = None
    for cost, lat, pred in price:
        post = [[] for _ in ops]
        for i in range(n):
            for j, d in pred[i]:
                post[j].append((i, d))
        level = [0.0] * n
        for i in range(n - 1, -1, -1):
            level[i] = cost[i] + max([d + level[k] for k, d in post[i]] + [lat[i]])
        tail = [lat[i] if not succ[i] else 0.0 for i in range(n)]
        for win, bias in TRY:
            prio = [level[i] + bias * ops[i]["h"] for i in range(n)]
            for it in range(SWEEPS):
                order, f = sweep(cost, pred, post, prio, [0.0] * n, win)
                w = worth(order)
                if best is None or w < best[0]:
                    best = (w, order, prio, cost, pred, post, win)
                if it < SWEEPS - 1:
                    prio = sweep(cost, post, pred, f, tail, win)[1]
    seed = 4321
    for it in range(SHAKE):
        w0, _, prio, cost, pred, post, win = best
        seed = (seed * 1103515245 + 12345) % 2 ** 31
        mid, p2 = max(prio) * (seed >> 8) / 2 ** 23, list(prio)
        for i in range(n):
            if abs(prio[i] - mid) < SPAN:
                seed = (seed * 1103515245 + 12345) % 2 ** 31
                p2[i] += NOISE * ((seed >> 8) / 2 ** 22 - 1.0)
        order = sweep(cost, pred, post, p2, [0.0] * n, win)[0]
        w = worth(order)
        if w <= w0:
            best = (w, order, p2, cost, pred, post, win)

    top, order = best[:2]
    seed, moved = 12345, False
    for it in range(CLIMB):
        seed = (seed * 1103515245 + 12345) % 2 ** 31
        if it == 0 or moved or it % 40 == 0:
            cost, lat, pred = price[(seed >> 10) % len(MODES)]
            at, lastq, f, why = {}, {}, [0.0] * n, [None] * n
            for p, i in enumerate(order):
                at[i] = p
                q = lastq.get(eng[i])
                st, why[i] = (f[q], (q, True)) if q is not None else (0.0, None)
                for j, d in pred[i]:
                    if f[j] + d >= st:
                        st, why[i] = f[j] + d, (j, False)
                f[i] = st + cost[i]
                lastq[eng[i]] = i
            i = max(ends, key=lambda i: f[i] + lat[i])
            arcs = []
            while why[i] is not None:
                if why[i][1]:
                    arcs.append((why[i][0], i))
                i = why[i][0]
            byq = {e: [i for i in order if eng[i] == e] for e in "VAPGS"}
        moved = False
        a, b = arcs[(seed >> 8) % len(arcs)]
        qa = byq[eng[a]]
        pa = qa.index(a)
        first = qa[max(0, pa - (0, 0, 1, 2, 3, 5)[(seed >> 20) % 6])]
        late = set(i for i in qa[qa.index(first):pa + 1])
        keep, push = [], []
        for i in order[at[first]:at[b] + 1]:
            if i in late or any(j in late for j in ops[i]["d"]):
                late.add(i); push.append(i)
            else:
                keep.append(i)
        if b in late:
            continue
        o2 = order[:at[first]] + keep + push + order[at[b] + 1:]
        w = worth(o2)
        if w <= top:
            top, order, moved = w, o2, True
    times = [replay(order, m, fin) for m in range(len(MODES) - 1, -1, -1)][::-1]
    cost, lat, pred = price[0]
    for i in order:
        ops[i]["t"] = fin[i] - cost[i]
    pos, seen = {}, {e: 0 for e in "VAPGS"}
    for i in order:
        if ops[i]["sem"] is None:
            seen[ops[i]["e"]] += 1
            pos[i] = (ops[i]["e"], seen[ops[i]["e"]])
        else:
            pos[i] = (ops[i]["sem"][0], 1)
    know = {e: {} for e in "VAPGS"}
    clock = {}
    need = set()
    lastg = []
    for i in order:
        o = ops[i]; kn = know[o["e"]]
        want = {}
        if o["e"] == "G" and o["sem"] is None:
            if lastg:
                want["G"] = (pos[lastg[-1]][1], lastg[-1])
            lastg.append(i)
        for j, sem in o["d"].items():
            if sem and pos[j][1] > want.get(pos[j][0], (0, 0))[0]:
                want[pos[j][0]] = (pos[j][1], j)
        o["w"] = []
        for key, (v, j) in sorted(want.items(), key=lambda kv: -fin[kv[1][1]] - lat[kv[1][1]]):
            if kn.get(key, 0) < v:
                o["w"].append(j); need.add(j)
                for k2, v2 in clock[j].items():
                    if kn.get(k2, 0) < v2:
                        kn[k2] = v2
        ck = {} if o["sem"] is not None and o["sem"][1] == 0 else dict(kn)
        ck[pos[i][0]] = pos[i][1]
        clock[i] = ck
    count = {e: 0 for e in CNT}
    for i in order:
        if ops[i]["sem"] is None and i in need:
            count[ops[i]["e"]] += 1
            ops[i]["n"] = count[ops[i]["e"]]
        else:
            ops[i]["n"] = 0
    return ops, order, times


PLAN = []


def route(T, topo, rank, m_):
    t = writes()[m_][1]
    src = T.cores[rank]
    dst = T.cores[(rank + 1 + t % (len(T.cores) - 1)) % len(T.cores)]
    if topo.may_write(src, dst):
        return dst, dst, topo.mask(src, dst)
    via = [c for c in topo.cores_of(src) if c != src and topo.may_write(c, dst) and topo.die(c) == topo.die(src)]
    c = via[m_ % len(via)]
    return c, dst, topo.mask(c, dst)


def bits(m):
    return bin(m).count("1")


def rank_program(g, core, T, topo):
    rank = T.rank_of(core)
    N = len(T.cores)
    if not PLAN:
        PLAN.append(schedule())
    ops, order, _ = PLAN[0]
    if rank is None:
        sent = 0
        for m_ in [int(ops[i]["sem"][0][3:]) for i in order if ops[i]["k"] == "r"]:
            _, t, n, v, lo, hi = writes()[m_]
            for r in range(N):
                via, dst, m = route(T, topo, r, m_)
                if via == core:
                    rid, pid = topo.addr(dst, core)
                    x = T["land" + v][:, n, lo:hi]
                    g.wait_ge(T.sem["arr%d" % m_], bits(m))
                    g.remote_dma(x, x, T.sem["arr%d" % m_], T.sem.loc, pid, rid, m)
                    sent += bits(m)
        if sent:
            g.wait_ge(T.sem.loc, sent)
        return
    sent = [0]

    def send(m_):
        _, t, n, v, lo, hi = writes()[m_]
        via, dst, m = route(T, topo, rank, m_)
        rid, pid = topo.addr(via, core)
        g.remote_dma(T["land" + v][:, n, lo:hi], T["pay" + v][:, n, lo:hi], T.sem["arr%d" % m_], T.sem.loc, pid, rid, m)
        sent[0] += bits(m)

    def arrivals(m_):
        t = writes()[m_][1]
        return bits(route(T, topo, (rank - 1 - t % (N - 1)) % N, m_)[2])

    Q = {"V": g.vector, "A": g.scalar, "P": g.tensor, "G": g, "S": g.sync}
    ctx = {"send": send}
    for i in order:
        o = ops[i]
        for j in o["w"]:
            p = ops[j]
            if p["sem"] is None:
                Q[o["e"]].wait_ge(T.sem[CNT[p["e"]]], p["n"])
            else:
                Q[o["e"]].wait_ge(T.sem[p["sem"][0]], p["sem"][1] or arrivals(int(p["sem"][0][3:])))
        ins = o["f"](g, T, ctx)
        if o["sem"] is not None and o["sem"][1]:
            ins.then_inc(T.sem[o["sem"][0]], o["sem"][1])
        elif o["n"]:
            ins.then_inc(T.sem[CNT[o["e"]]], 1)
    g.wait_ge(T.sem.loc, sent[0])
    for name in ("dyy", "dyc0", "dyc1"):
        g.sync.wait_ge(T.sem[name], 16)
